import numpy as np
import ml_dtypes


def mxq(x, axis, fmt="e4m3"):
    dtype, down = {"e4m3": (ml_dtypes.float8_e4m3fn, 7), "e5m2": (ml_dtypes.float8_e5m2, 14)}[fmt]
    v = np.moveaxis(np.asarray(x, np.float32).astype(ml_dtypes.bfloat16).astype(np.float64), axis, -1)
    blocks = v.reshape(v.shape[:-1] + (-1, 32))
    amax = np.abs(blocks).max(-1, keepdims=True)
    byte = np.maximum(np.where(amax > 0, np.frexp(amax)[1] - 1 + 127, 0) - down, 1)
    scale = np.exp2(byte - 127.0)
    codes = (blocks / scale).astype(np.float32).astype(dtype).astype(np.float64)
    return np.moveaxis((codes * scale).reshape(v.shape), -1, axis)


WIDE = False


def mx_kscale(k):
    if not WIDE:
        return np.ones(k)
    levels = np.array([10, -10, 5, -5, 0])
    if k % 512:
        return np.exp2(np.random.permutation(np.resize(levels, k // 32))).repeat(32)
    a = np.empty((k // 512, 16))
    for p in range(k // 512):
        a[p, :8] = np.random.permutation(np.resize(levels, 8))
        for g in range(8):
            far = levels[np.abs(levels - a[p, g]) >= 10]
            a[p, g + 8] = far[np.random.randint(len(far))]
    return np.exp2(a.ravel()).repeat(32)


BF16 = ml_dtypes.bfloat16


def bf(x):
    return np.asarray(x, np.float32).astype(BF16)


def f64(x):
    return np.asarray(x).astype(np.float64)

E4M3FN = np.array([(-1.0 if i & 128 else 1.0) * ((1.0 + (i & 7) / 8.0) * 2.0 ** (((i >> 3) & 15) - 7) if i & 120 else (i & 7) * 2.0 ** -9) for i in range(256)])


def e4m3fn_bytes(y):
    return np.clip(np.asarray(y, np.float64), -448.0, 448.0).astype(np.float32).astype(ml_dtypes.float8_e4m3fn).view(np.uint8)


def e4m3fn_values(b):
    return E4M3FN[b]

def planes(Y):
    n, m = Y.shape
    b = f64(bf(Y)).reshape(n // 32, 32, m)
    amax = np.abs(b).max(1)
    byte = np.clip(np.where(amax > 0, np.frexp(amax)[1] - 1 + 127 - 7, 1), 1, 254)
    codes = (b * np.exp2(127.0 - byte)[:, None, :]).reshape(n, m).astype(np.float32).astype(ml_dtypes.float8_e4m3fn).view(np.uint8)
    words = codes.reshape(n // 512, 128, 4, m).transpose(0, 1, 3, 2)
    return np.ascontiguousarray(words), np.ascontiguousarray(byte.astype(np.uint8).reshape(n // 512, 16, m))


T, D, F, B = 512, 1024, 4096, 128
E4MAX = 448.0


def setup_inputs():
    s = mx_kscale(D)
    t = mx_kscale(F)
    spread = np.exp(0.4 * np.random.randn(T, D // B))
    X = np.random.randn(T, D) * np.repeat(spread, B, axis=1) * s
    bscale = np.abs(X).reshape(T, D // B, B).max(axis=2) / E4MAX
    X_rscale = (bscale.max(axis=1, keepdims=True) / E4MAX).astype(np.float32)
    X_sbytes = np.maximum(e4m3fn_bytes(bscale / f64(X_rscale)), np.uint8(1))
    step = e4m3fn_values(X_sbytes) * f64(X_rscale)
    X_bytes = e4m3fn_bytes(X / np.repeat(step, B, axis=1))
    Wk = np.random.randn(D, F) / np.sqrt(D) / s[:, None] * t
    Wv = np.random.randn(F, D) / np.sqrt(F) * np.exp(0.8 * np.random.randn(D))
    Wv = Wv / (t ** 2)[:, None]
    R = np.random.randn(T, D)
    return {"X_bytes": X_bytes, "X_sbytes": X_sbytes, "X_rscale": X_rscale,
            "Wk": bf(Wk), "Wv": bf(Wv), "R": bf(R)}


def reference(X_bytes, X_sbytes, X_rscale, Wk, Wv, R):
    xb = np.repeat(e4m3fn_values(X_sbytes), B, axis=1)
    X = (e4m3fn_values(X_bytes) * xb) * f64(X_rscale)
    P = mxq(X, 1, "e4m3") @ mxq(f64(Wk), 0, "e4m3")
    H = np.square(np.maximum(P, 0.0))
    V = mxq(H, 1, "e4m3") @ mxq(f64(Wv), 0, "e4m3")
    y = V * (1.0 / (1.0 + np.exp(-f64(R))))
    words, scales = planes(y.T)
    return y, words, scales

@@ -1,0 +1,425 @@
+from contextlib import ExitStack
+
+import concourse.mybir as mybir
+from concourse.masks import make_identity
+
+T, D, F = 512, 1024, 4096
+FLOPS = 2 * 2 * T * D * F
+
+F32 = mybir.dt.float32
+BF16 = mybir.dt.bfloat16
+U32 = mybir.dt.uint32
+I32 = mybir.dt.int32
+U8 = mybir.dt.uint8
+FP8 = mybir.dt.float8_e4m3fn
+FP8X4 = mybir.dt.float8_e4m3fn_x4
+ACT = mybir.ActivationFunctionType
+ALU = mybir.AluOpType
+
+P = 128
+PACK = 4
+KP = P * PACK
+TT = T // P
+XP = D // KP
+FG = F // KP
+HALVES = D // KP
+BLOCK = 128
+RUN = 4
+HALF = KP // 2
+
+N_KRAW = 5
+N_KCODE = 8
+N_VRAW = 5
+N_VGRP = 4
+N_VCODE = 5
+N_HGRP = 3
+SCALAR_COLS = [0] * 9 + [512, 320, 320, 320, 320, 320, 192]
+H_LAG = 2
+EARLY = 4
+
+
+def tile_rwkv_channel_mix_gated_b14_kernel(
+    tc, X_bytes, X_sbytes, X_rscale, Wk, Wv, R, out_0, out_1, out_2
+):
+    nc = tc.nc
+    with ExitStack() as ctx:
+        sbuf = ctx.enter_context(tc.tile_pool(name="sbuf", bufs=1))
+        psum = ctx.enter_context(tc.psum_pool(name="psum", bufs=1))
+
+        def tiles(name, count, shape, dtype):
+            return [
+                sbuf.tile(shape, dtype, name="%s%d" % (name, i), align_bytes=64)
+                for i in range(count)
+            ]
+
+        banks = [psum.tile([P, KP], F32, name="bank%d" % i) for i in range(8)]
+        ident = sbuf.tile([P, P], F32, name="ident")
+        sbytes = sbuf.tile([P, TT, 32], U8, name="sbytes")
+        bscale = sbuf.tile([P, TT * D // BLOCK], F32, name="bscale")
+        rscale = sbuf.tile([P, TT, 1], F32, name="rscale")
+        xbytes = tiles("xbytes", TT, [P, D], U8)
+        xwide = tiles("xwide", 2, [P, D], BF16)
+        xfull = tiles("xfull", 2, [P, D], BF16)
+        xgrp = tiles("xgrp", TT, [P, D], BF16)
+        xcode = tiles("xcode", TT, [P, XP * P], U32)
+        xscal = tiles("xscal", TT, [P, XP * P], U8)
+        rraw = tiles("rraw", TT * HALVES, [P, KP], BF16)
+        gate = tiles("gate", TT * HALVES, [P, KP], F32)
+        kraw = tiles("kraw", N_KRAW, [P, PACK, KP], BF16)
+        kfirst = tiles("kfirst", 2, [P, PACK, HALF], BF16)
+        kgrp = tiles("kgrp", 3, [P, KP * PACK], BF16)
+        kcode = tiles("kcode", N_KCODE, [P, KP], U32)
+        kscal = tiles("kscal", N_KCODE, [P, KP], U8)
+        vraw = tiles("vraw", N_VRAW, [P, PACK, KP], BF16)
+        vgrp = tiles("vgrp", N_VGRP, [P, KP, PACK], BF16)
+        vcode = tiles("vcode", N_VCODE, [P, KP], U32)
+        vscal = tiles("vscal", N_VCODE, [P, KP], U8)
+        relu = tiles("relu", 2, [P, 2 * KP], F32)
+        hgrp = tiles("hgrp", N_HGRP, [P, T * PACK], BF16)
+        hcode = tiles("hcode", FG, [P, T], U32)
+        hscal = tiles("hscal", FG, [P, T], U8)
+        yout = tiles("yout", TT * HALVES, [P, KP], F32)
+        ybf = tiles("ybf", TT, [P, KP], BF16)
+        ygrp = tiles("ygrp", TT, [P, KP], BF16)
+        ycode = tiles("ycode", HALVES, [P, T], U32)
+        yscal = tiles("yscal", HALVES, [P, T], U8)
+
+        def rows(tt):
+            return slice(tt * P, (tt + 1) * P)
+
+        def span(i):
+            return slice(i * KP, (i + 1) * KP)
+
+        def load_k(n):
+            g, c = divmod(n, XP)
+            nc.sync.dma_start(
+                out=kraw[n % N_KRAW][:],
+                in_=Wk[span(c), span(g)].rearrange("(p j) f -> p j f", j=PACK),
+            )
+
+        def load_k_first(i):
+            nc.sync.dma_start(
+                out=kfirst[i][:],
+                in_=Wk[span(0), i * HALF : (i + 1) * HALF].rearrange("(p j) f -> p j f", j=PACK),
+            )
+
+        def load_v(n):
+            h, g = divmod(n, FG)
+            nc.sync.dma_start(
+                out=vraw[n % N_VRAW][:],
+                in_=Wv[span(g), span(h)].rearrange("(p j) d -> p j d", j=PACK),
+            )
+
+        def load_x(tt):
+            nc.sync.dma_start(out=xbytes[tt][:], in_=X_bytes[rows(tt), :])
+
+        def load_r(n, lo=0, hi=KP):
+            h, tt = divmod(n, TT)
+            nc.sync.dma_start(out=rraw[n][:, lo:hi], in_=R[rows(tt), h * KP + lo : h * KP + hi])
+
+        def widen_x(tt):
+            for j in range(D // BLOCK):
+                cols = slice(j * BLOCK, (j + 1) * BLOCK)
+                n = tt * (D // BLOCK) + j
+                nc.scalar.activation(
+                    out=xwide[tt % 2][:, cols],
+                    in_=xbytes[tt][:, cols].bitcast(FP8),
+                    func=ACT.Copy,
+                    scale=bscale[:, n : n + 1],
+                )
+
+        def scale_x(tt):
+            nc.vector.tensor_scalar(
+                out=xfull[tt % 2][:], in0=xwide[tt % 2][:], scalar1=rscale[:, tt, :],
+                scalar2=None, op0=ALU.mult,
+            )
+
+        def turn(bank, src, passes):
+            words = src.bitcast(F32)
+            for c in range(passes):
+                for u in range(2):
+                    q = 2 * c + u
+                    nc.tensor.transpose(
+                        bank[:, q * P : (q + 1) * P],
+                        words[:, 2 * P * c + u : 2 * P * (c + 1) : 2],
+                        ident[:],
+                    )
+
+        def unload_turn(dst, bank, passes):
+            nc.scalar.copy(
+                out=dst.bitcast(F32).rearrange("p (c n u) -> p c n u", c=passes, u=2),
+                in_=bank[:, : passes * 2 * P].rearrange("p (c u n) -> p c n u", c=passes, u=2),
+            )
+
+        def quant(code, scal, src):
+            nc.vector.quantize_mx(out=code.bitcast(FP8X4), scales=scal, in_=src)
+
+        def sigmoid(n, lo=0, hi=KP):
+            nc.scalar.activation(out=gate[n][:, lo:hi], in_=rraw[n][:, lo:hi], func=ACT.Sigmoid)
+
+        def group_k_cols(n, raw, lo, hi):
+            grouped = kgrp[n % 3][:].rearrange("p (t m j) -> p m j t", t=PACK, j=PACK)
+            nc.vector.tensor_copy(
+                out=grouped[:, lo // PACK : hi // PACK],
+                in_=raw.rearrange("p j (m t) -> p m j t", t=PACK),
+            )
+
+        def group_k(n):
+            group_k_cols(n, kraw[n % N_KRAW][:], 0, KP)
+            if n + N_KRAW < FG * XP:
+                load_k(n + N_KRAW)
+
+        def quant_k(n):
+            quant(kcode[n % N_KCODE][:], kscal[n % N_KCODE][:], kgrp[n % 3][:])
+
+        def group_v(copy, n, lo, hi):
+            if lo < hi:
+                copy(
+                    out=vgrp[n % N_VGRP][:, lo:hi, :].rearrange("p (c i) j -> p c j i", i=RUN),
+                    in_=vraw[n % N_VRAW][:, :, lo:hi].rearrange("p j (c i) -> p c j i", i=RUN),
+                )
+
+        def group_v_scalar(n):
+            group_v(nc.scalar.copy, n, 0, SCALAR_COLS[n])
+
+        def group_v_vector(n):
+            group_v(nc.vector.tensor_copy, n, SCALAR_COLS[n], KP)
+
+
+        def quant_v(n):
+            quant(
+                vcode[n % N_VCODE][:], vscal[n % N_VCODE][:],
+                vgrp[n % N_VGRP][:].rearrange("p d j -> p (d j)"),
+            )
+
+        def keys(g, tt):
+            bank = banks[TT + tt]
+            for t in range(PACK):
+                for c in range(XP):
+                    n = (g * XP + c) % N_KCODE
+                    nc.tensor.matmul_mx(
+                        out=bank[:, rows(t)],
+                        lhsT=kcode[n][:, rows(t)].bitcast(FP8X4),
+                        lhsT_scale=kscal[n][:, rows(t)],
+                        rhs=xcode[tt][:, rows(c)].bitcast(FP8X4),
+                        rhs_scale=xscal[tt][:, rows(c)],
+                        start=(c == 0),
+                        stop=(c == XP - 1),
+                    )
+
+        def rectify(tt):
+            nc.scalar.activation(
+                out=relu[tt // 2][:, span(tt % 2)].rearrange("p (n t) -> p n t", t=PACK),
+                in_=banks[TT + tt][:].rearrange("p (t n) -> p n t", t=PACK),
+                func=ACT.Relu,
+            )
+
+        def square(g, pair):
+            nc.scalar.activation(
+                out=hgrp[g % N_HGRP][:, 2 * KP * pair : 2 * KP * (pair + 1)],
+                in_=relu[pair][:],
+                func=ACT.Square,
+            )
+
+        def quant_h(g):
+            quant(hcode[g][:], hscal[g][:], hgrp[g % N_HGRP][:])
+
+        def values(n):
+            h, g = divmod(n, FG)
+            for tt in range(TT):
+                nc.tensor.matmul_mx(
+                    out=banks[h * TT + tt][:],
+                    lhsT=hcode[g][:, rows(tt)].bitcast(FP8X4),
+                    lhsT_scale=hscal[g][:, rows(tt)],
+                    rhs=vcode[n % N_VCODE][:].bitcast(FP8X4),
+                    rhs_scale=vscal[n % N_VCODE][:],
+                    start=(g == 0),
+                    stop=(g == FG - 1),
+                )
+
+        def gate_y(n):
+            h, tt = divmod(n, TT)
+            nc.vector.tensor_tensor(out=yout[n][:], in0=banks[n][:], in1=gate[n][:], op=ALU.mult)
+            nc.sync.dma_start(out=out_0[rows(tt), span(h)], in_=yout[n][:])
+
+        def round_y(copy, n):
+            copy(out=ybf[n % TT][:], in_=yout[n][:])
+
+        def turn_y(n):
+            turn(banks[n % TT], ybf[n % TT][:], 1)
+
+        def unload_y(n):
+            unload_turn(ygrp[n % TT][:], banks[n % TT], 1)
+
+        def quant_y(n):
+            h, tt = divmod(n, TT)
+            quant(ycode[h][:, rows(tt)], yscal[h][:, rows(tt)], ygrp[tt][:])
+
+        def store_words(h, lo, hi):
+            nc.sync.dma_start(
+                out=out_1[h].rearrange("p m t -> p (m t)").bitcast(I32)[:, lo * P : hi * P],
+                in_=ycode[h][:, lo * P : hi * P].bitcast(I32),
+            )
+
+        def store_scales(h, queues):
+            for q in range(4):
+                queues[q % len(queues)].dma_start(
+                    out=out_2[h, 4 * q : 4 * q + 4, :].bitcast(I32),
+                    in_=yscal[h][32 * q : 32 * q + 4, :].bitcast(I32),
+                )
+
+        def quant_x(tt):
+            quant(xcode[tt][:], xscal[tt][:], xgrp[tt][:])
+
+        def turn_x(tt):
+            turn(banks[TT + tt], xfull[tt % 2][:], XP)
+
+        def unload_x(tt):
+            unload_turn(xgrp[tt][:], banks[TT + tt], XP)
+
+        ctx.enter_context(tc.manual_schedule())
+        make_identity(nc, ident[:])
+        load_r(0, 0, P)
+        load_k_first(0)
+        nc.sync.dma_start(
+            out=sbytes[:, :, : D // BLOCK], in_=X_sbytes.rearrange("(t p) j -> p t j", p=P)
+        )
+        load_x(0)
+        with nc.allow_non_contiguous_dma(reason="one scale for each token"):
+            nc.scalar.dma_start(out=rscale[:], in_=X_rscale.rearrange("(t p) o -> p t o", p=P))
+        load_k_first(1)
+        load_x(1)
+        load_k(1)
+        load_x(2)
+        load_x(3)
+        load_k(2)
+        load_k(3)
+        load_v(0)
+        load_k(4)
+        load_k(5)
+        load_r(0, P, KP)
+
+        sigmoid(0, 0, P)
+        for tt in range(TT):
+            nc.scalar.copy(
+                out=bscale[:, tt * (D // BLOCK) : (tt + 1) * (D // BLOCK)],
+                in_=sbytes[:, tt, : D // BLOCK].bitcast(FP8),
+            )
+        group_k_cols(0, kfirst[0][:], 0, HALF)
+        widen_x(0)
+        widen_x(1)
+        group_k_cols(0, kfirst[1][:], HALF, KP)
+        scale_x(0)
+        turn_x(0)
+        widen_x(2)
+        group_k(1)
+        scale_x(1)
+        turn_x(1)
+        unload_x(0)
+        widen_x(3)
+        quant_k(0)
+        scale_x(2)
+        turn_x(2)
+        quant_k(1)
+        quant_x(0)
+        unload_x(1)
+        unload_x(2)
+        group_k(2)
+        scale_x(3)
+        turn_x(3)
+        unload_x(3)
+        quant_x(1)
+        quant_x(2)
+        group_k(3)
+        quant_x(3)
+        quant_k(2)
+        group_v_vector(0)
+        quant_k(3)
+        quant_v(0)
+
+        for g in range(FG):
+            for tt in range(TT):
+                keys(g, tt)
+            if g >= H_LAG + 1:
+                values(g - H_LAG - 1)
+            rectify(0)
+            rectify(1)
+            rectify(2)
+            square(g, 0)
+            rectify(3)
+            sigmoid(g, P if g == 0 else 0, KP)
+            square(g, 1)
+            if g + 1 < FG:
+                load_r(g + 1)
+            n = (g + 2) * XP
+            if n < FG * XP:
+                group_k(n)
+                group_k(n + 1)
+                if g >= H_LAG:
+                    quant_h(g - H_LAG)
+                quant_k(n)
+                if g % 2 == 0:
+                    load_v(g // 2 + 1)
+                else:
+                    group_v_vector(g // 2 + 1)
+                quant_k(n + 1)
+                if g % 2 == 1:
+                    quant_v(g // 2 + 1)
+                if g >= FG - 4:
+                    load_v(EARLY + 2 * (g + 4 - FG))
+                    load_v(EARLY + 2 * (g + 4 - FG) + 1)
+            else:
+                v = EARLY + 2 * (g + 2 - FG)
+                group_v_vector(v)
+                group_v_vector(v + 1)
+                load_v(v + 4)
+                load_v(v + 5)
+                quant_h(g - H_LAG)
+                quant_v(v)
+                quant_v(v + 1)
+        values(FG - 3)
+        group_v_vector(FG)
+        load_v(FG + 4)
+        quant_h(FG - 2)
+        values(FG - 2)
+        quant_h(FG - 1)
+        values(FG - 1)
+
+        for n in range(FG + 1, FG * HALVES + 1):
+            i = n - FG
+            if n < FG * HALVES:
+                group_v_scalar(n)
+                group_v_vector(n)
+                if n + 4 < FG * HALVES:
+                    load_v(n + 4)
+            if 2 <= i <= TT + 1:
+                gate_y(i - 2)
+            quant_v(n - 1)
+            values(n - 1)
+            if 3 <= i <= TT + 2:
+                round_y(nc.scalar.copy, i - 3)
+                turn_y(i - 3)
+            if 4 <= i <= TT + 3:
+                unload_y(i - 4)
+            if 5 <= i <= TT + 4:
+                quant_y(i - 5)
+        store_words(0, 0, TT)
+        store_scales(0, [nc.sync])
+        for tt in range(TT):
+            gate_y(TT + tt)
+            if tt < TT - 1:
+                round_y(nc.scalar.copy, TT + tt)
+                turn_y(TT + tt)
+            if 1 <= tt < TT - 1:
+                unload_y(TT + tt - 1)
+        quant_y(TT)
+        round_y(nc.vector.tensor_copy, 2 * TT - 1)
+        turn_y(2 * TT - 1)
+        unload_y(2 * TT - 2)
+        unload_y(2 * TT - 1)
+        quant_y(TT + 1)
+        store_words(1, 0, 2)
+        quant_y(TT + 2)
+        quant_y(TT + 3)
+        store_words(1, 2, TT)
+        store_scales(1, [nc.scalar, nc.sync])

@@ -27,15 +27,17 @@ BLOCK = 128
 RUN = 4
 HALF = KP // 2
 
-N_KRAW = 5
-N_KCODE = 8
-N_VRAW = 5
+N_KRAW = 3
+N_KCODE = 3
+N_RRAW = 4
+N_VRAW = 6
 N_VGRP = 4
 N_VCODE = 5
 N_HGRP = 3
-SCALAR_COLS = [0] * 9 + [512, 320, 320, 320, 320, 320, 192]
+SCALAR_COLS = [0] * 8 + [256,512,0,512,0,512,256,256]
 H_LAG = 2
-EARLY = 4
+PIECES_AT = [[0],[],[1],[2],[],[3],[4,5],[6,7]]
+VALUES_AT = [[],[],[],[0],[1],[2],[3],[4]]
 
 
 def tile_rwkv_channel_mix_gated_b14_kernel(
@@ -63,26 +65,26 @@ def tile_rwkv_channel_mix_gated_b14_kernel(
         xgrp = tiles("xgrp", TT, [P, D], BF16)
         xcode = tiles("xcode", TT, [P, XP * P], U32)
         xscal = tiles("xscal", TT, [P, XP * P], U8)
-        rraw = tiles("rraw", TT * HALVES, [P, KP], BF16)
+        rraw = tiles("rraw", N_RRAW, [P, KP], BF16)
         gate = tiles("gate", TT * HALVES, [P, KP], F32)
-        kraw = tiles("kraw", N_KRAW, [P, PACK, KP], BF16)
+        kraw = tiles("kraw", N_KRAW, [P, XP, PACK, KP], BF16)
         kfirst = tiles("kfirst", 2, [P, PACK, HALF], BF16)
-        kgrp = tiles("kgrp", 3, [P, KP * PACK], BF16)
-        kcode = tiles("kcode", N_KCODE, [P, KP], U32)
-        kscal = tiles("kscal", N_KCODE, [P, KP], U8)
+        kgrp = tiles("kgrp", 2, [P, XP * KP * PACK], BF16)
+        kcode = tiles("kcode", N_KCODE, [P, XP * KP], U32)
+        kscal = tiles("kscal", N_KCODE, [P, XP * KP], U8)
         vraw = tiles("vraw", N_VRAW, [P, PACK, KP], BF16)
         vgrp = tiles("vgrp", N_VGRP, [P, KP, PACK], BF16)
         vcode = tiles("vcode", N_VCODE, [P, KP], U32)
         vscal = tiles("vscal", N_VCODE, [P, KP], U8)
-        relu = tiles("relu", 2, [P, 2 * KP], F32)
+        relu = tiles("relu", 2, [P, T * PACK], F32)
         hgrp = tiles("hgrp", N_HGRP, [P, T * PACK], BF16)
         hcode = tiles("hcode", FG, [P, T], U32)
         hscal = tiles("hscal", FG, [P, T], U8)
-        yout = tiles("yout", TT * HALVES, [P, KP], F32)
-        ybf = tiles("ybf", TT, [P, KP], BF16)
-        ygrp = tiles("ygrp", TT, [P, KP], BF16)
+        yout = tiles("yout", TT, [P, KP], F32)
+        ybf = tiles("ybf", TT * HALVES, [P, KP], BF16)
+        ygrp = tiles("ygrp", HALVES, [P, T * PACK], BF16)
         ycode = tiles("ycode", HALVES, [P, T], U32)
-        yscal = tiles("yscal", HALVES, [P, T], U8)
+        yscal = sbuf.tile([P, HALVES, T], U8, name="yscal", align_bytes=64)
 
         def rows(tt):
             return slice(tt * P, (tt + 1) * P)
@@ -90,12 +92,15 @@ def tile_rwkv_channel_mix_gated_b14_kernel(
         def span(i):
             return slice(i * KP, (i + 1) * KP)
 
-        def load_k(n):
-            g, c = divmod(n, XP)
+        def load_k_pass(g, c):
             nc.sync.dma_start(
-                out=kraw[n % N_KRAW][:],
+                out=kraw[g % N_KRAW][:, c],
                 in_=Wk[span(c), span(g)].rearrange("(p j) f -> p j f", j=PACK),
             )
+
+        def load_k(g):
+            for c in range(XP):
+                load_k_pass(g, c)
 
         def load_k_first(i):
             nc.sync.dma_start(
@@ -115,7 +120,7 @@ def tile_rwkv_channel_mix_gated_b14_kernel(
 
         def load_r(n, lo=0, hi=KP):
             h, tt = divmod(n, TT)
-            nc.sync.dma_start(out=rraw[n][:, lo:hi], in_=R[rows(tt), h * KP + lo : h * KP + hi])
+            nc.sync.dma_start(out=rraw[n % N_RRAW][:, lo:hi], in_=R[rows(tt), h * KP + lo : h * KP + hi])
 
         def widen_x(tt):
             for j in range(D // BLOCK):
@@ -134,13 +139,12 @@ def tile_rwkv_channel_mix_gated_b14_kernel(
                 scalar2=None, op0=ALU.mult,
             )
 
-        def turn(bank, src, passes):
+        def turn(bank, first, src, passes):
             words = src.bitcast(F32)
             for c in range(passes):
                 for u in range(2):
-                    q = 2 * c + u
                     nc.tensor.transpose(
-                        bank[:, q * P : (q + 1) * P],
+                        bank[:, rows(2 * (first + c) + u)],
                         words[:, 2 * P * c + u : 2 * P * (c + 1) : 2],
                         ident[:],
                     )
@@ -155,22 +159,27 @@ def tile_rwkv_channel_mix_gated_b14_kernel(
             nc.vector.quantize_mx(out=code.bitcast(FP8X4), scales=scal, in_=src)
 
         def sigmoid(n, lo=0, hi=KP):
-            nc.scalar.activation(out=gate[n][:, lo:hi], in_=rraw[n][:, lo:hi], func=ACT.Sigmoid)
+            nc.scalar.activation(out=gate[n][:, lo:hi], in_=rraw[n % N_RRAW][:, lo:hi], func=ACT.Sigmoid)
 
-        def group_k_cols(n, raw, lo, hi):
-            grouped = kgrp[n % 3][:].rearrange("p (t m j) -> p m j t", t=PACK, j=PACK)
+        def k_grouped(g):
+            return kgrp[g % 2][:].rearrange("p (c t m j) -> p c m j t", c=XP, t=PACK, j=PACK)
+
+        def group_k_part(c, raw, lo, hi):
             nc.vector.tensor_copy(
-                out=grouped[:, lo // PACK : hi // PACK],
+                out=k_grouped(0)[:, c, lo // PACK : hi // PACK],
                 in_=raw.rearrange("p j (m t) -> p m j t", t=PACK),
             )
 
-        def group_k(n):
-            group_k_cols(n, kraw[n % N_KRAW][:], 0, KP)
-            if n + N_KRAW < FG * XP:
-                load_k(n + N_KRAW)
+        def group_k(g):
+            nc.vector.tensor_copy(
+                out=k_grouped(g),
+                in_=kraw[g % N_KRAW][:].rearrange("p c j (m t) -> p c m j t", t=PACK),
+            )
+            if g + N_KRAW < FG:
+                load_k(g + N_KRAW)
 
-        def quant_k(n):
-            quant(kcode[n % N_KCODE][:], kscal[n % N_KCODE][:], kgrp[n % 3][:])
+        def quant_k(g):
+            quant(kcode[g % N_KCODE][:], kscal[g % N_KCODE][:], kgrp[g % 2][:])
 
         def group_v(copy, n, lo, hi):
             if lo < hi:
@@ -196,30 +205,26 @@ def tile_rwkv_channel_mix_gated_b14_kernel(
             bank = banks[TT + tt]
             for t in range(PACK):
                 for c in range(XP):
-                    n = (g * XP + c) % N_KCODE
+                    cols = rows(c * PACK + t)
                     nc.tensor.matmul_mx(
                         out=bank[:, rows(t)],
-                        lhsT=kcode[n][:, rows(t)].bitcast(FP8X4),
-                        lhsT_scale=kscal[n][:, rows(t)],
+                        lhsT=kcode[g % N_KCODE][:, cols].bitcast(FP8X4),
+                        lhsT_scale=kscal[g % N_KCODE][:, cols],
                         rhs=xcode[tt][:, rows(c)].bitcast(FP8X4),
                         rhs_scale=xscal[tt][:, rows(c)],
                         start=(c == 0),
                         stop=(c == XP - 1),
                     )
 
-        def rectify(tt):
+        def rectify(g, tt):
             nc.scalar.activation(
-                out=relu[tt // 2][:, span(tt % 2)].rearrange("p (n t) -> p n t", t=PACK),
+                out=relu[g % 2][:, span(tt)].rearrange("p (n t) -> p n t", t=PACK),
                 in_=banks[TT + tt][:].rearrange("p (t n) -> p n t", t=PACK),
                 func=ACT.Relu,
             )
 
-        def square(g, pair):
-            nc.scalar.activation(
-                out=hgrp[g % N_HGRP][:, 2 * KP * pair : 2 * KP * (pair + 1)],
-                in_=relu[pair][:],
-                func=ACT.Square,
-            )
+        def square(g):
+            nc.scalar.activation(out=hgrp[g % N_HGRP][:], in_=relu[g % 2][:], func=ACT.Square)
 
         def quant_h(g):
             quant(hcode[g][:], hscal[g][:], hgrp[g % N_HGRP][:])
@@ -239,21 +244,27 @@ def tile_rwkv_channel_mix_gated_b14_kernel(
 
         def gate_y(n):
             h, tt = divmod(n, TT)
-            nc.vector.tensor_tensor(out=yout[n][:], in0=banks[n][:], in1=gate[n][:], op=ALU.mult)
-            nc.sync.dma_start(out=out_0[rows(tt), span(h)], in_=yout[n][:])
+            nc.vector.tensor_tensor(out=yout[n % TT][:], in0=banks[n][:], in1=gate[n][:], op=ALU.mult)
+            nc.sync.dma_start(out=out_0[rows(tt), span(h)], in_=yout[n % TT][:])
 
-        def round_y(copy, n):
-            copy(out=ybf[n % TT][:], in_=yout[n][:])
+        def round_y(n):
+            nc.scalar.copy(out=ybf[n][:], in_=yout[n % TT][:])
 
-        def turn_y(n):
-            turn(banks[n % TT], ybf[n % TT][:], 1)
+        def gate_y_rounded(n):
+            nc.vector.tensor_tensor(out=ybf[n][:], in0=banks[n][:], in1=gate[n][:], op=ALU.mult)
 
-        def unload_y(n):
-            unload_turn(ygrp[n % TT][:], banks[n % TT], 1)
+        def turn_y(bank, first, count):
+            for i in range(count):
+                turn(banks[bank], i, ybf[first + i][:], 1)
 
-        def quant_y(n):
-            h, tt = divmod(n, TT)
-            quant(ycode[h][:, rows(tt)], yscal[h][:, rows(tt)], ygrp[tt][:])
+        def unload_y(bank, first, count):
+            h, tt = divmod(first, TT)
+            unload_turn(ygrp[h][:, tt * KP : (tt + count) * KP], banks[bank], count)
+
+        def quant_y(first, count):
+            h, tt = divmod(first, TT)
+            cols = slice(tt * P, (tt + count) * P)
+            quant(ycode[h][:, cols], yscal[:, h, cols], ygrp[h][:, tt * KP : (tt + count) * KP])
 
         def store_words(h, lo, hi):
             nc.sync.dma_start(
@@ -261,18 +272,19 @@ def tile_rwkv_channel_mix_gated_b14_kernel(
                 in_=ycode[h][:, lo * P : hi * P].bitcast(I32),
             )
 
-        def store_scales(h, queues):
+        def store_scales():
             for q in range(4):
-                queues[q % len(queues)].dma_start(
-                    out=out_2[h, 4 * q : 4 * q + 4, :].bitcast(I32),
-                    in_=yscal[h][32 * q : 32 * q + 4, :].bitcast(I32),
+                queue = nc.scalar if q % 2 == 0 else nc.sync
+                queue.dma_start(
+                    out=out_2[:, 4 * q : 4 * q + 4, :].rearrange("h r m -> r h m").bitcast(I32),
+                    in_=yscal[32 * q : 32 * q + 4].bitcast(I32),
                 )
 
         def quant_x(tt):
             quant(xcode[tt][:], xscal[tt][:], xgrp[tt][:])
 
         def turn_x(tt):
-            turn(banks[TT + tt], xfull[tt % 2][:], XP)
+            turn(banks[TT + tt], 0, xfull[tt % 2][:], XP)
 
         def unload_x(tt):
             unload_turn(xgrp[tt][:], banks[TT + tt], XP)
@@ -280,24 +292,22 @@ def tile_rwkv_channel_mix_gated_b14_kernel(
         ctx.enter_context(tc.manual_schedule())
         make_identity(nc, ident[:])
         load_r(0, 0, P)
-        load_k_first(0)
         nc.sync.dma_start(
             out=sbytes[:, :, : D // BLOCK], in_=X_sbytes.rearrange("(t p) j -> p t j", p=P)
         )
+        load_k_first(0)
         load_x(0)
         with nc.allow_non_contiguous_dma(reason="one scale for each token"):
             nc.scalar.dma_start(out=rscale[:], in_=X_rscale.rearrange("(t p) o -> p t o", p=P))
         load_k_first(1)
         load_x(1)
-        load_k(1)
+        load_k_pass(0, 1)
         load_x(2)
         load_x(3)
+        load_k(1)
         load_k(2)
-        load_k(3)
-        load_v(0)
-        load_k(4)
-        load_k(5)
         load_r(0, P, KP)
+        load_v(0)
 
         sigmoid(0, 0, P)
         for tt in range(TT):
@@ -305,121 +315,121 @@ def tile_rwkv_channel_mix_gated_b14_kernel(
                 out=bscale[:, tt * (D // BLOCK) : (tt + 1) * (D // BLOCK)],
                 in_=sbytes[:, tt, : D // BLOCK].bitcast(FP8),
             )
-        group_k_cols(0, kfirst[0][:], 0, HALF)
+        group_k_part(0, kfirst[0][:], 0, HALF)
         widen_x(0)
         widen_x(1)
-        group_k_cols(0, kfirst[1][:], HALF, KP)
+        group_k_part(0, kfirst[1][:], HALF, KP)
         scale_x(0)
         turn_x(0)
+        unload_x(0)
+        group_k_part(1, kraw[0][:, 1], 0, KP)
+        load_k(N_KRAW)
         widen_x(2)
-        group_k(1)
         scale_x(1)
         turn_x(1)
-        unload_x(0)
-        widen_x(3)
+        quant_x(0)
         quant_k(0)
+        unload_x(1)
+        widen_x(3)
         scale_x(2)
         turn_x(2)
-        quant_k(1)
-        quant_x(0)
-        unload_x(1)
-        unload_x(2)
-        group_k(2)
+        keys(0, 0)
+        group_k(1)
         scale_x(3)
         turn_x(3)
+        unload_x(2)
+        rectify(0, 0)
         unload_x(3)
         quant_x(1)
         quant_x(2)
-        group_k(3)
+        quant_k(1)
         quant_x(3)
-        quant_k(2)
-        group_v_vector(0)
-        quant_k(3)
-        quant_v(0)
 
+        loaded = 1
+        grouped = 0
         for g in range(FG):
             for tt in range(TT):
-                keys(g, tt)
-            if g >= H_LAG + 1:
-                values(g - H_LAG - 1)
-            rectify(0)
-            rectify(1)
-            rectify(2)
-            square(g, 0)
-            rectify(3)
-            sigmoid(g, P if g == 0 else 0, KP)
-            square(g, 1)
+                if (g, tt) != (0, 0):
+                    keys(g, tt)
+            for v in VALUES_AT[g]:
+                values(v)
+            for tt in range(TT):
+                if (g, tt) != (0, 0):
+                    rectify(g, tt)
+            if g <= TT:
+                sigmoid(g, P if g == 0 else 0, KP)
+            square(g)
             if g + 1 < FG:
                 load_r(g + 1)
-            n = (g + 2) * XP
-            if n < FG * XP:
-                group_k(n)
-                group_k(n + 1)
-                if g >= H_LAG:
-                    quant_h(g - H_LAG)
-                quant_k(n)
-                if g % 2 == 0:
-                    load_v(g // 2 + 1)
-                else:
-                    group_v_vector(g // 2 + 1)
-                quant_k(n + 1)
-                if g % 2 == 1:
-                    quant_v(g // 2 + 1)
-                if g >= FG - 4:
-                    load_v(EARLY + 2 * (g + 4 - FG))
-                    load_v(EARLY + 2 * (g + 4 - FG) + 1)
-            else:
-                v = EARLY + 2 * (g + 2 - FG)
+            if g + 2 < FG:
+                group_k(g + 2)
+            for v in PIECES_AT[g]:
                 group_v_vector(v)
-                group_v_vector(v + 1)
-                load_v(v + 4)
-                load_v(v + 5)
+                grouped = v + 1
+            ahead = 2 if g < 3 else N_VRAW
+            while loaded < grouped + ahead:
+                load_v(loaded)
+                loaded = loaded + 1
+            if g >= H_LAG:
                 quant_h(g - H_LAG)
+            if g + 2 < FG:
+                quant_k(g + 2)
+            for v in PIECES_AT[g]:
                 quant_v(v)
-                quant_v(v + 1)
+
         values(FG - 3)
         group_v_vector(FG)
-        load_v(FG + 4)
         quant_h(FG - 2)
         values(FG - 2)
         quant_h(FG - 1)
         values(FG - 1)
-
-        for n in range(FG + 1, FG * HALVES + 1):
-            i = n - FG
-            if n < FG * HALVES:
-                group_v_scalar(n)
-                group_v_vector(n)
-                if n + 4 < FG * HALVES:
-                    load_v(n + 4)
-            if 2 <= i <= TT + 1:
-                gate_y(i - 2)
-            quant_v(n - 1)
-            values(n - 1)
-            if 3 <= i <= TT + 2:
-                round_y(nc.scalar.copy, i - 3)
-                turn_y(i - 3)
-            if 4 <= i <= TT + 3:
-                unload_y(i - 4)
-            if 5 <= i <= TT + 4:
-                quant_y(i - 5)
+        for r in range(TT):
+            a = FG + 2 * r
+            group_v_scalar(a)
+            group_v_scalar(a + 1)
+            if r >= 1:
+                group_v_vector(a)
+                group_v_vector(a + 1)
+            while loaded < min(a + 2 + N_VRAW, FG * HALVES):
+                load_v(loaded)
+                loaded = loaded + 1
+            if r >= 1:
+                quant_v(a - 1)
+                values(a - 1)
+                gate_y(r - 1)
+                sigmoid(TT + r)
+                round_y(r - 1)
+            quant_v(a)
+            values(a)
+            if r == 2:
+                turn_y(0, 0, 2)
+        last = FG * HALVES - 1
+        unload_y(0, 0, 2)
+        quant_v(last)
+        values(last)
+        gate_y(TT - 1)
+        round_y(TT - 1)
+        turn_y(1, 2, 2)
+        gate_y(TT)
+        round_y(TT)
+        unload_y(1, 2, 2)
+        gate_y(TT + 1)
+        round_y(TT + 1)
+        turn_y(2, TT, 2)
+        gate_y(TT + 2)
+        round_y(TT + 2)
+        turn_y(3, TT + 2, 1)
+        quant_y(0, TT)
         store_words(0, 0, TT)
-        store_scales(0, [nc.sync])
-        for tt in range(TT):
-            gate_y(TT + tt)
-            if tt < TT - 1:
-                round_y(nc.scalar.copy, TT + tt)
-                turn_y(TT + tt)
-            if 1 <= tt < TT - 1:
-                unload_y(TT + tt - 1)
-        quant_y(TT)
-        round_y(nc.vector.tensor_copy, 2 * TT - 1)
-        turn_y(2 * TT - 1)
-        unload_y(2 * TT - 2)
-        unload_y(2 * TT - 1)
-        quant_y(TT + 1)
+        gate_y_rounded(TT + 3)
+        turn_y(0, TT + 3, 1)
+        gate_y(TT + 3)
+        unload_y(2, TT, 2)
+        unload_y(3, TT + 2, 1)
+        unload_y(0, TT + 3, 1)
+        quant_y(TT, 2)
         store_words(1, 0, 2)
-        quant_y(TT + 2)
-        quant_y(TT + 3)
+        quant_y(TT + 2, 1)
+        quant_y(TT + 3, 1)
         store_words(1, 2, TT)
-        store_scales(1, [nc.scalar, nc.sync])
+        store_scales()

@@ -25,6 +25,7 @@ FG = F // KP
 HALVES = D // KP
 BLOCK = 128
 RUN = 4
+LINE = 8
 HALF = KP // 2
 
 N_KRAW = 3
@@ -34,10 +35,12 @@ N_VRAW = 6
 N_VGRP = 4
 N_VCODE = 5
 N_HGRP = 3
+N_YOUT = 5
 SCALAR_COLS = [0] * 8 + [256,512,0,512,0,512,256,256]
 H_LAG = 2
-PIECES_AT = [[0],[],[1],[2],[],[3],[4,5],[6,7]]
+PIECES_AT = [[0],[],[1],[2],[3],[],[4,5],[6,7]]
 VALUES_AT = [[],[],[],[0],[1],[2],[3],[4]]
+SIG_AT = [[],[1],[2],[3],[4],[],[],[]]
 
 
 def tile_rwkv_channel_mix_gated_b14_kernel(
@@ -56,9 +59,9 @@ def tile_rwkv_channel_mix_gated_b14_kernel(
 
         banks = [psum.tile([P, KP], F32, name="bank%d" % i) for i in range(8)]
         ident = sbuf.tile([P, P], F32, name="ident")
-        sbytes = sbuf.tile([P, TT, 32], U8, name="sbytes")
+        sbytes = sbuf.tile([P, TT * D // BLOCK], U8, name="sbytes")
         bscale = sbuf.tile([P, TT * D // BLOCK], F32, name="bscale")
-        rscale = sbuf.tile([P, TT, 1], F32, name="rscale")
+        rscale = sbuf.tile([P, TT], F32, name="rscale")
         xbytes = tiles("xbytes", TT, [P, D], U8)
         xwide = tiles("xwide", 2, [P, D], BF16)
         xfull = tiles("xfull", 2, [P, D], BF16)
@@ -80,7 +83,7 @@ def tile_rwkv_channel_mix_gated_b14_kernel(
         hgrp = tiles("hgrp", N_HGRP, [P, T * PACK], BF16)
         hcode = tiles("hcode", FG, [P, T], U32)
         hscal = tiles("hscal", FG, [P, T], U8)
-        yout = tiles("yout", TT, [P, KP], F32)
+        yout = tiles("yout", N_YOUT, [P, KP], F32)
         ybf = tiles("ybf", TT * HALVES, [P, KP], BF16)
         ygrp = tiles("ygrp", HALVES, [P, T * PACK], BF16)
         ycode = tiles("ycode", HALVES, [P, T], U32)
@@ -116,11 +119,20 @@ def tile_rwkv_channel_mix_gated_b14_kernel(
             )
 
         def load_x(tt):
-            nc.sync.dma_start(out=xbytes[tt][:], in_=X_bytes[rows(tt), :])
+            nc.sync.dma_start(out=xbytes[tt][:], in_=X_bytes.rearrange("(p a) d -> a p d", a=TT)[tt])
 
         def load_r(n, lo=0, hi=KP):
             h, tt = divmod(n, TT)
             nc.sync.dma_start(out=rraw[n % N_RRAW][:, lo:hi], in_=R[rows(tt), h * KP + lo : h * KP + hi])
+
+        def load_scales():
+            nc.sync.dma_start(out=sbytes[:], in_=X_sbytes.rearrange("(p a) j -> p (a j)", a=TT))
+
+        def load_rscale():
+            nc.scalar.dma_start(out=rscale[:], in_=X_rscale.rearrange("(p a) o -> p (a o)", a=TT))
+
+        def widen_scales():
+            nc.scalar.copy(out=bscale[:], in_=sbytes[:].bitcast(FP8))
 
         def widen_x(tt):
             for j in range(D // BLOCK):
@@ -135,7 +147,7 @@ def tile_rwkv_channel_mix_gated_b14_kernel(
 
         def scale_x(tt):
             nc.vector.tensor_scalar(
-                out=xfull[tt % 2][:], in0=xwide[tt % 2][:], scalar1=rscale[:, tt, :],
+                out=xfull[tt % 2][:], in0=xwide[tt % 2][:], scalar1=rscale[:, tt : tt + 1],
                 scalar2=None, op0=ALU.mult,
             )
 
@@ -162,18 +174,21 @@ def tile_rwkv_channel_mix_gated_b14_kernel(
             nc.scalar.activation(out=gate[n][:, lo:hi], in_=rraw[n % N_RRAW][:, lo:hi], func=ACT.Sigmoid)
 
         def k_grouped(g):
-            return kgrp[g % 2][:].rearrange("p (c t m j) -> p c m j t", c=XP, t=PACK, j=PACK)
+            return kgrp[g % 2][:].rearrange("p (t w e j) -> p w j e t", t=PACK, e=2, j=PACK)
+
+        def k_rows(raw):
+            return raw.rearrange("p j (w e t) -> p w j e t", e=2, t=PACK)
 
         def group_k_part(c, raw, lo, hi):
+            first = (c * KP + lo) // LINE
             nc.vector.tensor_copy(
-                out=k_grouped(0)[:, c, lo // PACK : hi // PACK],
-                in_=raw.rearrange("p j (m t) -> p m j t", t=PACK),
+                out=k_grouped(0)[:, first : first + (hi - lo) // LINE], in_=k_rows(raw)
             )
 
         def group_k(g):
             nc.vector.tensor_copy(
-                out=k_grouped(g),
-                in_=kraw[g % N_KRAW][:].rearrange("p c j (m t) -> p c m j t", t=PACK),
+                out=k_grouped(g).rearrange("p (c w) j e t -> p c w j e t", c=XP),
+                in_=kraw[g % N_KRAW][:].rearrange("p c j (w e t) -> p c w j e t", e=2, t=PACK),
             )
             if g + N_KRAW < FG:
                 load_k(g + N_KRAW)
@@ -205,7 +220,7 @@ def tile_rwkv_channel_mix_gated_b14_kernel(
             bank = banks[TT + tt]
             for t in range(PACK):
                 for c in range(XP):
-                    cols = rows(c * PACK + t)
+                    cols = rows(t * XP + c)
                     nc.tensor.matmul_mx(
                         out=bank[:, rows(t)],
                         lhsT=kcode[g % N_KCODE][:, cols].bitcast(FP8X4),
@@ -218,7 +233,7 @@ def tile_rwkv_channel_mix_gated_b14_kernel(
 
         def rectify(g, tt):
             nc.scalar.activation(
-                out=relu[g % 2][:, span(tt)].rearrange("p (n t) -> p n t", t=PACK),
+                out=relu[g % 2][:].rearrange("p (n a t) -> p a n t", a=TT, t=PACK)[:, tt],
                 in_=banks[TT + tt][:].rearrange("p (t n) -> p n t", t=PACK),
                 func=ACT.Relu,
             )
@@ -244,18 +259,28 @@ def tile_rwkv_channel_mix_gated_b14_kernel(
 
         def gate_y(n):
             h, tt = divmod(n, TT)
-            nc.vector.tensor_tensor(out=yout[n % TT][:], in0=banks[n][:], in1=gate[n][:], op=ALU.mult)
-            nc.sync.dma_start(out=out_0[rows(tt), span(h)], in_=yout[n % TT][:])
+            nc.vector.tensor_tensor(out=yout[n % N_YOUT][:], in0=banks[n][:], in1=gate[n][:], op=ALU.mult)
+            nc.sync.dma_start(out=out_0[rows(tt), span(h)], in_=yout[n % N_YOUT][:])
+
+        def by_halves(tile, is_sorted):
+            if is_sorted:
+                return tile[:].rearrange("p (u w e) -> p u w e", u=2, e=2)
+            return tile[:].rearrange("p (w u e) -> p u w e", u=2, e=2)
 
         def round_y(n):
-            nc.scalar.copy(out=ybf[n][:], in_=yout[n % TT][:])
+            nc.scalar.copy(out=by_halves(ybf[n], True), in_=by_halves(yout[n % N_YOUT], False))
 
         def gate_y_rounded(n):
-            nc.vector.tensor_tensor(out=ybf[n][:], in0=banks[n][:], in1=gate[n][:], op=ALU.mult)
+            nc.vector.tensor_tensor(
+                out=by_halves(ybf[n], True), in0=by_halves(banks[n], False),
+                in1=by_halves(gate[n], False), op=ALU.mult,
+            )
 
         def turn_y(bank, first, count):
             for i in range(count):
-                turn(banks[bank], i, ybf[first + i][:], 1)
+                words = ybf[first + i][:].bitcast(F32)
+                for u in range(2):
+                    nc.tensor.transpose(banks[bank][:, rows(2 * i + u)], words[:, rows(u)], ident[:])
 
         def unload_y(bank, first, count):
             h, tt = divmod(first, TT)
@@ -291,30 +316,25 @@ def tile_rwkv_channel_mix_gated_b14_kernel(
 
         ctx.enter_context(tc.manual_schedule())
         make_identity(nc, ident[:])
-        load_r(0, 0, P)
-        nc.sync.dma_start(
-            out=sbytes[:, :, : D // BLOCK], in_=X_sbytes.rearrange("(t p) j -> p t j", p=P)
-        )
         load_k_first(0)
+        load_r(0, 0, P)
+        load_scales()
         load_x(0)
-        with nc.allow_non_contiguous_dma(reason="one scale for each token"):
-            nc.scalar.dma_start(out=rscale[:], in_=X_rscale.rearrange("(t p) o -> p t o", p=P))
+        load_rscale()
         load_k_first(1)
         load_x(1)
         load_k_pass(0, 1)
         load_x(2)
         load_x(3)
-        load_k(1)
-        load_k(2)
+        load_k_pass(1, 0)
+        load_k_pass(1, 1)
+        load_k_pass(2, 0)
+        load_k_pass(2, 1)
         load_r(0, P, KP)
         load_v(0)
-
+        load_r(1)
         sigmoid(0, 0, P)
-        for tt in range(TT):
-            nc.scalar.copy(
-                out=bscale[:, tt * (D // BLOCK) : (tt + 1) * (D // BLOCK)],
-                in_=sbytes[:, tt, : D // BLOCK].bitcast(FP8),
-            )
+        widen_scales()
         group_k_part(0, kfirst[0][:], 0, HALF)
         widen_x(0)
         widen_x(1)
@@ -344,20 +364,36 @@ def tile_rwkv_channel_mix_gated_b14_kernel(
         quant_x(2)
         quant_k(1)
         quant_x(3)
+        keys(0, 1)
+        keys(0, 2)
+        keys(0, 3)
+        rectify(0, 1)
+        rectify(0, 2)
+        rectify(0, 3)
+        keys(1, 0)
+        rectify(1, 0)
+        sigmoid(0, P, KP)
+        square(0)
+        group_k(2)
+        group_v_vector(0)
+        load_v(1)
+        load_v(2)
+        quant_k(2)
+        quant_v(0)
 
-        loaded = 1
-        grouped = 0
-        for g in range(FG):
-            for tt in range(TT):
-                if (g, tt) != (0, 0):
-                    keys(g, tt)
+        loaded = 3
+        for g in range(1, FG):
+            for tt in range(1, TT):
+                keys(g, tt)
             for v in VALUES_AT[g]:
                 values(v)
-            for tt in range(TT):
-                if (g, tt) != (0, 0):
-                    rectify(g, tt)
-            if g <= TT:
-                sigmoid(g, P if g == 0 else 0, KP)
+            for tt in range(1, TT):
+                rectify(g, tt)
+            if g + 1 < FG:
+                keys(g + 1, 0)
+                rectify(g + 1, 0)
+            for v in SIG_AT[g]:
+                sigmoid(v)
             square(g)
             if g + 1 < FG:
                 load_r(g + 1)
@@ -365,65 +401,81 @@ def tile_rwkv_channel_mix_gated_b14_kernel(
                 group_k(g + 2)
             for v in PIECES_AT[g]:
                 group_v_vector(v)
-                grouped = v + 1
-            ahead = 2 if g < 3 else N_VRAW
-            while loaded < grouped + ahead:
-                load_v(loaded)
-                loaded = loaded + 1
+                while loaded <= min(v + (2 if g < 3 else N_VRAW), FG * HALVES - 1):
+                    load_v(loaded)
+                    loaded = loaded + 1
             if g >= H_LAG:
                 quant_h(g - H_LAG)
             if g + 2 < FG:
                 quant_k(g + 2)
             for v in PIECES_AT[g]:
                 quant_v(v)
-
-        values(FG - 3)
-        group_v_vector(FG)
-        quant_h(FG - 2)
-        values(FG - 2)
-        quant_h(FG - 1)
-        values(FG - 1)
-        for r in range(TT):
-            a = FG + 2 * r
-            group_v_scalar(a)
-            group_v_scalar(a + 1)
-            if r >= 1:
-                group_v_vector(a)
-                group_v_vector(a + 1)
-            while loaded < min(a + 2 + N_VRAW, FG * HALVES):
-                load_v(loaded)
-                loaded = loaded + 1
-            if r >= 1:
-                quant_v(a - 1)
-                values(a - 1)
-                gate_y(r - 1)
-                sigmoid(TT + r)
-                round_y(r - 1)
-            quant_v(a)
-            values(a)
-            if r == 2:
-                turn_y(0, 0, 2)
-        last = FG * HALVES - 1
+        values(5)
+        group_v_vector(8)
+        quant_h(6)
+        values(6)
+        quant_h(7)
+        values(7)
+        group_v_scalar(8)
+        group_v_scalar(9)
+        load_v(14)
+        load_v(15)
+        quant_v(8)
+        values(8)
+        group_v_scalar(10)
+        group_v_scalar(11)
+        group_v_vector(10)
+        group_v_vector(11)
+        quant_v(9)
+        values(9)
+        gate_y(0)
+        sigmoid(5)
+        round_y(0)
+        quant_v(10)
+        values(10)
+        group_v_scalar(12)
+        group_v_scalar(13)
+        group_v_vector(12)
+        group_v_vector(13)
+        quant_v(11)
+        values(11)
+        gate_y(1)
+        sigmoid(6)
+        round_y(1)
+        quant_v(12)
+        values(12)
+        turn_y(0, 0, 2)
+        group_v_scalar(14)
+        group_v_scalar(15)
+        group_v_vector(14)
+        group_v_vector(15)
+        quant_v(13)
+        values(13)
+        gate_y(2)
+        sigmoid(7)
+        round_y(2)
+        quant_v(14)
+        values(14)
         unload_y(0, 0, 2)
-        quant_v(last)
-        values(last)
+        quant_v(15)
+        values(15)
         gate_y(TT - 1)
         round_y(TT - 1)
         turn_y(1, 2, 2)
         gate_y(TT)
         round_y(TT)
-        unload_y(1, 2, 2)
         gate_y(TT + 1)
         round_y(TT + 1)
         turn_y(2, TT, 2)
+        unload_y(1, 2, 2)
         gate_y(TT + 2)
         round_y(TT + 2)
-        turn_y(3, TT + 2, 1)
-        quant_y(0, TT)
-        store_words(0, 0, TT)
         gate_y_rounded(TT + 3)
+        turn_y(3, TT + 2, 1)
         turn_y(0, TT + 3, 1)
         gate_y(TT + 3)
+        quant_y(0, TT)
+        store_words(0, 0, TT)
         unload_y(2, TT, 2)
         unload_y(3, TT + 2, 1)
         unload_y(0, TT + 3, 1)

@@ -25,6 +25,7 @@ FG = F // KP
 HALVES = D // KP
 BLOCK = 128
 RUN = 4
+N_XWIDE = 2
 LINE = 8
 HALF = KP // 2
 
@@ -36,11 +37,11 @@ N_VGRP = 4
 N_VCODE = 5
 N_HGRP = 3
 N_YOUT = 5
-SCALAR_COLS = [0] * 8 + [256,512,0,512,0,512,256,256]
+SCALAR_COLS = [0] * 8 + [384,512,0,512,0,512,256,256]
 H_LAG = 2
-PIECES_AT = [[0],[],[1],[2],[3],[],[4,5],[6,7]]
-VALUES_AT = [[],[],[],[0],[1],[2],[3],[4]]
-SIG_AT = [[],[1],[2],[3],[4],[],[],[]]
+PIECES_AT = [[0],[],[1],[2],[],[],[3,4,5],[6,7]]
+VALUES_AT = [[],[],[],[0],[1],[2],[],[3,4]]
+SIG_AT = [[],[],[],[4],[5],[6],[],[]]
 
 
 def tile_rwkv_channel_mix_gated_b14_kernel(
@@ -63,14 +64,14 @@ def tile_rwkv_channel_mix_gated_b14_kernel(
         bscale = sbuf.tile([P, TT * D // BLOCK], F32, name="bscale")
         rscale = sbuf.tile([P, TT], F32, name="rscale")
         xbytes = tiles("xbytes", TT, [P, D], U8)
-        xwide = tiles("xwide", 2, [P, D], BF16)
+        xwide = tiles("xwide", N_XWIDE, [P, D], BF16)
         xfull = tiles("xfull", 2, [P, D], BF16)
         xgrp = tiles("xgrp", TT, [P, D], BF16)
         xcode = tiles("xcode", TT, [P, XP * P], U32)
         xscal = tiles("xscal", TT, [P, XP * P], U8)
         rraw = tiles("rraw", N_RRAW, [P, KP], BF16)
         gate = tiles("gate", TT * HALVES, [P, KP], F32)
-        kraw = tiles("kraw", N_KRAW, [P, XP, PACK, KP], BF16)
+        kraw = tiles("kraw", N_KRAW, [P, PACK, XP, KP], BF16)
         kfirst = tiles("kfirst", 2, [P, PACK, HALF], BF16)
         kgrp = tiles("kgrp", 2, [P, XP * KP * PACK], BF16)
         kcode = tiles("kcode", N_KCODE, [P, XP * KP], U32)
@@ -97,7 +98,7 @@ def tile_rwkv_channel_mix_gated_b14_kernel(
 
         def load_k_pass(g, c):
             nc.sync.dma_start(
-                out=kraw[g % N_KRAW][:, c],
+                out=kraw[g % N_KRAW][:, :, c],
                 in_=Wk[span(c), span(g)].rearrange("(p j) f -> p j f", j=PACK),
             )
 
@@ -132,22 +133,31 @@ def tile_rwkv_channel_mix_gated_b14_kernel(
             nc.scalar.dma_start(out=rscale[:], in_=X_rscale.rearrange("(p a) o -> p (a o)", a=TT))
 
         def widen_scales():
-            nc.scalar.copy(out=bscale[:], in_=sbytes[:].bitcast(FP8))
+            nc.vector.tensor_copy(out=bscale[:], in_=sbytes[:].bitcast(FP8))
 
-        def widen_x(tt):
+        def x_blocks(tt):
+            for_each = []
             for j in range(D // BLOCK):
                 cols = slice(j * BLOCK, (j + 1) * BLOCK)
                 n = tt * (D // BLOCK) + j
-                nc.scalar.activation(
-                    out=xwide[tt % 2][:, cols],
-                    in_=xbytes[tt][:, cols].bitcast(FP8),
-                    func=ACT.Copy,
-                    scale=bscale[:, n : n + 1],
+                for_each.append(
+                    (xwide[tt % N_XWIDE][:, cols], xbytes[tt][:, cols].bitcast(FP8), bscale[:, n : n + 1])
+                )
+            return for_each
+
+        def widen_x(tt):
+            for wide, codes, scale in x_blocks(tt):
+                nc.scalar.activation(out=wide, in_=codes, func=ACT.Copy, scale=scale)
+
+        def widen_x_vector(tt):
+            for wide, codes, scale in x_blocks(tt):
+                nc.vector.tensor_scalar(
+                    out=wide, in0=codes, scalar1=scale, scalar2=None, op0=ALU.mult
                 )
 
         def scale_x(tt):
             nc.vector.tensor_scalar(
-                out=xfull[tt % 2][:], in0=xwide[tt % 2][:], scalar1=rscale[:, tt : tt + 1],
+                out=xfull[tt % 2][:], in0=xwide[tt % N_XWIDE][:], scalar1=rscale[:, tt : tt + 1],
                 scalar2=None, op0=ALU.mult,
             )
 
@@ -174,10 +184,10 @@ def tile_rwkv_channel_mix_gated_b14_kernel(
             nc.scalar.activation(out=gate[n][:, lo:hi], in_=rraw[n % N_RRAW][:, lo:hi], func=ACT.Sigmoid)
 
         def k_grouped(g):
-            return kgrp[g % 2][:].rearrange("p (t w e j) -> p w j e t", t=PACK, e=2, j=PACK)
+            return kgrp[g % 2][:].rearrange("p (t w e j) -> p w j t e", t=PACK, e=2, j=PACK)
 
         def k_rows(raw):
-            return raw.rearrange("p j (w e t) -> p w j e t", e=2, t=PACK)
+            return raw.rearrange("p j (w e t) -> p w j t e", e=2, t=PACK)
 
         def group_k_part(c, raw, lo, hi):
             first = (c * KP + lo) // LINE
@@ -187,8 +197,8 @@ def tile_rwkv_channel_mix_gated_b14_kernel(
 
         def group_k(g):
             nc.vector.tensor_copy(
-                out=k_grouped(g).rearrange("p (c w) j e t -> p c w j e t", c=XP),
-                in_=kraw[g % N_KRAW][:].rearrange("p c j (w e t) -> p c w j e t", e=2, t=PACK),
+                out=k_grouped(g),
+                in_=k_rows(kraw[g % N_KRAW][:].rearrange("p j c f -> p j (c f)")),
             )
             if g + N_KRAW < FG:
                 load_k(g + N_KRAW)
@@ -264,8 +274,8 @@ def tile_rwkv_channel_mix_gated_b14_kernel(
 
         def by_halves(tile, is_sorted):
             if is_sorted:
-                return tile[:].rearrange("p (u w e) -> p u w e", u=2, e=2)
-            return tile[:].rearrange("p (w u e) -> p u w e", u=2, e=2)
+                return tile[:].rearrange("p (u w e) -> p w u e", u=2, e=2)
+            return tile[:].rearrange("p (w u e) -> p w u e", u=2, e=2)
 
         def round_y(n):
             nc.scalar.copy(out=by_halves(ybf[n], True), in_=by_halves(yout[n % N_YOUT], False))
@@ -316,63 +326,68 @@ def tile_rwkv_channel_mix_gated_b14_kernel(
 
         ctx.enter_context(tc.manual_schedule())
         make_identity(nc, ident[:])
-        load_k_first(0)
-        load_r(0, 0, P)
         load_scales()
+        load_x(1)
+        load_r(0, 0, P)
         load_x(0)
         load_rscale()
+        load_k_first(0)
         load_k_first(1)
-        load_x(1)
-        load_k_pass(0, 1)
         load_x(2)
+        load_k_pass(0, 1)
         load_x(3)
         load_k_pass(1, 0)
         load_k_pass(1, 1)
+        load_r(0, P, KP)
+        load_r(1)
+        load_r(2)
         load_k_pass(2, 0)
         load_k_pass(2, 1)
-        load_r(0, P, KP)
+        load_r(3)
         load_v(0)
-        load_r(1)
         sigmoid(0, 0, P)
         widen_scales()
-        group_k_part(0, kfirst[0][:], 0, HALF)
+        widen_x_vector(1)
         widen_x(0)
-        widen_x(1)
-        group_k_part(0, kfirst[1][:], HALF, KP)
-        scale_x(0)
-        turn_x(0)
-        unload_x(0)
-        group_k_part(1, kraw[0][:, 1], 0, KP)
-        load_k(N_KRAW)
-        widen_x(2)
         scale_x(1)
         turn_x(1)
-        quant_x(0)
-        quant_k(0)
+        group_k_part(0, kfirst[0][:], 0, HALF)
+        scale_x(0)
+        turn_x(0)
         unload_x(1)
+        widen_x(2)
+        group_k_part(0, kfirst[1][:], HALF, KP)
+        quant_x(1)
+        unload_x(0)
         widen_x(3)
+        group_k_part(1, kraw[0][:, :, 1], 0, KP)
+        load_k(N_KRAW)
         scale_x(2)
         turn_x(2)
-        keys(0, 0)
-        group_k(1)
+        quant_k(0)
+        quant_x(0)
         scale_x(3)
         turn_x(3)
-        unload_x(2)
-        rectify(0, 0)
-        unload_x(3)
-        quant_x(1)
-        quant_x(2)
-        quant_k(1)
-        quant_x(3)
+        keys(0, 0)
         keys(0, 1)
+        sigmoid(0, P, KP)
+        sigmoid(1)
+        unload_x(2)
+        unload_x(3)
+        group_k(1)
+        quant_x(2)
+        quant_x(3)
+        quant_k(1)
         keys(0, 2)
         keys(0, 3)
+        sigmoid(2)
+        rectify(0, 0)
         rectify(0, 1)
+        sigmoid(3)
         rectify(0, 2)
         rectify(0, 3)
         keys(1, 0)
         rectify(1, 0)
-        sigmoid(0, P, KP)
         square(0)
         group_k(2)
         group_v_vector(0)
@@ -395,8 +410,8 @@ def tile_rwkv_channel_mix_gated_b14_kernel(
             for v in SIG_AT[g]:
                 sigmoid(v)
             square(g)
-            if g + 1 < FG:
-                load_r(g + 1)
+            if g <= TT:
+                load_r(TT - 1 + g)
             if g + 2 < FG:
                 group_k(g + 2)
             for v in PIECES_AT[g]:
@@ -429,7 +444,6 @@ def tile_rwkv_channel_mix_gated_b14_kernel(
         quant_v(9)
         values(9)
         gate_y(0)
-        sigmoid(5)
         round_y(0)
         quant_v(10)
         values(10)
@@ -440,7 +454,6 @@ def tile_rwkv_channel_mix_gated_b14_kernel(
         quant_v(11)
         values(11)
         gate_y(1)
-        sigmoid(6)
         round_y(1)
         quant_v(12)
         values(12)

@@ -37,11 +37,11 @@ N_VGRP = 4
 N_VCODE = 5
 N_HGRP = 3
 N_YOUT = 5
-SCALAR_COLS = [0] * 8 + [384,512,0,512,0,512,256,256]
+SCALAR_COLS = [0] * 8 + [384,512,0,512,0,512,0,512]
 H_LAG = 2
 PIECES_AT = [[0],[],[1],[2],[],[],[3,4,5],[6,7]]
 VALUES_AT = [[],[],[],[0],[1],[2],[],[3,4]]
-SIG_AT = [[],[],[],[4],[5],[6],[],[]]
+SIG_AT = [[],[],[],[4,5],[6],[],[],[7]]
 
 
 def tile_rwkv_channel_mix_gated_b14_kernel(
@@ -206,18 +206,18 @@ def tile_rwkv_channel_mix_gated_b14_kernel(
         def quant_k(g):
             quant(kcode[g % N_KCODE][:], kscal[g % N_KCODE][:], kgrp[g % 2][:])
 
-        def group_v(copy, n, lo, hi):
+        def group_v(copy, n, lo, hi, run):
             if lo < hi:
                 copy(
-                    out=vgrp[n % N_VGRP][:, lo:hi, :].rearrange("p (c i) j -> p c j i", i=RUN),
-                    in_=vraw[n % N_VRAW][:, :, lo:hi].rearrange("p j (c i) -> p c j i", i=RUN),
+                    out=vgrp[n % N_VGRP][:, lo:hi, :].rearrange("p (c i) j -> p c j i", i=run),
+                    in_=vraw[n % N_VRAW][:, :, lo:hi].rearrange("p j (c i) -> p c j i", i=run),
                 )
 
         def group_v_scalar(n):
-            group_v(nc.scalar.copy, n, 0, SCALAR_COLS[n])
+            group_v(nc.scalar.copy, n, 0, SCALAR_COLS[n], RUN)
 
         def group_v_vector(n):
-            group_v(nc.vector.tensor_copy, n, SCALAR_COLS[n], KP)
+            group_v(nc.vector.tensor_copy, n, SCALAR_COLS[n], KP, LINE)
 
 
         def quant_v(n):
@@ -389,9 +389,9 @@ def tile_rwkv_channel_mix_gated_b14_kernel(
         keys(1, 0)
         rectify(1, 0)
         square(0)
+        load_v(1)
         group_k(2)
         group_v_vector(0)
-        load_v(1)
         load_v(2)
         quant_k(2)
         quant_v(0)
@@ -461,18 +461,19 @@ def tile_rwkv_channel_mix_gated_b14_kernel(
         group_v_scalar(14)
         group_v_scalar(15)
         group_v_vector(14)
-        group_v_vector(15)
         quant_v(13)
         values(13)
         gate_y(2)
-        sigmoid(7)
-        round_y(2)
         quant_v(14)
         values(14)
+        group_v_vector(15)
         unload_y(0, 0, 2)
+        round_y(2)
+        gate_y(TT - 1)
         quant_v(15)
         values(15)
-        gate_y(TT - 1)
+        quant_y(0, 2)
+        store_words(0, 0, 2)
         round_y(TT - 1)
         turn_y(1, 2, 2)
         gate_y(TT)
@@ -487,8 +488,8 @@ def tile_rwkv_channel_mix_gated_b14_kernel(
         turn_y(3, TT + 2, 1)
         turn_y(0, TT + 3, 1)
         gate_y(TT + 3)
-        quant_y(0, TT)
-        store_words(0, 0, TT)
+        quant_y(2, 2)
+        store_words(0, 2, TT)
         unload_y(2, TT, 2)
         unload_y(3, TT + 2, 1)
         unload_y(0, TT + 3, 1)

@@ -32,16 +32,13 @@ HALF = KP // 2
 N_KRAW = 3
 N_KCODE = 3
 N_RRAW = 4
-N_VRAW = 6
-N_VGRP = 4
-N_VCODE = 5
+N_VRAW = [4, 4]
+N_VGRP = 3
+N_VCODE = 4
 N_HGRP = 3
-N_YOUT = 5
-SCALAR_COLS = [0] * 8 + [384,512,0,512,0,512,0,512]
-H_LAG = 2
-PIECES_AT = [[0],[],[1],[2],[],[],[3,4,5],[6,7]]
-VALUES_AT = [[],[],[],[0],[1],[2],[],[3,4]]
-SIG_AT = [[],[],[],[4,5],[6],[],[],[7]]
+RING = 4
+WOVEN = 5
+PLAIN_AT = [[], [], [(1, 0)], [], [(1, 1)], [], [(0, 6), (1, 2)]]
 
 
 def tile_rwkv_channel_mix_gated_b14_kernel(
@@ -60,33 +57,35 @@ def tile_rwkv_channel_mix_gated_b14_kernel(
 
         banks = [psum.tile([P, KP], F32, name="bank%d" % i) for i in range(8)]
         ident = sbuf.tile([P, P], F32, name="ident")
+        ident16 = sbuf.tile([P, P], BF16, name="ident16")
         sbytes = sbuf.tile([P, TT * D // BLOCK], U8, name="sbytes")
         bscale = sbuf.tile([P, TT * D // BLOCK], F32, name="bscale")
         rscale = sbuf.tile([P, TT], F32, name="rscale")
-        xbytes = tiles("xbytes", TT, [P, D], U8)
+        xbytes = tiles("xbytes", 2, [P, 2, D], U8)
         xwide = tiles("xwide", N_XWIDE, [P, D], BF16)
         xfull = tiles("xfull", 2, [P, D], BF16)
-        xgrp = tiles("xgrp", TT, [P, D], BF16)
-        xcode = tiles("xcode", TT, [P, XP * P], U32)
-        xscal = tiles("xscal", TT, [P, XP * P], U8)
+        xgrp = tiles("xgrp", 2, [P, 2 * D], BF16)
+        xcode = tiles("xcode", 2, [P, XP * HALF], U32)
+        xscal = tiles("xscal", 2, [P, XP * HALF], U8)
         rraw = tiles("rraw", N_RRAW, [P, KP], BF16)
-        gate = tiles("gate", TT * HALVES, [P, KP], F32)
+        gate = [t[:] for t in tiles("gate", TT, [P, KP], F32)] + [
+            t[:].bitcast(F32)[:, i * KP : (i + 1) * KP] for t in xgrp for i in range(2)
+        ]
         kraw = tiles("kraw", N_KRAW, [P, PACK, XP, KP], BF16)
-        kfirst = tiles("kfirst", 2, [P, PACK, HALF], BF16)
         kgrp = tiles("kgrp", 2, [P, XP * KP * PACK], BF16)
         kcode = tiles("kcode", N_KCODE, [P, XP * KP], U32)
         kscal = tiles("kscal", N_KCODE, [P, XP * KP], U8)
-        vraw = tiles("vraw", N_VRAW, [P, PACK, KP], BF16)
-        vgrp = tiles("vgrp", N_VGRP, [P, KP, PACK], BF16)
-        vcode = tiles("vcode", N_VCODE, [P, KP], U32)
-        vscal = tiles("vscal", N_VCODE, [P, KP], U8)
+        vraw = [tiles("vraw%d_" % h, N_VRAW[h], [P, PACK, KP], BF16) for h in range(HALVES)]
+        vgrp = [tiles("vgrp%d_" % h, N_VGRP, [P, KP, PACK], BF16) for h in range(HALVES)]
+        vcode = [tiles("vcode0_", N_VCODE, [P, KP], U32), tiles("vcode1_", FG, [P, KP], U32)]
+        vscal = [tiles("vscal0_", N_VCODE, [P, KP], U8), tiles("vscal1_", FG, [P, KP], U8)]
         relu = tiles("relu", 2, [P, T * PACK], F32)
         hgrp = tiles("hgrp", N_HGRP, [P, T * PACK], BF16)
         hcode = tiles("hcode", FG, [P, T], U32)
         hscal = tiles("hscal", FG, [P, T], U8)
-        yout = tiles("yout", N_YOUT, [P, KP], F32)
-        ybf = tiles("ybf", TT * HALVES, [P, KP], BF16)
-        ygrp = tiles("ygrp", HALVES, [P, T * PACK], BF16)
+        yout = [t[:, i * KP : (i + 1) * KP] for t in relu for i in range(TT)]
+        ybf = [t[:, i * KP : (i + 1) * KP] for t in xwide + xfull for i in range(2)]
+        ygrp = [kgrp[0][:, i * T * PACK : (i + 1) * T * PACK] for i in range(HALVES)]
         ycode = tiles("ycode", HALVES, [P, T], U32)
         yscal = sbuf.tile([P, HALVES, T], U8, name="yscal", align_bytes=64)
 
@@ -95,6 +94,9 @@ def tile_rwkv_channel_mix_gated_b14_kernel(
 
         def span(i):
             return slice(i * KP, (i + 1) * KP)
+
+        def half(i):
+            return slice(i * HALF, (i + 1) * HALF)
 
         def load_k_pass(g, c):
             nc.sync.dma_start(
@@ -106,21 +108,19 @@ def tile_rwkv_channel_mix_gated_b14_kernel(
             for c in range(XP):
                 load_k_pass(g, c)
 
-        def load_k_first(i):
-            nc.sync.dma_start(
-                out=kfirst[i][:],
-                in_=Wk[span(0), i * HALF : (i + 1) * HALF].rearrange("(p j) f -> p j f", j=PACK),
-            )
+        def ring(group, i):
+            return group[i % len(group)]
 
-        def load_v(n):
-            h, g = divmod(n, FG)
+        def load_v(h, g):
             nc.sync.dma_start(
-                out=vraw[n % N_VRAW][:],
+                out=ring(vraw[h], g)[:],
                 in_=Wv[span(g), span(h)].rearrange("(p j) d -> p j d", j=PACK),
             )
 
-        def load_x(tt):
-            nc.sync.dma_start(out=xbytes[tt][:], in_=X_bytes.rearrange("(p a) d -> a p d", a=TT)[tt])
+        def load_x(q):
+            nc.sync.dma_start(
+                out=xbytes[q][:], in_=X_bytes.rearrange("(p q a) d -> q p a d", q=2, a=2)[q]
+            )
 
         def load_r(n, lo=0, hi=KP):
             h, tt = divmod(n, TT)
@@ -141,7 +141,7 @@ def tile_rwkv_channel_mix_gated_b14_kernel(
                 cols = slice(j * BLOCK, (j + 1) * BLOCK)
                 n = tt * (D // BLOCK) + j
                 for_each.append(
-                    (xwide[tt % N_XWIDE][:, cols], xbytes[tt][:, cols].bitcast(FP8), bscale[:, n : n + 1])
+                    (xwide[tt % N_XWIDE][:, cols], xbytes[tt // 2][:, tt % 2, cols].bitcast(FP8), bscale[:, n : n + 1])
                 )
             return for_each
 
@@ -189,10 +189,27 @@ def tile_rwkv_channel_mix_gated_b14_kernel(
         def k_rows(raw):
             return raw.rearrange("p j (w e t) -> p w j t e", e=2, t=PACK)
 
-        def group_k_part(c, raw, lo, hi):
-            first = (c * KP + lo) // LINE
+        def group_k_pass(g, c):
+            first = c * KP // LINE
             nc.vector.tensor_copy(
-                out=k_grouped(0)[:, first : first + (hi - lo) // LINE], in_=k_rows(raw)
+                out=k_grouped(g)[:, first : first + KP // LINE], in_=k_rows(kraw[g % N_KRAW][:, :, c])
+            )
+
+        def weave_k(bank, g, c, part):
+            for i in range(2):
+                lo = part * HALF + i * P
+                nc.tensor.matmul(
+                    out=bank[:].bitcast(BF16).rearrange("p (t i m j) -> p i j m t", t=PACK, i=2, j=PACK)[:, i],
+                    lhsT=ident16[:],
+                    rhs=kraw[g % N_KRAW][:, :, c, lo : lo + P].rearrange("p j (m t) -> p j m t", t=PACK),
+                    start=True,
+                    stop=True,
+                )
+
+        def unload_k(bank, g, c, part):
+            nc.scalar.copy(
+                out=kgrp[g % 2][:].bitcast(F32).rearrange("p (t c r w) -> p c r t w", t=PACK, c=XP, r=2)[:, c, part],
+                in_=bank[:].rearrange("p (t w) -> p t w", t=PACK),
             )
 
         def group_k(g):
@@ -200,95 +217,116 @@ def tile_rwkv_channel_mix_gated_b14_kernel(
                 out=k_grouped(g),
                 in_=k_rows(kraw[g % N_KRAW][:].rearrange("p j c f -> p j (c f)")),
             )
-            if g + N_KRAW < FG:
-                load_k(g + N_KRAW)
 
         def quant_k(g):
             quant(kcode[g % N_KCODE][:], kscal[g % N_KCODE][:], kgrp[g % 2][:])
 
-        def group_v(copy, n, lo, hi, run):
-            if lo < hi:
-                copy(
-                    out=vgrp[n % N_VGRP][:, lo:hi, :].rearrange("p (c i) j -> p c j i", i=run),
-                    in_=vraw[n % N_VRAW][:, :, lo:hi].rearrange("p j (c i) -> p c j i", i=run),
-                )
-
-        def group_v_scalar(n):
-            group_v(nc.scalar.copy, n, 0, SCALAR_COLS[n], RUN)
-
-        def group_v_vector(n):
-            group_v(nc.vector.tensor_copy, n, SCALAR_COLS[n], KP, LINE)
-
-
-        def quant_v(n):
-            quant(
-                vcode[n % N_VCODE][:], vscal[n % N_VCODE][:],
-                vgrp[n % N_VGRP][:].rearrange("p d j -> p (d j)"),
+        def group_v(copy, h, g, run):
+            copy(
+                out=ring(vgrp[h], g)[:].rearrange("p (c i) j -> p c j i", i=run),
+                in_=ring(vraw[h], g)[:].rearrange("p j (c i) -> p c j i", i=run),
             )
 
-        def keys(g, tt):
-            bank = banks[TT + tt]
-            for t in range(PACK):
+        def weave_v(bank, h, g, part):
+            for i in range(2):
+                lo = part * HALF + i * P
+                nc.tensor.matmul(
+                    out=bank[:].bitcast(BF16)[:, span(i)].rearrange("p (n j) -> p j n", j=PACK),
+                    lhsT=ident16[:],
+                    rhs=ring(vraw[h], g)[:, :, lo : lo + P],
+                    start=True,
+                    stop=True,
+                )
+
+        def unload_v(bank, h, g, part):
+            nc.scalar.copy(
+                out=ring(vgrp[h], g)[:].rearrange("p d j -> p (d j)").bitcast(F32)[:, span(part)],
+                in_=bank[:],
+            )
+
+        def quant_v(h, g):
+            quant(
+                ring(vcode[h], g)[:], ring(vscal[h], g)[:],
+                ring(vgrp[h], g)[:].rearrange("p d j -> p (d j)"),
+            )
+
+        def key_bank(g, tt):
+            return banks[TT + (2 * g + tt) % RING]
+
+        def weave_bank(g, part):
+            return banks[TT + (2 * g + part) % RING]
+
+        acc = banks[:TT] + [key_bank(FG - 1, tt) for tt in range(TT)]
+
+        def keys(g, i):
+            q, u = divmod(i, 2)
+            for e in range(2):
+                cols = [rows((2 * u + e) * XP + c) for c in range(XP)]
                 for c in range(XP):
-                    cols = rows(t * XP + c)
                     nc.tensor.matmul_mx(
-                        out=bank[:, rows(t)],
-                        lhsT=kcode[g % N_KCODE][:, cols].bitcast(FP8X4),
-                        lhsT_scale=kscal[g % N_KCODE][:, cols],
-                        rhs=xcode[tt][:, rows(c)].bitcast(FP8X4),
-                        rhs_scale=xscal[tt][:, rows(c)],
+                        out=key_bank(g, i)[:, half(e)],
+                        lhsT=kcode[g % N_KCODE][:, cols[c]].bitcast(FP8X4),
+                        lhsT_scale=kscal[g % N_KCODE][:, cols[c]],
+                        rhs=xcode[q][:, half(c)].bitcast(FP8X4),
+                        rhs_scale=xscal[q][:, half(c)],
                         start=(c == 0),
                         stop=(c == XP - 1),
                     )
 
-        def rectify(g, tt):
+        def rectify(g, i):
+            q, u = divmod(i, 2)
             nc.scalar.activation(
-                out=relu[g % 2][:].rearrange("p (n a t) -> p a n t", a=TT, t=PACK)[:, tt],
-                in_=banks[TT + tt][:].rearrange("p (t n) -> p n t", t=PACK),
+                out=relu[g % 2][:].rearrange("p (u n q a e) -> p u q n a e", u=2, q=2, a=2, e=2)[:, u, q],
+                in_=key_bank(g, i)[:].rearrange("p (e a n) -> p n a e", e=2, a=2),
                 func=ACT.Relu,
             )
 
         def square(g):
-            nc.scalar.activation(out=hgrp[g % N_HGRP][:], in_=relu[g % 2][:], func=ACT.Square)
+            nc.scalar.activation(
+                out=hgrp[g % N_HGRP][:].rearrange("p (m u e) -> p m u e", u=2, e=2),
+                in_=relu[g % 2][:].rearrange("p (u m e) -> p m u e", u=2, e=2),
+                func=ACT.Square,
+            )
 
         def quant_h(g):
             quant(hcode[g][:], hscal[g][:], hgrp[g % N_HGRP][:])
 
-        def values(n):
-            h, g = divmod(n, FG)
-            for tt in range(TT):
-                nc.tensor.matmul_mx(
-                    out=banks[h * TT + tt][:],
-                    lhsT=hcode[g][:, rows(tt)].bitcast(FP8X4),
-                    lhsT_scale=hscal[g][:, rows(tt)],
-                    rhs=vcode[n % N_VCODE][:].bitcast(FP8X4),
-                    rhs_scale=vscal[n % N_VCODE][:],
-                    start=(g == 0),
-                    stop=(g == FG - 1),
-                )
+        def values(h, g, tt):
+            nc.tensor.matmul_mx(
+                out=acc[h * TT + tt][:],
+                lhsT=hcode[g][:, rows(tt)].bitcast(FP8X4),
+                lhsT_scale=hscal[g][:, rows(tt)],
+                rhs=ring(vcode[h], g)[:].bitcast(FP8X4),
+                rhs_scale=ring(vscal[h], g)[:],
+                start=(g == 0),
+                stop=(g == FG - 1),
+            )
 
         def gate_y(n):
             h, tt = divmod(n, TT)
-            nc.vector.tensor_tensor(out=yout[n % N_YOUT][:], in0=banks[n][:], in1=gate[n][:], op=ALU.mult)
-            nc.sync.dma_start(out=out_0[rows(tt), span(h)], in_=yout[n % N_YOUT][:])
+            nc.vector.tensor_tensor(out=yout[n], in0=acc[n][:], in1=gate[n], op=ALU.mult)
+            nc.sync.dma_start(out=out_0[rows(tt), span(h)], in_=yout[n])
 
         def by_halves(tile, is_sorted):
             if is_sorted:
-                return tile[:].rearrange("p (u w e) -> p w u e", u=2, e=2)
-            return tile[:].rearrange("p (w u e) -> p w u e", u=2, e=2)
+                return tile.rearrange("p (u w e) -> p w u e", u=2, e=2)
+            return tile.rearrange("p (w u e) -> p w u e", u=2, e=2)
 
         def round_y(n):
-            nc.scalar.copy(out=by_halves(ybf[n], True), in_=by_halves(yout[n % N_YOUT], False))
+            nc.scalar.copy(out=by_halves(ybf[n], True), in_=by_halves(yout[n], False))
+
+        def round_v(n):
+            nc.vector.tensor_copy(out=by_halves(ybf[n], True), in_=by_halves(yout[n], False))
 
         def gate_y_rounded(n):
             nc.vector.tensor_tensor(
-                out=by_halves(ybf[n], True), in0=by_halves(banks[n], False),
+                out=by_halves(ybf[n], True), in0=by_halves(acc[n][:], False),
                 in1=by_halves(gate[n], False), op=ALU.mult,
             )
 
         def turn_y(bank, first, count):
             for i in range(count):
-                words = ybf[first + i][:].bitcast(F32)
+                words = ybf[first + i].bitcast(F32)
                 for u in range(2):
                     nc.tensor.transpose(banks[bank][:, rows(2 * i + u)], words[:, rows(u)], ident[:])
 
@@ -315,187 +353,201 @@ def tile_rwkv_channel_mix_gated_b14_kernel(
                     in_=yscal[32 * q : 32 * q + 4].bitcast(I32),
                 )
 
-        def quant_x(tt):
-            quant(xcode[tt][:], xscal[tt][:], xgrp[tt][:])
+        def quant_x(q):
+            quant(xcode[q][:], xscal[q][:], xgrp[q][:])
 
         def turn_x(tt):
             turn(banks[TT + tt], 0, xfull[tt % 2][:], XP)
 
         def unload_x(tt):
-            unload_turn(xgrp[tt][:], banks[TT + tt], XP)
+            nc.scalar.copy(
+                out=xgrp[tt // 2][:].bitcast(F32).rearrange("p (c a n u) -> p a c n u", c=XP, a=2, u=2)[:, tt % 2],
+                in_=banks[TT + tt][:].rearrange("p (c u n) -> p c n u", c=XP, u=2),
+            )
 
         ctx.enter_context(tc.manual_schedule())
         make_identity(nc, ident[:])
         load_scales()
-        load_x(1)
         load_r(0, 0, P)
         load_x(0)
         load_rscale()
-        load_k_first(0)
-        load_k_first(1)
-        load_x(2)
-        load_k_pass(0, 1)
-        load_x(3)
-        load_k_pass(1, 0)
-        load_k_pass(1, 1)
+        load_x(1)
+        load_k(0)
+        load_k(1)
         load_r(0, P, KP)
         load_r(1)
-        load_r(2)
-        load_k_pass(2, 0)
-        load_k_pass(2, 1)
-        load_r(3)
-        load_v(0)
+        load_k(2)
+        load_v(0, 0)
         sigmoid(0, 0, P)
+        nc.vector.tensor_copy(out=ident16[:], in_=ident[:])
         widen_scales()
         widen_x_vector(1)
         widen_x(0)
         scale_x(1)
-        turn_x(1)
-        group_k_part(0, kfirst[0][:], 0, HALF)
-        scale_x(0)
-        turn_x(0)
-        unload_x(1)
-        widen_x(2)
-        group_k_part(0, kfirst[1][:], HALF, KP)
-        quant_x(1)
-        unload_x(0)
         widen_x(3)
-        group_k_part(1, kraw[0][:, :, 1], 0, KP)
-        load_k(N_KRAW)
-        scale_x(2)
-        turn_x(2)
-        quant_k(0)
-        quant_x(0)
+        scale_x(0)
+        turn_x(1)
+        turn_x(0)
+        widen_x(2)
+        group_k_pass(0, 0)
         scale_x(3)
         turn_x(3)
+        group_k_pass(0, 1)
+        load_k(3)
+        load_v(0, 1)
+        load_r(2)
+        scale_x(2)
+        unload_x(1)
+        unload_x(0)
+        unload_x(3)
+        weave_k(banks[0], 1, 0, 0)
+        turn_x(2)
+        weave_k(banks[1], 1, 0, 1)
+        quant_k(0)
+        quant_x(0)
+        unload_k(banks[0], 1, 0, 0)
+        unload_x(2)
+        unload_k(banks[1], 1, 0, 1)
         keys(0, 0)
         keys(0, 1)
-        sigmoid(0, P, KP)
-        sigmoid(1)
-        unload_x(2)
-        unload_x(3)
-        group_k(1)
-        quant_x(2)
-        quant_x(3)
+        group_k_pass(1, 1)
+        load_k(4)
+        load_r(3)
+        load_v(1, 0)
+        quant_x(1)
         quant_k(1)
         keys(0, 2)
         keys(0, 3)
-        sigmoid(2)
-        rectify(0, 0)
-        rectify(0, 1)
-        sigmoid(3)
-        rectify(0, 2)
-        rectify(0, 3)
-        keys(1, 0)
-        rectify(1, 0)
-        square(0)
-        load_v(1)
-        group_k(2)
-        group_v_vector(0)
-        load_v(2)
-        quant_k(2)
-        quant_v(0)
 
-        loaded = 3
-        for g in range(1, FG):
-            for tt in range(1, TT):
-                keys(g, tt)
-            for v in VALUES_AT[g]:
-                values(v)
-            for tt in range(1, TT):
-                rectify(g, tt)
-            if g + 1 < FG:
-                keys(g + 1, 0)
-                rectify(g + 1, 0)
-            for v in SIG_AT[g]:
-                sigmoid(v)
-            square(g)
-            if g <= TT:
-                load_r(TT - 1 + g)
+        def four(h, g):
+            for tt in range(TT):
+                values(h, g, tt)
+
+        def next_v(h, g):
+            if g + N_VRAW[h] < FG:
+                load_v(h, g + N_VRAW[h])
+
+        def by_vector(h, g):
+            group_v(nc.vector.tensor_copy, h, g, LINE)
+            if h == 1:
+                next_v(h, g)
+
+        for g in range(FG - 1):
+            woven = 1 <= g <= WOVEN
+            for i in range(4):
+                rectify(g, i)
+            if g >= 1:
+                square(g - 1)
+            else:
+                sigmoid(0, P, KP)
+                sigmoid(1)
+            if g == 1:
+                weave_v(banks[2], 0, 0, 0)
+                weave_v(banks[3], 0, 0, 1)
+            if woven:
+                weave_v(weave_bank(g, 0), 0, g, 0)
+                weave_v(weave_bank(g, 1), 0, g, 1)
+            keys(g + 1, 0)
+            keys(g + 1, 1)
+            if g == 1:
+                unload_v(banks[2], 0, 0, 0)
+                unload_v(banks[3], 0, 0, 1)
             if g + 2 < FG:
+                load_v(0, g + 2)
                 group_k(g + 2)
-            for v in PIECES_AT[g]:
-                group_v_vector(v)
-                while loaded <= min(v + (2 if g < 3 else N_VRAW), FG * HALVES - 1):
-                    load_v(loaded)
-                    loaded = loaded + 1
-            if g >= H_LAG:
-                quant_h(g - H_LAG)
+                if g + 5 < FG:
+                    load_k(g + 5)
+            if 2 <= g <= 4:
+                load_v(1, g - 1)
+            for h, j in PLAIN_AT[g][:1]:
+                by_vector(h, j)
+            if g >= 2:
+                quant_h(g - 2)
             if g + 2 < FG:
                 quant_k(g + 2)
-            for v in PIECES_AT[g]:
-                quant_v(v)
-        values(5)
-        group_v_vector(8)
+            if g == 1:
+                quant_v(0, 0)
+            if 2 <= g <= WOVEN + 1:
+                quant_v(0, g - 1)
+            for n in range(len(PLAIN_AT[g])):
+                if n + 1 < len(PLAIN_AT[g]):
+                    by_vector(*PLAIN_AT[g][n + 1])
+                quant_v(*PLAIN_AT[g][n])
+            if woven:
+                unload_v(weave_bank(g, 0), 0, g, 0)
+                unload_v(weave_bank(g, 1), 0, g, 1)
+            if g >= 2:
+                four(0, g - 2)
+            keys(g + 1, 2)
+            keys(g + 1, 3)
+        for i in range(4):
+            rectify(FG - 1, i)
+        square(FG - 2)
+        square(FG - 1)
+        load_r(4)
+        load_r(5)
+        quant_h(5)
+        by_vector(0, 7)
+        four(0, 5)
+        four(1, 0)
+        four(1, 1)
+        by_vector(1, 3)
+        quant_v(0, 7)
+        by_vector(1, 4)
+        quant_v(1, 3)
         quant_h(6)
-        values(6)
+        four(1, 2)
+        four(0, 6)
+        four(1, 3)
+        by_vector(1, 5)
+        quant_v(1, 4)
         quant_h(7)
-        values(7)
-        group_v_scalar(8)
-        group_v_scalar(9)
-        load_v(14)
-        load_v(15)
-        quant_v(8)
-        values(8)
-        group_v_scalar(10)
-        group_v_scalar(11)
-        group_v_vector(10)
-        group_v_vector(11)
-        quant_v(9)
-        values(9)
+        four(0, 7)
+        four(1, 4)
+        sigmoid(2)
+        sigmoid(3)
+        load_r(6)
+        load_r(7)
+        quant_v(1, 5)
+        four(1, 5)
+        by_vector(1, 6)
+        group_v(nc.scalar.copy, 1, 7, RUN)
         gate_y(0)
-        round_y(0)
-        quant_v(10)
-        values(10)
-        group_v_scalar(12)
-        group_v_scalar(13)
-        group_v_vector(12)
-        group_v_vector(13)
-        quant_v(11)
-        values(11)
+        quant_v(1, 6)
+        four(1, 6)
         gate_y(1)
+        quant_v(1, 7)
+        four(1, 7)
+        sigmoid(4)
+        round_y(0)
+        sigmoid(5)
         round_y(1)
-        quant_v(12)
-        values(12)
         turn_y(0, 0, 2)
-        group_v_scalar(14)
-        group_v_scalar(15)
-        group_v_vector(14)
-        quant_v(13)
-        values(13)
         gate_y(2)
-        quant_v(14)
-        values(14)
-        group_v_vector(15)
-        unload_y(0, 0, 2)
+        gate_y(3)
+        sigmoid(6)
         round_y(2)
-        gate_y(TT - 1)
-        quant_v(15)
-        values(15)
-        quant_y(0, 2)
-        store_words(0, 0, 2)
-        round_y(TT - 1)
-        turn_y(1, 2, 2)
+        sigmoid(7)
         gate_y(TT)
+        round_v(3)
+        turn_y(1, 2, 2)
+        unload_y(0, 0, 2)
         round_y(TT)
         gate_y(TT + 1)
-        round_y(TT + 1)
+        gate_y(TT + 2)
+        round_v(TT + 1)
         turn_y(2, TT, 2)
         unload_y(1, 2, 2)
-        gate_y(TT + 2)
-        round_y(TT + 2)
         gate_y_rounded(TT + 3)
-        turn_y(3, TT + 2, 1)
-        turn_y(0, TT + 3, 1)
-        gate_y(TT + 3)
-        quant_y(2, 2)
-        store_words(0, 2, TT)
+        round_v(TT + 2)
+        turn_y(3, TT + 2, 2)
         unload_y(2, TT, 2)
-        unload_y(3, TT + 2, 1)
-        unload_y(0, TT + 3, 1)
+        gate_y(TT + 3)
+        quant_y(0, 4)
+        store_words(0, 0, TT)
+        unload_y(3, TT + 2, 2)
         quant_y(TT, 2)
         store_words(1, 0, 2)
-        quant_y(TT + 2, 1)
-        quant_y(TT + 3, 1)
+        quant_y(TT + 2, 2)
         store_words(1, 2, TT)
         store_scales()

@@ -32,13 +32,14 @@ HALF = KP // 2
 N_KRAW = 3
 N_KCODE = 3
 N_RRAW = 4
-N_VRAW = [4, 4]
-N_VGRP = 3
-N_VCODE = 4
+N_VRAW = [3, 3]
+N_VGRP = [2, 3]
 N_HGRP = 3
 RING = 4
+VALUES_AT = [[], [], [], [0], [], [1, 2], [3, 4]]
+PLAIN_AT = [[], [], [(0, 5)], [], [(1, 0)], [], [(1, 1), (0, 6)]]
+ROADS = [[(0, 0), (0, 1), (0, 2), (0, 3), (0, 4), (1, 6), (1, 7)], [(0, 5), (1, 0), (1, 1), (0, 6), (1, 2), (0, 7), (1, 3), (1, 4), (1, 5)]]
 WOVEN = 5
-PLAIN_AT = [[], [], [(1, 0)], [], [(1, 1)], [], [(0, 6), (1, 2)]]
 
 
 def tile_rwkv_channel_mix_gated_b14_kernel(
@@ -75,10 +76,10 @@ def tile_rwkv_channel_mix_gated_b14_kernel(
         kgrp = tiles("kgrp", 2, [P, XP * KP * PACK], BF16)
         kcode = tiles("kcode", N_KCODE, [P, XP * KP], U32)
         kscal = tiles("kscal", N_KCODE, [P, XP * KP], U8)
-        vraw = [tiles("vraw%d_" % h, N_VRAW[h], [P, PACK, KP], BF16) for h in range(HALVES)]
-        vgrp = [tiles("vgrp%d_" % h, N_VGRP, [P, KP, PACK], BF16) for h in range(HALVES)]
-        vcode = [tiles("vcode0_", N_VCODE, [P, KP], U32), tiles("vcode1_", FG, [P, KP], U32)]
-        vscal = [tiles("vscal0_", N_VCODE, [P, KP], U8), tiles("vscal1_", FG, [P, KP], U8)]
+        vraw = [tiles("vraw%d_" % r, N_VRAW[r], [P, PACK, KP], BF16) for r in range(2)]
+        vgrp = [tiles("vgrp%d_" % r, N_VGRP[r], [P, KP, PACK], BF16) for r in range(2)]
+        vcode = [tiles("vcode%d_" % h, FG, [P, KP], U32) for h in range(HALVES)]
+        vscal = [tiles("vscal%d_" % h, FG, [P, KP], U8) for h in range(HALVES)]
         relu = tiles("relu", 2, [P, T * PACK], F32)
         hgrp = tiles("hgrp", N_HGRP, [P, T * PACK], BF16)
         hcode = tiles("hcode", FG, [P, T], U32)
@@ -108,12 +109,19 @@ def tile_rwkv_channel_mix_gated_b14_kernel(
             for c in range(XP):
                 load_k_pass(g, c)
 
-        def ring(group, i):
-            return group[i % len(group)]
+        def staged(group, h, g):
+            r = 0 if (h, g) in ROADS[0] else 1
+            return group[r][ROADS[r].index((h, g)) % len(group[r])]
+
+        def load_next(h, g):
+            r = 0 if (h, g) in ROADS[0] else 1
+            n = ROADS[r].index((h, g)) + N_VRAW[r]
+            if n < len(ROADS[r]):
+                load_v(*ROADS[r][n])
 
         def load_v(h, g):
             nc.sync.dma_start(
-                out=ring(vraw[h], g)[:],
+                out=staged(vraw, h, g)[:],
                 in_=Wv[span(g), span(h)].rearrange("(p j) d -> p j d", j=PACK),
             )
 
@@ -189,10 +197,11 @@ def tile_rwkv_channel_mix_gated_b14_kernel(
         def k_rows(raw):
             return raw.rearrange("p j (w e t) -> p w j t e", e=2, t=PACK)
 
-        def group_k_pass(g, c):
-            first = c * KP // LINE
+        def group_k_pass(g, c, lo=0):
+            first = (c * KP + lo) // LINE
             nc.vector.tensor_copy(
-                out=k_grouped(g)[:, first : first + KP // LINE], in_=k_rows(kraw[g % N_KRAW][:, :, c])
+                out=k_grouped(g)[:, first : (c + 1) * KP // LINE],
+                in_=k_rows(kraw[g % N_KRAW][:, :, c, lo:]),
             )
 
         def weave_k(bank, g, c, part):
@@ -223,8 +232,8 @@ def tile_rwkv_channel_mix_gated_b14_kernel(
 
         def group_v(copy, h, g, run):
             copy(
-                out=ring(vgrp[h], g)[:].rearrange("p (c i) j -> p c j i", i=run),
-                in_=ring(vraw[h], g)[:].rearrange("p j (c i) -> p c j i", i=run),
+                out=staged(vgrp, h, g)[:].rearrange("p (c i) j -> p c j i", i=run),
+                in_=staged(vraw, h, g)[:].rearrange("p j (c i) -> p c j i", i=run),
             )
 
         def weave_v(bank, h, g, part):
@@ -233,21 +242,21 @@ def tile_rwkv_channel_mix_gated_b14_kernel(
                 nc.tensor.matmul(
                     out=bank[:].bitcast(BF16)[:, span(i)].rearrange("p (n j) -> p j n", j=PACK),
                     lhsT=ident16[:],
-                    rhs=ring(vraw[h], g)[:, :, lo : lo + P],
+                    rhs=staged(vraw, h, g)[:, :, lo : lo + P],
                     start=True,
                     stop=True,
                 )
 
         def unload_v(bank, h, g, part):
             nc.scalar.copy(
-                out=ring(vgrp[h], g)[:].rearrange("p d j -> p (d j)").bitcast(F32)[:, span(part)],
+                out=staged(vgrp, h, g)[:].rearrange("p d j -> p (d j)").bitcast(F32)[:, span(part)],
                 in_=bank[:],
             )
 
         def quant_v(h, g):
             quant(
-                ring(vcode[h], g)[:], ring(vscal[h], g)[:],
-                ring(vgrp[h], g)[:].rearrange("p d j -> p (d j)"),
+                vcode[h][g][:], vscal[h][g][:],
+                staged(vgrp, h, g)[:].rearrange("p d j -> p (d j)"),
             )
 
         def key_bank(g, tt):
@@ -296,8 +305,8 @@ def tile_rwkv_channel_mix_gated_b14_kernel(
                 out=acc[h * TT + tt][:],
                 lhsT=hcode[g][:, rows(tt)].bitcast(FP8X4),
                 lhsT_scale=hscal[g][:, rows(tt)],
-                rhs=ring(vcode[h], g)[:].bitcast(FP8X4),
-                rhs_scale=ring(vscal[h], g)[:],
+                rhs=vcode[h][g][:].bitcast(FP8X4),
+                rhs_scale=vscal[h][g][:],
                 start=(g == 0),
                 stop=(g == FG - 1),
             )
@@ -376,8 +385,9 @@ def tile_rwkv_channel_mix_gated_b14_kernel(
         load_k(1)
         load_r(0, P, KP)
         load_r(1)
-        load_k(2)
         load_v(0, 0)
+        load_r(2)
+        load_k(2)
         sigmoid(0, 0, P)
         nc.vector.tensor_copy(out=ident16[:], in_=ident[:])
         widen_scales()
@@ -395,80 +405,73 @@ def tile_rwkv_channel_mix_gated_b14_kernel(
         group_k_pass(0, 1)
         load_k(3)
         load_v(0, 1)
-        load_r(2)
         scale_x(2)
         unload_x(1)
         unload_x(0)
         unload_x(3)
+        sigmoid(0, P, KP)
         weave_k(banks[0], 1, 0, 0)
         turn_x(2)
-        weave_k(banks[1], 1, 0, 1)
         quant_k(0)
         quant_x(0)
         unload_k(banks[0], 1, 0, 0)
         unload_x(2)
-        unload_k(banks[1], 1, 0, 1)
         keys(0, 0)
         keys(0, 1)
+        group_k_pass(1, 0, HALF)
         group_k_pass(1, 1)
         load_k(4)
         load_r(3)
-        load_v(1, 0)
+        load_v(0, 2)
         quant_x(1)
         quant_k(1)
+        weave_v(banks[1], 0, 0, 0)
         keys(0, 2)
         keys(0, 3)
+        weave_v(banks[2], 0, 0, 1)
+        load_next(0, 0)
 
         def four(h, g):
             for tt in range(TT):
                 values(h, g, tt)
 
-        def next_v(h, g):
-            if g + N_VRAW[h] < FG:
-                load_v(h, g + N_VRAW[h])
-
         def by_vector(h, g):
             group_v(nc.vector.tensor_copy, h, g, LINE)
-            if h == 1:
-                next_v(h, g)
+            load_next(h, g)
 
         for g in range(FG - 1):
-            woven = 1 <= g <= WOVEN
+            woven = 1 <= g < WOVEN
             for i in range(4):
                 rectify(g, i)
+                if g == 0 and i == 1:
+                    sigmoid(1)
+                    unload_v(banks[1], 0, 0, 0)
             if g >= 1:
                 square(g - 1)
             else:
-                sigmoid(0, P, KP)
-                sigmoid(1)
-            if g == 1:
-                weave_v(banks[2], 0, 0, 0)
-                weave_v(banks[3], 0, 0, 1)
+                sigmoid(2)
+                unload_v(banks[2], 0, 0, 1)
             if woven:
                 weave_v(weave_bank(g, 0), 0, g, 0)
                 weave_v(weave_bank(g, 1), 0, g, 1)
             keys(g + 1, 0)
             keys(g + 1, 1)
-            if g == 1:
-                unload_v(banks[2], 0, 0, 0)
-                unload_v(banks[3], 0, 0, 1)
             if g + 2 < FG:
-                load_v(0, g + 2)
                 group_k(g + 2)
-                if g + 5 < FG:
-                    load_k(g + 5)
-            if 2 <= g <= 4:
-                load_v(1, g - 1)
+            if woven:
+                load_next(0, g)
+            if g < N_VRAW[1]:
+                load_v(*ROADS[1][g])
+            if g + 5 < FG:
+                load_k(g + 5)
             for h, j in PLAIN_AT[g][:1]:
                 by_vector(h, j)
             if g >= 2:
                 quant_h(g - 2)
+            if 1 <= g <= WOVEN:
+                quant_v(0, g - 1)
             if g + 2 < FG:
                 quant_k(g + 2)
-            if g == 1:
-                quant_v(0, 0)
-            if 2 <= g <= WOVEN + 1:
-                quant_v(0, g - 1)
             for n in range(len(PLAIN_AT[g])):
                 if n + 1 < len(PLAIN_AT[g]):
                     by_vector(*PLAIN_AT[g][n + 1])
@@ -476,55 +479,58 @@ def tile_rwkv_channel_mix_gated_b14_kernel(
             if woven:
                 unload_v(weave_bank(g, 0), 0, g, 0)
                 unload_v(weave_bank(g, 1), 0, g, 1)
-            if g >= 2:
-                four(0, g - 2)
+            for j in VALUES_AT[g][:1]:
+                four(0, j)
             keys(g + 1, 2)
             keys(g + 1, 3)
+            for j in VALUES_AT[g][1:]:
+                four(0, j)
         for i in range(4):
             rectify(FG - 1, i)
         square(FG - 2)
         square(FG - 1)
         load_r(4)
         load_r(5)
+        load_r(6)
+        by_vector(1, 2)
         quant_h(5)
-        by_vector(0, 7)
-        four(0, 5)
         four(1, 0)
-        four(1, 1)
+        four(0, 5)
+        by_vector(0, 7)
+        quant_v(1, 2)
         by_vector(1, 3)
         quant_v(0, 7)
-        by_vector(1, 4)
-        quant_v(1, 3)
         quant_h(6)
+        four(1, 1)
         four(1, 2)
         four(0, 6)
+        by_vector(1, 4)
+        quant_v(1, 3)
+        quant_h(7)
         four(1, 3)
+        four(0, 7)
+        sigmoid(3)
+        load_r(7)
+        group_v(nc.scalar.copy, 1, 6, RUN)
         by_vector(1, 5)
         quant_v(1, 4)
-        quant_h(7)
-        four(0, 7)
         four(1, 4)
-        sigmoid(2)
-        sigmoid(3)
-        load_r(6)
-        load_r(7)
+        gate_y(0)
         quant_v(1, 5)
         four(1, 5)
-        by_vector(1, 6)
+        gate_y(1)
         group_v(nc.scalar.copy, 1, 7, RUN)
-        gate_y(0)
         quant_v(1, 6)
         four(1, 6)
-        gate_y(1)
+        gate_y(2)
         quant_v(1, 7)
         four(1, 7)
+        gate_y(3)
         sigmoid(4)
         round_y(0)
         sigmoid(5)
         round_y(1)
         turn_y(0, 0, 2)
-        gate_y(2)
-        gate_y(3)
         sigmoid(6)
         round_y(2)
         sigmoid(7)

@@ -19,27 +19,31 @@ ALU = mybir.AluOpType
 P = 128
 PACK = 4
 KP = P * PACK
+HALF = KP // 2
 TT = T // P
 XP = D // KP
 FG = F // KP
 HALVES = D // KP
 BLOCK = 128
-RUN = 4
-N_XWIDE = 2
 LINE = 8
-HALF = KP // 2
+RUN = 4
+RING = 4
+
+WOVEN = 5
+LATE = 2
+SCALAR_ROAD = [(0, g) for g in range(WOVEN)] + [(1, g) for g in range(FG - LATE, FG)]
+VECTOR_ROAD = [(h, g + WOVEN * (1 - h)) for g in range(FG - WOVEN) for h in range(HALVES)] + [
+    (1, g) for g in range(FG - WOVEN, FG - LATE)
+]
+ROADS = [SCALAR_ROAD, VECTOR_ROAD]
+FIRST_PLAIN = 3
 
 N_KRAW = 3
+N_KGRP = 2
 N_KCODE = 3
-N_RRAW = 4
-N_VRAW = [3, 3]
+N_VRAW = 3
 N_VGRP = [2, 3]
 N_HGRP = 3
-RING = 4
-VALUES_AT = [[], [], [], [0], [], [1, 2], [3, 4]]
-PLAIN_AT = [[], [], [(0, 5)], [], [(1, 0)], [], [(1, 1), (0, 6)]]
-ROADS = [[(0, 0), (0, 1), (0, 2), (0, 3), (0, 4), (1, 6), (1, 7)], [(0, 5), (1, 0), (1, 1), (0, 6), (1, 2), (0, 7), (1, 3), (1, 4), (1, 5)]]
-WOVEN = 5
 
 
 def tile_rwkv_channel_mix_gated_b14_kernel(
@@ -56,27 +60,27 @@ def tile_rwkv_channel_mix_gated_b14_kernel(
                 for i in range(count)
             ]
 
-        banks = [psum.tile([P, KP], F32, name="bank%d" % i) for i in range(8)]
+        def cut(i, width):
+            return slice(i * width, (i + 1) * width)
+
+        banks = [psum.tile([P, KP], F32, name="bank%d" % i) for i in range(TT + RING)]
         ident = sbuf.tile([P, P], F32, name="ident")
         ident16 = sbuf.tile([P, P], BF16, name="ident16")
         sbytes = sbuf.tile([P, TT * D // BLOCK], U8, name="sbytes")
         bscale = sbuf.tile([P, TT * D // BLOCK], F32, name="bscale")
         rscale = sbuf.tile([P, TT], F32, name="rscale")
         xbytes = tiles("xbytes", 2, [P, 2, D], U8)
-        xwide = tiles("xwide", N_XWIDE, [P, D], BF16)
+        xwide = tiles("xwide", 2, [P, D], BF16)
         xfull = tiles("xfull", 2, [P, D], BF16)
         xgrp = tiles("xgrp", 2, [P, 2 * D], BF16)
         xcode = tiles("xcode", 2, [P, XP * HALF], U32)
         xscal = tiles("xscal", 2, [P, XP * HALF], U8)
-        rraw = tiles("rraw", N_RRAW, [P, KP], BF16)
-        gate = [t[:] for t in tiles("gate", TT, [P, KP], F32)] + [
-            t[:].bitcast(F32)[:, i * KP : (i + 1) * KP] for t in xgrp for i in range(2)
-        ]
+        rraw = tiles("rraw", TT, [P, KP], BF16)
         kraw = tiles("kraw", N_KRAW, [P, PACK, XP, KP], BF16)
-        kgrp = tiles("kgrp", 2, [P, XP * KP * PACK], BF16)
+        kgrp = tiles("kgrp", N_KGRP, [P, XP * KP * PACK], BF16)
         kcode = tiles("kcode", N_KCODE, [P, XP * KP], U32)
         kscal = tiles("kscal", N_KCODE, [P, XP * KP], U8)
-        vraw = [tiles("vraw%d_" % r, N_VRAW[r], [P, PACK, KP], BF16) for r in range(2)]
+        vraw = [tiles("vraw%d_" % r, N_VRAW, [P, PACK, KP], BF16) for r in range(2)]
         vgrp = [tiles("vgrp%d_" % r, N_VGRP[r], [P, KP, PACK], BF16) for r in range(2)]
         vcode = [tiles("vcode%d_" % h, FG, [P, KP], U32) for h in range(HALVES)]
         vscal = [tiles("vscal%d_" % h, FG, [P, KP], U8) for h in range(HALVES)]
@@ -84,46 +88,23 @@ def tile_rwkv_channel_mix_gated_b14_kernel(
         hgrp = tiles("hgrp", N_HGRP, [P, T * PACK], BF16)
         hcode = tiles("hcode", FG, [P, T], U32)
         hscal = tiles("hscal", FG, [P, T], U8)
-        yout = [t[:, i * KP : (i + 1) * KP] for t in relu for i in range(TT)]
-        ybf = [t[:, i * KP : (i + 1) * KP] for t in xwide + xfull for i in range(2)]
-        ygrp = [kgrp[0][:, i * T * PACK : (i + 1) * T * PACK] for i in range(HALVES)]
         ycode = tiles("ycode", HALVES, [P, T], U32)
         yscal = sbuf.tile([P, HALVES, T], U8, name="yscal", align_bytes=64)
+        gate = [t[:] for t in tiles("gate", TT, [P, KP], F32)] + [
+            t[:].bitcast(F32)[:, cut(i, KP)] for t in xgrp for i in range(2)
+        ]
+        yout = [t[:, cut(i, KP)] for t in relu for i in range(TT)]
+        ybf = [t[:, cut(i, KP)] for t in xwide + xfull for i in range(2)]
+        ygrp = [kgrp[0][:, cut(h, T * PACK)] for h in range(HALVES)]
 
-        def rows(tt):
-            return slice(tt * P, (tt + 1) * P)
+        def quant(code, scal, src):
+            nc.vector.quantize_mx(out=code.bitcast(FP8X4), scales=scal, in_=src)
 
-        def span(i):
-            return slice(i * KP, (i + 1) * KP)
+        def load_scales():
+            nc.sync.dma_start(out=sbytes[:], in_=X_sbytes.rearrange("(p a) j -> p (a j)", a=TT))
 
-        def half(i):
-            return slice(i * HALF, (i + 1) * HALF)
-
-        def load_k_pass(g, c):
-            nc.sync.dma_start(
-                out=kraw[g % N_KRAW][:, :, c],
-                in_=Wk[span(c), span(g)].rearrange("(p j) f -> p j f", j=PACK),
-            )
-
-        def load_k(g):
-            for c in range(XP):
-                load_k_pass(g, c)
-
-        def staged(group, h, g):
-            r = 0 if (h, g) in ROADS[0] else 1
-            return group[r][ROADS[r].index((h, g)) % len(group[r])]
-
-        def load_next(h, g):
-            r = 0 if (h, g) in ROADS[0] else 1
-            n = ROADS[r].index((h, g)) + N_VRAW[r]
-            if n < len(ROADS[r]):
-                load_v(*ROADS[r][n])
-
-        def load_v(h, g):
-            nc.sync.dma_start(
-                out=staged(vraw, h, g)[:],
-                in_=Wv[span(g), span(h)].rearrange("(p j) d -> p j d", j=PACK),
-            )
+        def load_rscale():
+            nc.scalar.dma_start(out=rscale[:], in_=X_rscale.rearrange("(p a) o -> p (a o)", a=TT))
 
         def load_x(q):
             nc.sync.dma_start(
@@ -132,152 +113,143 @@ def tile_rwkv_channel_mix_gated_b14_kernel(
 
         def load_r(n, lo=0, hi=KP):
             h, tt = divmod(n, TT)
-            nc.sync.dma_start(out=rraw[n % N_RRAW][:, lo:hi], in_=R[rows(tt), h * KP + lo : h * KP + hi])
+            nc.sync.dma_start(out=rraw[tt][:, lo:hi], in_=R[cut(tt, P), h * KP + lo : h * KP + hi])
 
-        def load_scales():
-            nc.sync.dma_start(out=sbytes[:], in_=X_sbytes.rearrange("(p a) j -> p (a j)", a=TT))
-
-        def load_rscale():
-            nc.scalar.dma_start(out=rscale[:], in_=X_rscale.rearrange("(p a) o -> p (a o)", a=TT))
-
-        def widen_scales():
-            nc.vector.tensor_copy(out=bscale[:], in_=sbytes[:].bitcast(FP8))
-
-        def x_blocks(tt):
-            for_each = []
-            for j in range(D // BLOCK):
-                cols = slice(j * BLOCK, (j + 1) * BLOCK)
-                n = tt * (D // BLOCK) + j
-                for_each.append(
-                    (xwide[tt % N_XWIDE][:, cols], xbytes[tt // 2][:, tt % 2, cols].bitcast(FP8), bscale[:, n : n + 1])
+        def load_k(g):
+            for c in range(XP):
+                nc.sync.dma_start(
+                    out=kraw[g % N_KRAW][:, :, c],
+                    in_=Wk[cut(c, KP), cut(g, KP)].rearrange("(p j) f -> p j f", j=PACK),
                 )
-            return for_each
 
-        def widen_x(tt):
-            for wide, codes, scale in x_blocks(tt):
+        def staged(by_road, piece):
+            r = 0 if piece in SCALAR_ROAD else 1
+            return by_road[r][ROADS[r].index(piece) % len(by_road[r])]
+
+        def load_v(piece):
+            h, g = piece
+            nc.sync.dma_start(
+                out=staged(vraw, piece)[:],
+                in_=Wv[cut(g, KP), cut(h, KP)].rearrange("(p j) d -> p j d", j=PACK),
+            )
+
+        def load_behind(piece):
+            road = SCALAR_ROAD if piece in SCALAR_ROAD else VECTOR_ROAD
+            for later in road[road.index(piece) + N_VRAW :][:1]:
+                load_v(later)
+
+        def x_blocks(a):
+            per_row = D // BLOCK
+            return [
+                (
+                    xwide[a % 2][:, cut(b, BLOCK)],
+                    xbytes[a // 2][:, a % 2, cut(b, BLOCK)].bitcast(FP8),
+                    bscale[:, a * per_row + b : a * per_row + b + 1],
+                )
+                for b in range(per_row)
+            ]
+
+        def widen_x_scalar(a):
+            for wide, codes, scale in x_blocks(a):
                 nc.scalar.activation(out=wide, in_=codes, func=ACT.Copy, scale=scale)
 
-        def widen_x_vector(tt):
-            for wide, codes, scale in x_blocks(tt):
-                nc.vector.tensor_scalar(
-                    out=wide, in0=codes, scalar1=scale, scalar2=None, op0=ALU.mult
-                )
+        def widen_x_vector(a):
+            for wide, codes, scale in x_blocks(a):
+                nc.vector.tensor_scalar(out=wide, in0=codes, scalar1=scale, scalar2=None, op0=ALU.mult)
 
-        def scale_x(tt):
+        def scale_x(a):
             nc.vector.tensor_scalar(
-                out=xfull[tt % 2][:], in0=xwide[tt % N_XWIDE][:], scalar1=rscale[:, tt : tt + 1],
+                out=xfull[a % 2][:], in0=xwide[a % 2][:], scalar1=rscale[:, a : a + 1],
                 scalar2=None, op0=ALU.mult,
             )
 
-        def turn(bank, first, src, passes):
-            words = src.bitcast(F32)
-            for c in range(passes):
+        def turn_x(a):
+            words = xfull[a % 2][:].bitcast(F32)
+            for c in range(XP):
                 for u in range(2):
                     nc.tensor.transpose(
-                        bank[:, rows(2 * (first + c) + u)],
+                        banks[TT + a][:, cut(2 * c + u, P)],
                         words[:, 2 * P * c + u : 2 * P * (c + 1) : 2],
                         ident[:],
                     )
 
-        def unload_turn(dst, bank, passes):
+        def unload_x(a):
+            words = xgrp[a // 2][:].bitcast(F32).rearrange("p (c a n u) -> p a c n u", c=XP, a=2, u=2)
             nc.scalar.copy(
-                out=dst.bitcast(F32).rearrange("p (c n u) -> p c n u", c=passes, u=2),
-                in_=bank[:, : passes * 2 * P].rearrange("p (c u n) -> p c n u", c=passes, u=2),
+                out=words[:, a % 2],
+                in_=banks[TT + a][:].rearrange("p (c u n) -> p c n u", c=XP, u=2),
             )
 
-        def quant(code, scal, src):
-            nc.vector.quantize_mx(out=code.bitcast(FP8X4), scales=scal, in_=src)
+        def quant_x(q):
+            quant(xcode[q][:], xscal[q][:], xgrp[q][:])
 
-        def sigmoid(n, lo=0, hi=KP):
-            nc.scalar.activation(out=gate[n][:, lo:hi], in_=rraw[n % N_RRAW][:, lo:hi], func=ACT.Sigmoid)
-
-        def k_grouped(g):
-            return kgrp[g % 2][:].rearrange("p (t w e j) -> p w j t e", t=PACK, e=2, j=PACK)
-
-        def k_rows(raw):
-            return raw.rearrange("p j (w e t) -> p w j t e", e=2, t=PACK)
-
-        def group_k_pass(g, c, lo=0):
-            first = (c * KP + lo) // LINE
+        def group_k(g, c, lo=0):
+            grouped = kgrp[g % N_KGRP][:].rearrange("p (t w e j) -> p w j t e", t=PACK, e=2, j=PACK)
             nc.vector.tensor_copy(
-                out=k_grouped(g)[:, first : (c + 1) * KP // LINE],
-                in_=k_rows(kraw[g % N_KRAW][:, :, c, lo:]),
+                out=grouped[:, (c * KP + lo) // LINE : (c + 1) * KP // LINE],
+                in_=kraw[g % N_KRAW][:, :, c, lo:].rearrange("p j (w e t) -> p w j t e", e=2, t=PACK),
             )
 
-        def weave_k(bank, g, c, part):
+        def weave_k(bank, g, c):
+            woven = bank[:].bitcast(BF16).rearrange("p (t i m j) -> p i j m t", t=PACK, i=2, j=PACK)
             for i in range(2):
-                lo = part * HALF + i * P
                 nc.tensor.matmul(
-                    out=bank[:].bitcast(BF16).rearrange("p (t i m j) -> p i j m t", t=PACK, i=2, j=PACK)[:, i],
+                    out=woven[:, i],
                     lhsT=ident16[:],
-                    rhs=kraw[g % N_KRAW][:, :, c, lo : lo + P].rearrange("p j (m t) -> p j m t", t=PACK),
+                    rhs=kraw[g % N_KRAW][:, :, c, cut(i, P)].rearrange("p j (m t) -> p j m t", t=PACK),
                     start=True,
                     stop=True,
                 )
 
-        def unload_k(bank, g, c, part):
-            nc.scalar.copy(
-                out=kgrp[g % 2][:].bitcast(F32).rearrange("p (t c r w) -> p c r t w", t=PACK, c=XP, r=2)[:, c, part],
-                in_=bank[:].rearrange("p (t w) -> p t w", t=PACK),
-            )
-
-        def group_k(g):
-            nc.vector.tensor_copy(
-                out=k_grouped(g),
-                in_=k_rows(kraw[g % N_KRAW][:].rearrange("p j c f -> p j (c f)")),
-            )
+        def unload_k(bank, g, c):
+            words = kgrp[g % N_KGRP][:].bitcast(F32).rearrange("p (t c r w) -> p c r t w", t=PACK, c=XP, r=2)
+            nc.scalar.copy(out=words[:, c, 0], in_=bank[:].rearrange("p (t w) -> p t w", t=PACK))
 
         def quant_k(g):
-            quant(kcode[g % N_KCODE][:], kscal[g % N_KCODE][:], kgrp[g % 2][:])
+            quant(kcode[g % N_KCODE][:], kscal[g % N_KCODE][:], kgrp[g % N_KGRP][:])
 
-        def group_v(copy, h, g, run):
+        def group_v(copy, run, piece):
             copy(
-                out=staged(vgrp, h, g)[:].rearrange("p (c i) j -> p c j i", i=run),
-                in_=staged(vraw, h, g)[:].rearrange("p j (c i) -> p c j i", i=run),
+                out=staged(vgrp, piece)[:].rearrange("p (c i) j -> p c j i", i=run),
+                in_=staged(vraw, piece)[:].rearrange("p j (c i) -> p c j i", i=run),
             )
 
-        def weave_v(bank, h, g, part):
+        def group_v_vector(piece):
+            group_v(nc.vector.tensor_copy, LINE, piece)
+            load_behind(piece)
+
+        def weave_v(bank, g, part):
             for i in range(2):
-                lo = part * HALF + i * P
                 nc.tensor.matmul(
-                    out=bank[:].bitcast(BF16)[:, span(i)].rearrange("p (n j) -> p j n", j=PACK),
+                    out=bank[:].bitcast(BF16)[:, cut(i, KP)].rearrange("p (n j) -> p j n", j=PACK),
                     lhsT=ident16[:],
-                    rhs=staged(vraw, h, g)[:, :, lo : lo + P],
+                    rhs=staged(vraw, (0, g))[:, :, cut(2 * part + i, P)],
                     start=True,
                     stop=True,
                 )
 
-        def unload_v(bank, h, g, part):
-            nc.scalar.copy(
-                out=staged(vgrp, h, g)[:].rearrange("p d j -> p (d j)").bitcast(F32)[:, span(part)],
-                in_=bank[:],
-            )
+        def unload_v(bank, g, part):
+            words = staged(vgrp, (0, g))[:].rearrange("p d j -> p (d j)").bitcast(F32)
+            nc.scalar.copy(out=words[:, cut(part, KP)], in_=bank[:])
 
-        def quant_v(h, g):
-            quant(
-                vcode[h][g][:], vscal[h][g][:],
-                staged(vgrp, h, g)[:].rearrange("p d j -> p (d j)"),
-            )
+        def quant_v(piece):
+            h, g = piece
+            quant(vcode[h][g][:], vscal[h][g][:], staged(vgrp, piece)[:].rearrange("p d j -> p (d j)"))
 
-        def key_bank(g, tt):
-            return banks[TT + (2 * g + tt) % RING]
-
-        def weave_bank(g, part):
-            return banks[TT + (2 * g + part) % RING]
-
-        acc = banks[:TT] + [key_bank(FG - 1, tt) for tt in range(TT)]
+        def ring_bank(g, i):
+            return banks[TT + (2 * g + i) % RING]
 
         def keys(g, i):
             q, u = divmod(i, 2)
             for e in range(2):
-                cols = [rows((2 * u + e) * XP + c) for c in range(XP)]
                 for c in range(XP):
+                    cols = cut((2 * u + e) * XP + c, P)
                     nc.tensor.matmul_mx(
-                        out=key_bank(g, i)[:, half(e)],
-                        lhsT=kcode[g % N_KCODE][:, cols[c]].bitcast(FP8X4),
-                        lhsT_scale=kscal[g % N_KCODE][:, cols[c]],
-                        rhs=xcode[q][:, half(c)].bitcast(FP8X4),
-                        rhs_scale=xscal[q][:, half(c)],
+                        out=ring_bank(g, i)[:, cut(e, HALF)],
+                        lhsT=kcode[g % N_KCODE][:, cols].bitcast(FP8X4),
+                        lhsT_scale=kscal[g % N_KCODE][:, cols],
+                        rhs=xcode[q][:, cut(c, HALF)].bitcast(FP8X4),
+                        rhs_scale=xscal[q][:, cut(c, HALF)],
                         start=(c == 0),
                         stop=(c == XP - 1),
                     )
@@ -286,7 +258,7 @@ def tile_rwkv_channel_mix_gated_b14_kernel(
             q, u = divmod(i, 2)
             nc.scalar.activation(
                 out=relu[g % 2][:].rearrange("p (u n q a e) -> p u q n a e", u=2, q=2, a=2, e=2)[:, u, q],
-                in_=key_bank(g, i)[:].rearrange("p (e a n) -> p n a e", e=2, a=2),
+                in_=ring_bank(g, i)[:].rearrange("p (e a n) -> p n a e", e=2, a=2),
                 func=ACT.Relu,
             )
 
@@ -300,81 +272,73 @@ def tile_rwkv_channel_mix_gated_b14_kernel(
         def quant_h(g):
             quant(hcode[g][:], hscal[g][:], hgrp[g % N_HGRP][:])
 
-        def values(h, g, tt):
-            nc.tensor.matmul_mx(
-                out=acc[h * TT + tt][:],
-                lhsT=hcode[g][:, rows(tt)].bitcast(FP8X4),
-                lhsT_scale=hscal[g][:, rows(tt)],
-                rhs=vcode[h][g][:].bitcast(FP8X4),
-                rhs_scale=vscal[h][g][:],
-                start=(g == 0),
-                stop=(g == FG - 1),
-            )
+        acc = banks[:TT] + [ring_bank(FG - 1, tt) for tt in range(TT)]
+
+        def values(piece):
+            h, g = piece
+            for tt in range(TT):
+                nc.tensor.matmul_mx(
+                    out=acc[h * TT + tt][:],
+                    lhsT=hcode[g][:, cut(tt, P)].bitcast(FP8X4),
+                    lhsT_scale=hscal[g][:, cut(tt, P)],
+                    rhs=vcode[h][g][:].bitcast(FP8X4),
+                    rhs_scale=vscal[h][g][:],
+                    start=(g == 0),
+                    stop=(g == FG - 1),
+                )
+
+        def sigmoid(n, lo=0, hi=KP):
+            nc.scalar.activation(out=gate[n][:, lo:hi], in_=rraw[n % TT][:, lo:hi], func=ACT.Sigmoid)
 
         def gate_y(n):
             h, tt = divmod(n, TT)
             nc.vector.tensor_tensor(out=yout[n], in0=acc[n][:], in1=gate[n], op=ALU.mult)
-            nc.sync.dma_start(out=out_0[rows(tt), span(h)], in_=yout[n])
+            nc.sync.dma_start(out=out_0[cut(tt, P), cut(h, KP)], in_=yout[n])
 
-        def by_halves(tile, is_sorted):
-            if is_sorted:
-                return tile.rearrange("p (u w e) -> p w u e", u=2, e=2)
-            return tile.rearrange("p (w u e) -> p w u e", u=2, e=2)
+        def as_stored(ap):
+            return ap.rearrange("p (w u e) -> p w u e", u=2, e=2)
 
-        def round_y(n):
-            nc.scalar.copy(out=by_halves(ybf[n], True), in_=by_halves(yout[n], False))
+        def as_sorted(ap):
+            return ap.rearrange("p (u w e) -> p w u e", u=2, e=2)
 
-        def round_v(n):
-            nc.vector.tensor_copy(out=by_halves(ybf[n], True), in_=by_halves(yout[n], False))
+        def round_y(copy, n):
+            copy(out=as_sorted(ybf[n]), in_=as_stored(yout[n]))
 
         def gate_y_rounded(n):
             nc.vector.tensor_tensor(
-                out=by_halves(ybf[n], True), in0=by_halves(acc[n][:], False),
-                in1=by_halves(gate[n], False), op=ALU.mult,
+                out=as_sorted(ybf[n]), in0=as_stored(acc[n][:]), in1=as_stored(gate[n]), op=ALU.mult
             )
 
-        def turn_y(bank, first, count):
-            for i in range(count):
-                words = ybf[first + i].bitcast(F32)
+        def turn_y(pair):
+            for i in range(2):
+                words = ybf[2 * pair + i].bitcast(F32)
                 for u in range(2):
-                    nc.tensor.transpose(banks[bank][:, rows(2 * i + u)], words[:, rows(u)], ident[:])
+                    nc.tensor.transpose(banks[pair][:, cut(2 * i + u, P)], words[:, cut(u, P)], ident[:])
 
-        def unload_y(bank, first, count):
-            h, tt = divmod(first, TT)
-            unload_turn(ygrp[h][:, tt * KP : (tt + count) * KP], banks[bank], count)
+        def unload_y(pair):
+            h, r = divmod(pair, 2)
+            nc.scalar.copy(
+                out=ygrp[h][:, cut(r, 2 * KP)].bitcast(F32).rearrange("p (i n u) -> p i n u", i=2, u=2),
+                in_=banks[pair][:].rearrange("p (i u n) -> p i n u", i=2, u=2),
+            )
 
-        def quant_y(first, count):
-            h, tt = divmod(first, TT)
-            cols = slice(tt * P, (tt + count) * P)
-            quant(ycode[h][:, cols], yscal[:, h, cols], ygrp[h][:, tt * KP : (tt + count) * KP])
-
-        def store_words(h, lo, hi):
+        def quant_y(h, lo, hi):
+            quant(ycode[h][:, lo:hi], yscal[:, h, lo:hi], ygrp[h][:, lo * PACK : hi * PACK])
             nc.sync.dma_start(
-                out=out_1[h].rearrange("p m t -> p (m t)").bitcast(I32)[:, lo * P : hi * P],
-                in_=ycode[h][:, lo * P : hi * P].bitcast(I32),
+                out=out_1[h].rearrange("p m t -> p (m t)").bitcast(I32)[:, lo:hi],
+                in_=ycode[h][:, lo:hi].bitcast(I32),
             )
 
         def store_scales():
             for q in range(4):
                 queue = nc.scalar if q % 2 == 0 else nc.sync
                 queue.dma_start(
-                    out=out_2[:, 4 * q : 4 * q + 4, :].rearrange("h r m -> r h m").bitcast(I32),
+                    out=out_2[:, cut(q, 4), :].rearrange("h r m -> r h m").bitcast(I32),
                     in_=yscal[32 * q : 32 * q + 4].bitcast(I32),
                 )
 
-        def quant_x(q):
-            quant(xcode[q][:], xscal[q][:], xgrp[q][:])
-
-        def turn_x(tt):
-            turn(banks[TT + tt], 0, xfull[tt % 2][:], XP)
-
-        def unload_x(tt):
-            nc.scalar.copy(
-                out=xgrp[tt // 2][:].bitcast(F32).rearrange("p (c a n u) -> p a c n u", c=XP, a=2, u=2)[:, tt % 2],
-                in_=banks[TT + tt][:].rearrange("p (c u n) -> p c n u", c=XP, u=2),
-            )
-
         ctx.enter_context(tc.manual_schedule())
+
         make_identity(nc, ident[:])
         load_scales()
         load_r(0, 0, P)
@@ -384,176 +348,164 @@ def tile_rwkv_channel_mix_gated_b14_kernel(
         load_k(0)
         load_k(1)
         load_r(0, P, KP)
+        load_v((0, 0))
         load_r(1)
-        load_v(0, 0)
-        load_r(2)
         load_k(2)
         sigmoid(0, 0, P)
         nc.vector.tensor_copy(out=ident16[:], in_=ident[:])
-        widen_scales()
+        nc.vector.tensor_copy(out=bscale[:], in_=sbytes[:].bitcast(FP8))
         widen_x_vector(1)
-        widen_x(0)
+        widen_x_scalar(0)
         scale_x(1)
-        widen_x(3)
+        widen_x_scalar(3)
         scale_x(0)
         turn_x(1)
         turn_x(0)
-        widen_x(2)
-        group_k_pass(0, 0)
+        widen_x_scalar(2)
+        group_k(0, 0)
         scale_x(3)
         turn_x(3)
-        group_k_pass(0, 1)
+        group_k(0, 1)
         load_k(3)
-        load_v(0, 1)
+        load_v((0, 1))
+        load_r(2)
         scale_x(2)
         unload_x(1)
         unload_x(0)
         unload_x(3)
         sigmoid(0, P, KP)
-        weave_k(banks[0], 1, 0, 0)
+        weave_k(banks[0], 1, 0)
         turn_x(2)
         quant_k(0)
         quant_x(0)
-        unload_k(banks[0], 1, 0, 0)
+        unload_k(banks[0], 1, 0)
         unload_x(2)
         keys(0, 0)
         keys(0, 1)
-        group_k_pass(1, 0, HALF)
-        group_k_pass(1, 1)
+        group_k(1, 0, HALF)
+        group_k(1, 1)
         load_k(4)
-        load_r(3)
-        load_v(0, 2)
+        load_v((0, 2))
+        load_v(VECTOR_ROAD[0])
         quant_x(1)
         quant_k(1)
-        weave_v(banks[1], 0, 0, 0)
+        weave_v(banks[1], 0, 0)
         keys(0, 2)
         keys(0, 3)
-        weave_v(banks[2], 0, 0, 1)
-        load_next(0, 0)
+        weave_v(banks[2], 0, 1)
+        rectify(0, 0)
+        rectify(0, 1)
+        sigmoid(1)
+        unload_v(banks[1], 0, 0)
+        rectify(0, 2)
+        rectify(0, 3)
+        unload_v(banks[2], 0, 1)
 
-        def four(h, g):
-            for tt in range(TT):
-                values(h, g, tt)
-
-        def by_vector(h, g):
-            group_v(nc.vector.tensor_copy, h, g, LINE)
-            load_next(h, g)
-
+        copied = 0
+        added = 0
         for g in range(FG - 1):
             woven = 1 <= g < WOVEN
-            for i in range(4):
-                rectify(g, i)
-                if g == 0 and i == 1:
-                    sigmoid(1)
-                    unload_v(banks[1], 0, 0, 0)
             if g >= 1:
+                for i in range(RING):
+                    rectify(g, i)
                 square(g - 1)
-            else:
+            if g == 1:
                 sigmoid(2)
-                unload_v(banks[2], 0, 0, 1)
             if woven:
-                weave_v(weave_bank(g, 0), 0, g, 0)
-                weave_v(weave_bank(g, 1), 0, g, 1)
+                weave_v(ring_bank(g, 0), g, 0)
+                weave_v(ring_bank(g, 1), g, 1)
             keys(g + 1, 0)
             keys(g + 1, 1)
-            if g + 2 < FG:
-                group_k(g + 2)
-            if woven:
-                load_next(0, g)
-            if g < N_VRAW[1]:
-                load_v(*ROADS[1][g])
-            if g + 5 < FG:
-                load_k(g + 5)
-            for h, j in PLAIN_AT[g][:1]:
-                by_vector(h, j)
+            keys_left = g + 2 < FG
+            if keys_left:
+                group_k(g + 2, 0)
+                group_k(g + 2, 1)
+                if g + 2 + N_KRAW < FG:
+                    load_k(g + 2 + N_KRAW)
+            if g < WOVEN:
+                load_behind((0, g))
+            if 1 <= g < N_VRAW:
+                load_v(VECTOR_ROAD[g])
+            if g == N_VRAW:
+                load_r(TT - 1)
+            if keys_left:
+                count = 1 if g >= FIRST_PLAIN and (g - FIRST_PLAIN) % 2 == 0 else 0
+            else:
+                count = 2
+            plain = VECTOR_ROAD[copied : copied + count]
+            copied = copied + count
+            for piece in plain[:1]:
+                group_v_vector(piece)
             if g >= 2:
                 quant_h(g - 2)
             if 1 <= g <= WOVEN:
-                quant_v(0, g - 1)
-            if g + 2 < FG:
+                quant_v((0, g - 1))
+            if keys_left:
                 quant_k(g + 2)
-            for n in range(len(PLAIN_AT[g])):
-                if n + 1 < len(PLAIN_AT[g]):
-                    by_vector(*PLAIN_AT[g][n + 1])
-                quant_v(*PLAIN_AT[g][n])
+            for piece in plain[1:]:
+                group_v_vector(piece)
+            for piece in plain:
+                quant_v(piece)
             if woven:
-                unload_v(weave_bank(g, 0), 0, g, 0)
-                unload_v(weave_bank(g, 1), 0, g, 1)
-            for j in VALUES_AT[g][:1]:
-                four(0, j)
+                unload_v(ring_bank(g, 0), g, 0)
+                unload_v(ring_bank(g, 1), g, 1)
+            count = 2 if g >= WOVEN else (1 if g == FIRST_PLAIN else 0)
+            for j in range(added, added + count)[:1]:
+                values((0, j))
             keys(g + 1, 2)
             keys(g + 1, 3)
-            for j in VALUES_AT[g][1:]:
-                four(0, j)
-        for i in range(4):
+            for j in range(added, added + count)[1:]:
+                values((0, j))
+            added = added + count
+
+        for i in range(RING):
             rectify(FG - 1, i)
         square(FG - 2)
         square(FG - 1)
-        load_r(4)
-        load_r(5)
-        load_r(6)
-        by_vector(1, 2)
-        quant_h(5)
-        four(1, 0)
-        four(0, 5)
-        by_vector(0, 7)
-        quant_v(1, 2)
-        by_vector(1, 3)
-        quant_v(0, 7)
-        quant_h(6)
-        four(1, 1)
-        four(1, 2)
-        four(0, 6)
-        by_vector(1, 4)
-        quant_v(1, 3)
-        quant_h(7)
-        four(1, 3)
-        four(0, 7)
-        sigmoid(3)
-        load_r(7)
-        group_v(nc.scalar.copy, 1, 6, RUN)
-        by_vector(1, 5)
-        quant_v(1, 4)
-        four(1, 4)
-        gate_y(0)
-        quant_v(1, 5)
-        four(1, 5)
-        gate_y(1)
-        group_v(nc.scalar.copy, 1, 7, RUN)
-        quant_v(1, 6)
-        four(1, 6)
-        gate_y(2)
-        quant_v(1, 7)
-        four(1, 7)
-        gate_y(3)
-        sigmoid(4)
-        round_y(0)
-        sigmoid(5)
-        round_y(1)
-        turn_y(0, 0, 2)
-        sigmoid(6)
-        round_y(2)
-        sigmoid(7)
+        for n in range(TT, 2 * TT - 1):
+            load_r(n)
+        rest = VECTOR_ROAD[copied:]
+        for i in range(TT):
+            group_v_vector(rest[i])
+            if i >= 1:
+                quant_v(rest[i - 1])
+            values((1, i))
+            if i != 1:
+                quant_h(added)
+                values((0, added))
+                added = added + 1
+        group_v_vector(rest[TT])
+        sigmoid(TT - 1)
+        load_r(2 * TT - 1)
+        for piece in SCALAR_ROAD[WOVEN:]:
+            group_v(nc.scalar.copy, RUN, piece)
+
+        for n in range(TT):
+            quant_v((1, TT + n))
+            values((1, TT + n))
+            gate_y(n)
+            sigmoid(TT + n)
+            if n + 1 < TT:
+                round_y(nc.scalar.copy, n)
+
+        turn_y(0)
         gate_y(TT)
-        round_v(3)
-        turn_y(1, 2, 2)
-        unload_y(0, 0, 2)
-        round_y(TT)
+        round_y(nc.vector.tensor_copy, TT - 1)
+        turn_y(1)
+        unload_y(0)
+        round_y(nc.scalar.copy, TT)
         gate_y(TT + 1)
         gate_y(TT + 2)
-        round_v(TT + 1)
-        turn_y(2, TT, 2)
-        unload_y(1, 2, 2)
+        round_y(nc.vector.tensor_copy, TT + 1)
+        turn_y(2)
+        unload_y(1)
         gate_y_rounded(TT + 3)
-        round_v(TT + 2)
-        turn_y(3, TT + 2, 2)
-        unload_y(2, TT, 2)
+        round_y(nc.vector.tensor_copy, TT + 2)
+        turn_y(3)
+        unload_y(2)
         gate_y(TT + 3)
-        quant_y(0, 4)
-        store_words(0, 0, TT)
-        unload_y(3, TT + 2, 2)
-        quant_y(TT, 2)
-        store_words(1, 0, 2)
-        quant_y(TT + 2, 2)
-        store_words(1, 2, TT)
+        quant_y(0, 0, T)
+        unload_y(3)
+        quant_y(1, 0, T // 2)
+        quant_y(1, T // 2, T)
         store_scales()

@@ -183,11 +183,12 @@ def tile_rwkv_channel_mix_gated_b14_kernel(
         def quant_x(q):
             quant(xcode[q][:], xscal[q][:], xgrp[q][:])
 
-        def group_k(g, c, lo=0):
+        def group_k(g, lo, hi):
+            raw = kraw[g % N_KRAW][:].rearrange("p j c f -> p j (c f)")
             grouped = kgrp[g % N_KGRP][:].rearrange("p (t w e j) -> p w j t e", t=PACK, e=2, j=PACK)
             nc.vector.tensor_copy(
-                out=grouped[:, (c * KP + lo) // LINE : (c + 1) * KP // LINE],
-                in_=kraw[g % N_KRAW][:, :, c, lo:].rearrange("p j (w e t) -> p w j t e", e=2, t=PACK),
+                out=grouped[:, lo // LINE : hi // LINE],
+                in_=raw[:, :, lo:hi].rearrange("p j (w e t) -> p w j t e", e=2, t=PACK),
             )
 
         def weave_k(bank, g, c):
@@ -351,6 +352,7 @@ def tile_rwkv_channel_mix_gated_b14_kernel(
         load_v((0, 0))
         load_r(1)
         load_k(2)
+        load_r(2)
         sigmoid(0, 0, P)
         nc.vector.tensor_copy(out=ident16[:], in_=ident[:])
         nc.vector.tensor_copy(out=bscale[:], in_=sbytes[:].bitcast(FP8))
@@ -362,13 +364,12 @@ def tile_rwkv_channel_mix_gated_b14_kernel(
         turn_x(1)
         turn_x(0)
         widen_x_scalar(2)
-        group_k(0, 0)
+        group_k(0, 0, KP)
         scale_x(3)
         turn_x(3)
-        group_k(0, 1)
+        group_k(0, KP, D)
         load_k(3)
         load_v((0, 1))
-        load_r(2)
         scale_x(2)
         unload_x(1)
         unload_x(0)
@@ -382,8 +383,7 @@ def tile_rwkv_channel_mix_gated_b14_kernel(
         unload_x(2)
         keys(0, 0)
         keys(0, 1)
-        group_k(1, 0, HALF)
-        group_k(1, 1)
+        group_k(1, HALF, D)
         load_k(4)
         load_v((0, 2))
         load_v(VECTOR_ROAD[0])
@@ -399,6 +399,7 @@ def tile_rwkv_channel_mix_gated_b14_kernel(
         unload_v(banks[1], 0, 0)
         rectify(0, 2)
         rectify(0, 3)
+        sigmoid(2)
         unload_v(banks[2], 0, 1)
 
         copied = 0
@@ -409,17 +410,18 @@ def tile_rwkv_channel_mix_gated_b14_kernel(
                 for i in range(RING):
                     rectify(g, i)
                 square(g - 1)
-            if g == 1:
-                sigmoid(2)
             if woven:
                 weave_v(ring_bank(g, 0), g, 0)
                 weave_v(ring_bank(g, 1), g, 1)
+            if g >= WOVEN:
+                values((0, added))
+                added = added + 1
             keys(g + 1, 0)
             keys(g + 1, 1)
             keys_left = g + 2 < FG
             if keys_left:
-                group_k(g + 2, 0)
-                group_k(g + 2, 1)
+                for lo in range(0, D, KP if g == 0 else D):
+                    group_k(g + 2, lo, lo + (KP if g == 0 else D))
                 if g + 2 + N_KRAW < FG:
                     load_k(g + 2 + N_KRAW)
             if g < WOVEN:
@@ -449,14 +451,11 @@ def tile_rwkv_channel_mix_gated_b14_kernel(
             if woven:
                 unload_v(ring_bank(g, 0), g, 0)
                 unload_v(ring_bank(g, 1), g, 1)
-            count = 2 if g >= WOVEN else (1 if g == FIRST_PLAIN else 0)
-            for j in range(added, added + count)[:1]:
-                values((0, j))
+            if g >= WOVEN or g == FIRST_PLAIN:
+                values((0, added))
+                added = added + 1
             keys(g + 1, 2)
             keys(g + 1, 3)
-            for j in range(added, added + count)[1:]:
-                values((0, j))
-            added = added + count
 
         for i in range(RING):
             rectify(FG - 1, i)

@@ -29,21 +29,13 @@ LINE = 8
 RUN = 4
 RING = 4
 
-WOVEN = 5
-LATE = 2
-SCALAR_ROAD = [(0, g) for g in range(WOVEN)] + [(1, g) for g in range(FG - LATE, FG)]
-VECTOR_ROAD = [(h, g + WOVEN * (1 - h)) for g in range(FG - WOVEN) for h in range(HALVES)] + [
-    (1, g) for g in range(FG - WOVEN, FG - LATE)
-]
-ROADS = [SCALAR_ROAD, VECTOR_ROAD]
-FIRST_PLAIN = 3
+WOVEN = 2
 
-N_KRAW = 3
-N_KGRP = 2
-N_KCODE = 3
-N_VRAW = 3
-N_VGRP = [2, 3]
+N_GRP = 2
+N_KCODE = 4
 N_HGRP = 3
+HALVED = 3
+SLAB = 2 * KP
 
 
 def tile_rwkv_channel_mix_gated_b14_kernel(
@@ -76,18 +68,17 @@ def tile_rwkv_channel_mix_gated_b14_kernel(
         xcode = tiles("xcode", 2, [P, XP * HALF], U32)
         xscal = tiles("xscal", 2, [P, XP * HALF], U8)
         rraw = tiles("rraw", TT, [P, KP], BF16)
-        kraw = tiles("kraw", N_KRAW, [P, PACK, XP, KP], BF16)
-        kgrp = tiles("kgrp", N_KGRP, [P, XP * KP * PACK], BF16)
-        kcode = tiles("kcode", N_KCODE, [P, XP * KP], U32)
-        kscal = tiles("kscal", N_KCODE, [P, XP * KP], U8)
-        vraw = [tiles("vraw%d_" % r, N_VRAW, [P, PACK, KP], BF16) for r in range(2)]
-        vgrp = [tiles("vgrp%d_" % r, N_VGRP[r], [P, KP, PACK], BF16) for r in range(2)]
-        vcode = [tiles("vcode%d_" % h, FG, [P, KP], U32) for h in range(HALVES)]
-        vscal = [tiles("vscal%d_" % h, FG, [P, KP], U8) for h in range(HALVES)]
-        relu = tiles("relu", 2, [P, T * PACK], F32)
+        raw = tiles("raw", 3, [P, 2 * PACK * SLAB], BF16)
+        grp = tiles("grp", N_GRP, [P, SLAB * PACK], BF16)
+        sgrp = sbuf.tile([P, SLAB * PACK], BF16, name="sgrp", align_bytes=64)
+        kcode = tiles("kcode", N_KCODE, [P, SLAB], U32)
+        kscal = tiles("kscal", N_KCODE, [P, SLAB], U8)
+        vcode = tiles("vcode", FG, [P, SLAB], U32)
+        vscal = tiles("vscal", FG, [P, SLAB], U8)
         hgrp = tiles("hgrp", N_HGRP, [P, T * PACK], BF16)
         hcode = tiles("hcode", FG, [P, T], U32)
         hscal = tiles("hscal", FG, [P, T], U8)
+        relu = tiles("relu", 2, [P, T * PACK], F32)
         ycode = tiles("ycode", HALVES, [P, T], U32)
         yscal = sbuf.tile([P, HALVES, T], U8, name="yscal", align_bytes=64)
         gate = [t[:] for t in tiles("gate", TT, [P, KP], F32)] + [
@@ -95,7 +86,7 @@ def tile_rwkv_channel_mix_gated_b14_kernel(
         ]
         yout = [t[:, cut(i, KP)] for t in relu for i in range(TT)]
         ybf = [t[:, cut(i, KP)] for t in xwide + xfull for i in range(2)]
-        ygrp = [kgrp[0][:, cut(h, T * PACK)] for h in range(HALVES)]
+        ygrp = [grp[0][:, cut(h, T * PACK)] for h in range(HALVES)]
 
         def quant(code, scal, src):
             nc.vector.quantize_mx(out=code.bitcast(FP8X4), scales=scal, in_=src)
@@ -115,28 +106,33 @@ def tile_rwkv_channel_mix_gated_b14_kernel(
             h, tt = divmod(n, TT)
             nc.sync.dma_start(out=rraw[tt][:, lo:hi], in_=R[cut(tt, P), h * KP + lo : h * KP + hi])
 
-        def load_k(g):
+        def kraw(s):
+            rows = raw[s // 2 % 2][:]
+            if s < 2:
+                return rows.rearrange("p (g c j f) -> p g j c f", g=2, c=XP, j=PACK)[:, s]
+            return rows.rearrange("p (c j x f) -> p c j x f", c=XP, j=PACK, x=2)[:, s % 2]
+
+        def vraw(g):
+            return raw[(g // 2 + 2) % 3][:].rearrange("p (x j h d) -> p x j h d", x=2, j=PACK, h=HALVES)
+
+        def load_k_group(g):
             for c in range(XP):
                 nc.sync.dma_start(
-                    out=kraw[g % N_KRAW][:, :, c],
+                    out=kraw(g)[:, :, c],
                     in_=Wk[cut(c, KP), cut(g, KP)].rearrange("(p j) f -> p j f", j=PACK),
                 )
 
-        def staged(by_road, piece):
-            r = 0 if piece in SCALAR_ROAD else 1
-            return by_road[r][ROADS[r].index(piece) % len(by_road[r])]
-
-        def load_v(piece):
-            h, g = piece
+        def load_k(s):
             nc.sync.dma_start(
-                out=staged(vraw, piece)[:],
-                in_=Wv[cut(g, KP), cut(h, KP)].rearrange("(p j) d -> p j d", j=PACK),
+                out=kraw(s).rearrange("p j x f -> p j (x f)"),
+                in_=Wk[cut(s % 2, KP), cut(s // 2, SLAB)].rearrange("(p j) f -> p j f", j=PACK),
             )
 
-        def load_behind(piece):
-            road = SCALAR_ROAD if piece in SCALAR_ROAD else VECTOR_ROAD
-            for later in road[road.index(piece) + N_VRAW :][:1]:
-                load_v(later)
+        def load_v(g):
+            nc.sync.dma_start(
+                out=vraw(g)[:, g % 2].rearrange("p j h d -> p (j h d)"),
+                in_=Wv[cut(g, KP), :].rearrange("(p j) d -> p (j d)", j=PACK),
+            )
 
         def x_blocks(a):
             per_row = D // BLOCK
@@ -183,59 +179,72 @@ def tile_rwkv_channel_mix_gated_b14_kernel(
         def quant_x(q):
             quant(xcode[q][:], xscal[q][:], xgrp[q][:])
 
-        def group_k(g, lo, hi):
-            raw = kraw[g % N_KRAW][:].rearrange("p j c f -> p j (c f)")
-            grouped = kgrp[g % N_KGRP][:].rearrange("p (t w e j) -> p w j t e", t=PACK, e=2, j=PACK)
+        def group_k(staged, rows, lo=0):
+            grouped = staged.rearrange("p (t w e j) -> p w j t e", t=PACK, e=2, j=PACK)
             nc.vector.tensor_copy(
-                out=grouped[:, lo // LINE : hi // LINE],
-                in_=raw[:, :, lo:hi].rearrange("p j (w e t) -> p w j t e", e=2, t=PACK),
+                out=grouped[:, lo // LINE :],
+                in_=rows.rearrange("p j (w e t) -> p w j t e", e=2, t=PACK),
             )
 
-        def weave_k(bank, g, c):
+        def group_k_slab(s):
+            group_k(grp[s % N_GRP][:], kraw(s).rearrange("p j x f -> p j (x f)"))
+
+        def group_k_half(s, x, lo=0):
+            group_k(grp[s % N_GRP][:, cut(x, KP * PACK)], kraw(s)[:, :, x, lo:], lo)
+
+        def weave_k(bank, g, part):
             woven = bank[:].bitcast(BF16).rearrange("p (t i m j) -> p i j m t", t=PACK, i=2, j=PACK)
             for i in range(2):
                 nc.tensor.matmul(
                     out=woven[:, i],
                     lhsT=ident16[:],
-                    rhs=kraw[g % N_KRAW][:, :, c, cut(i, P)].rearrange("p j (m t) -> p j m t", t=PACK),
+                    rhs=kraw(g)[:, :, 0, cut(2 * part + i, P)].rearrange("p j (m t) -> p j m t", t=PACK),
                     start=True,
                     stop=True,
                 )
 
-        def unload_k(bank, g, c):
-            words = kgrp[g % N_KGRP][:].bitcast(F32).rearrange("p (t c r w) -> p c r t w", t=PACK, c=XP, r=2)
-            nc.scalar.copy(out=words[:, c, 0], in_=bank[:].rearrange("p (t w) -> p t w", t=PACK))
+        def unload_k(bank, g, part):
+            words = grp[g % N_GRP][:].bitcast(F32).rearrange("p (x t r w) -> p x r t w", t=PACK, x=2, r=2)
+            nc.scalar.copy(out=words[:, 0, part], in_=bank[:].rearrange("p (t w) -> p t w", t=PACK))
 
-        def quant_k(g):
-            quant(kcode[g % N_KCODE][:], kscal[g % N_KCODE][:], kgrp[g % N_KGRP][:])
+        def quant_k(s):
+            quant(kcode[s % N_KCODE][:], kscal[s % N_KCODE][:], grp[s % N_GRP][:])
 
-        def group_v(copy, run, piece):
-            copy(
-                out=staged(vgrp, piece)[:].rearrange("p (c i) j -> p c j i", i=run),
-                in_=staged(vraw, piece)[:].rearrange("p j (c i) -> p c j i", i=run),
+        def key_place(g, c):
+            return (g, c) if g < 2 else (g - g % 2 + c, g % 2)
+
+        def value_place(h, g):
+            return (g, h) if g < WOVEN else (WOVEN + (FG - WOVEN) // 2 * h + (g - WOVEN) // 2, g % 2)
+
+        def group_v(h, g, staged):
+            nc.vector.tensor_copy(
+                out=staged[:].rearrange(
+                    "p (x c i j) -> p x c j i", x=2, i=LINE, j=PACK
+                ),
+                in_=vraw(g)[:, :, :, h].rearrange("p x j (c i) -> p x c j i", i=LINE),
             )
 
-        def group_v_vector(piece):
-            group_v(nc.vector.tensor_copy, LINE, piece)
-            load_behind(piece)
+        def group_v_scalar(g):
+            nc.scalar.copy(
+                out=sgrp[:, cut(g % 2, KP * PACK)].rearrange("p (c i j) -> p c j i", i=RUN, j=PACK),
+                in_=vraw(g)[:, g % 2, :, 1].rearrange("p j (c i) -> p c j i", i=RUN),
+            )
 
-        def weave_v(bank, g, part):
+        def weave_v(bank, h, g, part):
             for i in range(2):
                 nc.tensor.matmul(
                     out=bank[:].bitcast(BF16)[:, cut(i, KP)].rearrange("p (n j) -> p j n", j=PACK),
                     lhsT=ident16[:],
-                    rhs=staged(vraw, (0, g))[:, :, cut(2 * part + i, P)],
+                    rhs=vraw(g)[:, g % 2, :, h, cut(2 * part + i, P)],
                     start=True,
                     stop=True,
                 )
 
         def unload_v(bank, g, part):
-            words = staged(vgrp, (0, g))[:].rearrange("p d j -> p (d j)").bitcast(F32)
-            nc.scalar.copy(out=words[:, cut(part, KP)], in_=bank[:])
+            nc.scalar.copy(out=sgrp[:].bitcast(F32)[:, cut(2 * g + part, KP)], in_=bank[:])
 
-        def quant_v(piece):
-            h, g = piece
-            quant(vcode[h][g][:], vscal[h][g][:], staged(vgrp, piece)[:].rearrange("p d j -> p (d j)"))
+        def quant_v(s, staged, lo=0, hi=SLAB):
+            quant(vcode[s][:, lo:hi], vscal[s][:, lo:hi], staged[:, lo * PACK : hi * PACK])
 
         def ring_bank(g, i):
             return banks[TT + (2 * g + i) % RING]
@@ -244,11 +253,12 @@ def tile_rwkv_channel_mix_gated_b14_kernel(
             q, u = divmod(i, 2)
             for e in range(2):
                 for c in range(XP):
-                    cols = cut((2 * u + e) * XP + c, P)
+                    s, x = key_place(g, c)
+                    cols = cut(PACK * x + 2 * u + e if s < HALVED else (2 * u + e) * 2 + x, P)
                     nc.tensor.matmul_mx(
                         out=ring_bank(g, i)[:, cut(e, HALF)],
-                        lhsT=kcode[g % N_KCODE][:, cols].bitcast(FP8X4),
-                        lhsT_scale=kscal[g % N_KCODE][:, cols],
+                        lhsT=kcode[s % N_KCODE][:, cols].bitcast(FP8X4),
+                        lhsT_scale=kscal[s % N_KCODE][:, cols],
                         rhs=xcode[q][:, cut(c, HALF)].bitcast(FP8X4),
                         rhs_scale=xscal[q][:, cut(c, HALF)],
                         start=(c == 0),
@@ -275,15 +285,15 @@ def tile_rwkv_channel_mix_gated_b14_kernel(
 
         acc = banks[:TT] + [ring_bank(FG - 1, tt) for tt in range(TT)]
 
-        def values(piece):
-            h, g = piece
-            for tt in range(TT):
+        def values(h, g, tts=range(TT)):
+            s, x = value_place(h, g)
+            for tt in tts:
                 nc.tensor.matmul_mx(
                     out=acc[h * TT + tt][:],
                     lhsT=hcode[g][:, cut(tt, P)].bitcast(FP8X4),
                     lhsT_scale=hscal[g][:, cut(tt, P)],
-                    rhs=vcode[h][g][:].bitcast(FP8X4),
-                    rhs_scale=vscal[h][g][:],
+                    rhs=vcode[s][:, cut(x, KP)].bitcast(FP8X4),
+                    rhs_scale=vscal[s][:, cut(x, KP)],
                     start=(g == 0),
                     stop=(g == FG - 1),
                 )
@@ -346,13 +356,14 @@ def tile_rwkv_channel_mix_gated_b14_kernel(
         load_x(0)
         load_rscale()
         load_x(1)
-        load_k(0)
-        load_k(1)
+        load_k_group(0)
+        load_k_group(1)
         load_r(0, P, KP)
-        load_v((0, 0))
-        load_r(1)
         load_k(2)
+        load_r(1)
+        load_k(3)
         load_r(2)
+        load_v(0)
         sigmoid(0, 0, P)
         nc.vector.tensor_copy(out=ident16[:], in_=ident[:])
         nc.vector.tensor_copy(out=bscale[:], in_=sbytes[:].bitcast(FP8))
@@ -364,12 +375,10 @@ def tile_rwkv_channel_mix_gated_b14_kernel(
         turn_x(1)
         turn_x(0)
         widen_x_scalar(2)
-        group_k(0, 0, KP)
+        group_k_half(0, 0)
         scale_x(3)
         turn_x(3)
-        group_k(0, KP, D)
-        load_k(3)
-        load_v((0, 1))
+        group_k_half(0, 1)
         scale_x(2)
         unload_x(1)
         unload_x(0)
@@ -383,79 +392,87 @@ def tile_rwkv_channel_mix_gated_b14_kernel(
         unload_x(2)
         keys(0, 0)
         keys(0, 1)
-        group_k(1, HALF, D)
+        group_k_half(1, 1)
+        group_k_half(1, 0, HALF)
         load_k(4)
-        load_v((0, 2))
-        load_v(VECTOR_ROAD[0])
+        load_k(5)
+        load_v(1)
         quant_x(1)
         quant_k(1)
-        weave_v(banks[1], 0, 0)
+        weave_k(banks[1], 2, 0)
         keys(0, 2)
         keys(0, 3)
-        weave_v(banks[2], 0, 1)
+        weave_k(banks[2], 2, 1)
         rectify(0, 0)
         rectify(0, 1)
         sigmoid(1)
-        unload_v(banks[1], 0, 0)
+        unload_k(banks[1], 2, 0)
         rectify(0, 2)
         rectify(0, 3)
         sigmoid(2)
-        unload_v(banks[2], 0, 1)
+        unload_k(banks[2], 2, 1)
+        group_k_half(2, 1)
 
-        copied = 0
         added = 0
         for g in range(FG - 1):
-            woven = 1 <= g < WOVEN
+            woven = 1 <= g <= 4
+            wg, wh = divmod(g - 1, 2)
             if g >= 1:
                 for i in range(RING):
                     rectify(g, i)
                 square(g - 1)
             if woven:
-                weave_v(ring_bank(g, 0), g, 0)
-                weave_v(ring_bank(g, 1), g, 1)
-            if g >= WOVEN:
-                values((0, added))
-                added = added + 1
-            keys(g + 1, 0)
-            keys(g + 1, 1)
-            keys_left = g + 2 < FG
-            if keys_left:
-                for lo in range(0, D, KP if g == 0 else D):
-                    group_k(g + 2, lo, lo + (KP if g == 0 else D))
-                if g + 2 + N_KRAW < FG:
-                    load_k(g + 2 + N_KRAW)
-            if g < WOVEN:
-                load_behind((0, g))
-            if 1 <= g < N_VRAW:
-                load_v(VECTOR_ROAD[g])
-            if g == N_VRAW:
-                load_r(TT - 1)
-            if keys_left:
-                count = 1 if g >= FIRST_PLAIN and (g - FIRST_PLAIN) % 2 == 0 else 0
+                weave_v(ring_bank(g, 0), wh, wg, 0)
+                weave_v(ring_bank(g, 1), wh, wg, 1)
+            if g <= 4:
+                keys(g + 1, 0)
+                keys(g + 1, 1)
             else:
-                count = 2
-            plain = VECTOR_ROAD[copied : copied + count]
-            copied = copied + count
-            for piece in plain[:1]:
-                group_v_vector(piece)
-            if g >= 2:
+                for i in (2, 3, 0, 1):
+                    keys(g + 1, i)
+            s = g + 3
+            if g == 3:
+                quant_v(0, sgrp)
+            if s < FG:
+                group_k_slab(s)
+            else:
+                group_v(0, 2 * (s - FG) + 2, grp[s % 2])
+            if g == 0:
+                quant_k(2)
+                load_k(6)
+                load_k(7)
+            if g == 2:
+                load_v(2)
+                load_v(3)
+                load_r(3)
+            if g == 4:
+                load_v(4)
+                load_v(5)
+                load_v(6)
+                load_v(7)
+            if g == 1:
+                quant_h(0)
+            if g >= 3:
                 quant_h(g - 2)
-            if 1 <= g <= WOVEN:
-                quant_v((0, g - 1))
-            if keys_left:
-                quant_k(g + 2)
-            for piece in plain[1:]:
-                group_v_vector(piece)
-            for piece in plain:
-                quant_v(piece)
+            if g == 5:
+                quant_v(1, sgrp)
+            if s < FG:
+                quant_k(s)
+            else:
+                quant_v(s - FG + 2, grp[s % 2])
             if woven:
-                unload_v(ring_bank(g, 0), g, 0)
-                unload_v(ring_bank(g, 1), g, 1)
-            if g >= WOVEN or g == FIRST_PLAIN:
-                values((0, added))
+                unload_v(ring_bank(g, 0), wh, 0)
+                unload_v(ring_bank(g, 1), wh, 1)
+            if g == 3:
+                values(0, added)
                 added = added + 1
-            keys(g + 1, 2)
-            keys(g + 1, 3)
+            if g <= 4:
+                keys(g + 1, 2)
+                keys(g + 1, 3)
+            else:
+                values(0, added)
+                values(0, added + 1)
+                added = added + 2
 
         for i in range(RING):
             rectify(FG - 1, i)
@@ -463,31 +480,44 @@ def tile_rwkv_channel_mix_gated_b14_kernel(
         square(FG - 1)
         for n in range(TT, 2 * TT - 1):
             load_r(n)
-        rest = VECTOR_ROAD[copied:]
-        for i in range(TT):
-            group_v_vector(rest[i])
-            if i >= 1:
-                quant_v(rest[i - 1])
-            values((1, i))
-            if i != 1:
-                quant_h(added)
-                values((0, added))
-                added = added + 1
-        group_v_vector(rest[TT])
+        group_v(0, 6, grp[0])
+        values(1, 0)
+        values(1, 1)
+        quant_h(5)
+        values(0, 5)
+        quant_v(4, grp[0])
+        group_v(1, 2, grp[1])
+        quant_h(6)
+        values(0, 6)
+        quant_v(5, grp[1])
+        values(1, 2)
+        values(1, 3)
+        group_v(1, 4, grp[0])
+        quant_h(7)
+        values(0, 7)
         sigmoid(TT - 1)
         load_r(2 * TT - 1)
-        for piece in SCALAR_ROAD[WOVEN:]:
-            group_v(nc.scalar.copy, RUN, piece)
-
+        group_v_scalar(6)
+        group_v_scalar(7)
+        quant_v(6, grp[0])
+        values(1, 4)
+        values(1, 5)
         for n in range(TT):
-            quant_v((1, TT + n))
-            values((1, TT + n))
             gate_y(n)
+            if n < 2:
+                quant_v(7, sgrp, n * KP, (n + 1) * KP)
+            if n == 1:
+                for tt in range(2):
+                    values(1, 6, [tt])
+                    values(1, 7, [tt])
             sigmoid(TT + n)
             if n + 1 < TT:
                 round_y(nc.scalar.copy, n)
 
         turn_y(0)
+        for tt in range(2, TT):
+            values(1, 6, [tt])
+            values(1, 7, [tt])
         gate_y(TT)
         round_y(nc.vector.tensor_copy, TT - 1)
         turn_y(1)

@@ -34,7 +34,8 @@ WOVEN = 2
 N_GRP = 2
 N_KCODE = 4
 N_HGRP = 3
-HALVED = 3
+HALVED = (0, 1, 2, 4)
+PRE = 16
 SLAB = 2 * KP
 
 
@@ -62,12 +63,12 @@ def tile_rwkv_channel_mix_gated_b14_kernel(
         bscale = sbuf.tile([P, TT * D // BLOCK], F32, name="bscale")
         rscale = sbuf.tile([P, TT], F32, name="rscale")
         xbytes = tiles("xbytes", 2, [P, 2, D], U8)
-        xwide = tiles("xwide", 2, [P, D], BF16)
-        xfull = tiles("xfull", 2, [P, D], BF16)
+        xwide = tiles("xwide", TT, [P, D], BF16)
+        xfull = tiles("xfull", TT, [P, D], BF16)
         xgrp = tiles("xgrp", 2, [P, 2 * D], BF16)
         xcode = tiles("xcode", 2, [P, XP * HALF], U32)
         xscal = tiles("xscal", 2, [P, XP * HALF], U8)
-        rraw = tiles("rraw", TT, [P, KP], BF16)
+        rraw = tiles("rraw", 2, [P, D], BF16) + xfull[:2]
         raw = tiles("raw", 3, [P, 2 * PACK * SLAB], BF16)
         grp = tiles("grp", N_GRP, [P, SLAB * PACK], BF16)
         sgrp = sbuf.tile([P, SLAB * PACK], BF16, name="sgrp", align_bytes=64)
@@ -80,12 +81,10 @@ def tile_rwkv_channel_mix_gated_b14_kernel(
         hscal = tiles("hscal", FG, [P, T], U8)
         relu = tiles("relu", 2, [P, T * PACK], F32)
         ycode = tiles("ycode", HALVES, [P, T], U32)
-        yscal = sbuf.tile([P, HALVES, T], U8, name="yscal", align_bytes=64)
-        gate = [t[:] for t in tiles("gate", TT, [P, KP], F32)] + [
-            t[:].bitcast(F32)[:, cut(i, KP)] for t in xgrp for i in range(2)
-        ]
+        yscal = sbuf.tile([P, T], U8, name="yscal", align_bytes=64)
+        gate = [t[:] for t in tiles("gate", 2, [P, D], F32)] + [t[:].bitcast(F32) for t in xgrp]
         yout = [t[:, cut(i, KP)] for t in relu for i in range(TT)]
-        ybf = [t[:, cut(i, KP)] for t in xwide + xfull for i in range(2)]
+        ybf = [t[:, cut(i, KP)] for t in xwide for i in range(2)]
         ygrp = [grp[0][:, cut(h, T * PACK)] for h in range(HALVES)]
 
         def quant(code, scal, src):
@@ -102,9 +101,8 @@ def tile_rwkv_channel_mix_gated_b14_kernel(
                 out=xbytes[q][:], in_=X_bytes.rearrange("(p q a) d -> q p a d", q=2, a=2)[q]
             )
 
-        def load_r(n, lo=0, hi=KP):
-            h, tt = divmod(n, TT)
-            nc.sync.dma_start(out=rraw[tt][:, lo:hi], in_=R[cut(tt, P), h * KP + lo : h * KP + hi])
+        def load_r(tt, lo=0, hi=D):
+            nc.sync.dma_start(out=rraw[tt][:, lo:hi], in_=R[cut(tt, P), lo:hi])
 
         def kraw(s):
             rows = raw[s // 2 % 2][:]
@@ -138,7 +136,7 @@ def tile_rwkv_channel_mix_gated_b14_kernel(
             per_row = D // BLOCK
             return [
                 (
-                    xwide[a % 2][:, cut(b, BLOCK)],
+                    xwide[a][:, cut(b, BLOCK)],
                     xbytes[a // 2][:, a % 2, cut(b, BLOCK)].bitcast(FP8),
                     bscale[:, a * per_row + b : a * per_row + b + 1],
                 )
@@ -155,42 +153,38 @@ def tile_rwkv_channel_mix_gated_b14_kernel(
 
         def scale_x(a):
             nc.vector.tensor_scalar(
-                out=xfull[a % 2][:], in0=xwide[a % 2][:], scalar1=rscale[:, a : a + 1],
-                scalar2=None, op0=ALU.mult,
+                out=xfull[a][:].rearrange("p (u w e) -> p u w e", u=2, e=2),
+                in0=xwide[a][:].rearrange("p (w u e) -> p u w e", u=2, e=2),
+                scalar1=rscale[:, a : a + 1], scalar2=None, op0=ALU.mult,
             )
 
         def turn_x(a):
-            words = xfull[a % 2][:].bitcast(F32)
-            for c in range(XP):
-                for u in range(2):
-                    nc.tensor.transpose(
-                        banks[TT + a][:, cut(2 * c + u, P)],
-                        words[:, 2 * P * c + u : 2 * P * (c + 1) : 2],
-                        ident[:],
-                    )
+            words = xfull[a][:].bitcast(F32)
+            for i in range(2 * XP):
+                nc.tensor.transpose(banks[TT + a][:, cut(i, P)], words[:, cut(i, P)], ident[:])
 
         def unload_x(a):
             words = xgrp[a // 2][:].bitcast(F32).rearrange("p (c a n u) -> p a c n u", c=XP, a=2, u=2)
             nc.scalar.copy(
                 out=words[:, a % 2],
-                in_=banks[TT + a][:].rearrange("p (c u n) -> p c n u", c=XP, u=2),
+                in_=banks[TT + a][:].rearrange("p (u c n) -> p c n u", c=XP, u=2),
             )
 
         def quant_x(q):
             quant(xcode[q][:], xscal[q][:], xgrp[q][:])
 
-        def group_k(staged, rows, lo=0):
+        def group_k(copy, staged, rows, lo=0):
             grouped = staged.rearrange("p (t w e j) -> p w j t e", t=PACK, e=2, j=PACK)
-            nc.vector.tensor_copy(
+            copy(
                 out=grouped[:, lo // LINE :],
                 in_=rows.rearrange("p j (w e t) -> p w j t e", e=2, t=PACK),
             )
 
         def group_k_slab(s):
-            group_k(grp[s % N_GRP][:], kraw(s).rearrange("p j x f -> p j (x f)"))
+            group_k(nc.vector.tensor_copy, grp[s % N_GRP][:], kraw(s).rearrange("p j x f -> p j (x f)"))
 
-        def group_k_half(s, x, lo=0):
-            group_k(grp[s % N_GRP][:, cut(x, KP * PACK)], kraw(s)[:, :, x, lo:], lo)
+        def group_k_half(s, x, lo=0, copy=nc.vector.tensor_copy):
+            group_k(copy, grp[s % N_GRP][:, cut(x, KP * PACK)], kraw(s)[:, :, x, lo:], lo)
 
         def weave_k(bank, g, part):
             woven = bank[:].bitcast(BF16).rearrange("p (t i m j) -> p i j m t", t=PACK, i=2, j=PACK)
@@ -224,6 +218,12 @@ def tile_rwkv_channel_mix_gated_b14_kernel(
                 in_=vraw(g)[:, :, :, h].rearrange("p x j (c i) -> p x c j i", i=LINE),
             )
 
+        def group_v_one(h, g):
+            nc.vector.tensor_copy(
+                out=sgrp[:, cut(h, KP * PACK)].rearrange("p (c i j) -> p c j i", i=LINE, j=PACK),
+                in_=vraw(g)[:, g % 2, :, h].rearrange("p j (c i) -> p c j i", i=LINE),
+            )
+
         def group_v_scalar(g):
             nc.scalar.copy(
                 out=sgrp[:, cut(g % 2, KP * PACK)].rearrange("p (c i j) -> p c j i", i=RUN, j=PACK),
@@ -254,7 +254,7 @@ def tile_rwkv_channel_mix_gated_b14_kernel(
             for e in range(2):
                 for c in range(XP):
                     s, x = key_place(g, c)
-                    cols = cut(PACK * x + 2 * u + e if s < HALVED else (2 * u + e) * 2 + x, P)
+                    cols = cut(PACK * x + 2 * u + e if s in HALVED else (2 * u + e) * 2 + x, P)
                     nc.tensor.matmul_mx(
                         out=ring_bank(g, i)[:, cut(e, HALF)],
                         lhsT=kcode[s % N_KCODE][:, cols].bitcast(FP8X4),
@@ -298,12 +298,16 @@ def tile_rwkv_channel_mix_gated_b14_kernel(
                     stop=(g == FG - 1),
                 )
 
-        def sigmoid(n, lo=0, hi=KP):
-            nc.scalar.activation(out=gate[n][:, lo:hi], in_=rraw[n % TT][:, lo:hi], func=ACT.Sigmoid)
+        def sigmoid(tt, lo=0, hi=D):
+            nc.scalar.activation(out=gate[tt][:, lo:hi], in_=rraw[tt][:, lo:hi], func=ACT.Sigmoid)
+
+        def gate_of(n):
+            h, tt = divmod(n, TT)
+            return gate[tt][:, cut(h, KP)]
 
         def gate_y(n):
             h, tt = divmod(n, TT)
-            nc.vector.tensor_tensor(out=yout[n], in0=acc[n][:], in1=gate[n], op=ALU.mult)
+            nc.vector.tensor_tensor(out=yout[n], in0=acc[n][:], in1=gate_of(n), op=ALU.mult)
             nc.sync.dma_start(out=out_0[cut(tt, P), cut(h, KP)], in_=yout[n])
 
         def as_stored(ap):
@@ -317,7 +321,7 @@ def tile_rwkv_channel_mix_gated_b14_kernel(
 
         def gate_y_rounded(n):
             nc.vector.tensor_tensor(
-                out=as_sorted(ybf[n]), in0=as_stored(acc[n][:]), in1=as_stored(gate[n]), op=ALU.mult
+                out=as_sorted(ybf[n]), in0=as_stored(acc[n][:]), in1=as_stored(gate_of(n)), op=ALU.mult
             )
 
         def turn_y(pair):
@@ -334,7 +338,7 @@ def tile_rwkv_channel_mix_gated_b14_kernel(
             )
 
         def quant_y(h, lo, hi):
-            quant(ycode[h][:, lo:hi], yscal[:, h, lo:hi], ygrp[h][:, lo * PACK : hi * PACK])
+            quant(ycode[h][:, lo:hi], yscal[PACK * h :, lo:hi], ygrp[h][:, lo * PACK : hi * PACK])
             nc.sync.dma_start(
                 out=out_1[h].rearrange("p m t -> p (m t)").bitcast(I32)[:, lo:hi],
                 in_=ycode[h][:, lo:hi].bitcast(I32),
@@ -344,176 +348,210 @@ def tile_rwkv_channel_mix_gated_b14_kernel(
             for q in range(4):
                 queue = nc.scalar if q % 2 == 0 else nc.sync
                 queue.dma_start(
-                    out=out_2[:, cut(q, 4), :].rearrange("h r m -> r h m").bitcast(I32),
-                    in_=yscal[32 * q : 32 * q + 4].bitcast(I32),
+                    out=out_2[:, cut(q, 4), :].bitcast(I32),
+                    in_=yscal[32 * q : 32 * q + 8].bitcast(I32),
                 )
 
         ctx.enter_context(tc.manual_schedule())
 
         make_identity(nc, ident[:])
         load_scales()
-        load_r(0, 0, P)
+        load_r(0, 0, PRE)
         load_x(0)
         load_rscale()
         load_x(1)
         load_k_group(0)
         load_k_group(1)
-        load_r(0, P, KP)
         load_k(2)
-        load_r(1)
         load_k(3)
-        load_r(2)
-        load_v(0)
-        sigmoid(0, 0, P)
+        load_r(0, PRE, D)
+        sigmoid(0, 0, PRE)
         nc.vector.tensor_copy(out=ident16[:], in_=ident[:])
         nc.vector.tensor_copy(out=bscale[:], in_=sbytes[:].bitcast(FP8))
         widen_x_vector(1)
         widen_x_scalar(0)
-        scale_x(1)
+        widen_x_vector(2)
         widen_x_scalar(3)
+        scale_x(1)
         scale_x(0)
+        scale_x(2)
         turn_x(1)
         turn_x(0)
-        widen_x_scalar(2)
+        turn_x(2)
         group_k_half(0, 0)
         scale_x(3)
         turn_x(3)
-        group_k_half(0, 1)
-        scale_x(2)
         unload_x(1)
         unload_x(0)
-        unload_x(3)
-        sigmoid(0, P, KP)
-        weave_k(banks[0], 1, 0)
-        turn_x(2)
-        quant_k(0)
-        quant_x(0)
-        unload_k(banks[0], 1, 0)
         unload_x(2)
+        unload_x(3)
+        group_k_half(0, 1)
+        weave_k(banks[0], 1, 0)
+        group_k_half(1, 0, HALF, nc.scalar.copy)
+        quant_x(0)
+        quant_k(0)
+        unload_k(banks[0], 1, 0)
         keys(0, 0)
         keys(0, 1)
-        group_k_half(1, 1)
-        group_k_half(1, 0, HALF)
-        load_k(4)
-        load_k(5)
-        load_v(1)
         quant_x(1)
-        quant_k(1)
-        weave_k(banks[1], 2, 0)
+        group_k_half(1, 1)
+        load_k(4)
+        load_r(1)
+        load_k(5)
+        load_v(0)
         keys(0, 2)
         keys(0, 3)
-        weave_k(banks[2], 2, 1)
-        rectify(0, 0)
-        rectify(0, 1)
-        sigmoid(1)
-        unload_k(banks[1], 2, 0)
-        rectify(0, 2)
-        rectify(0, 3)
-        sigmoid(2)
-        unload_k(banks[2], 2, 1)
+        quant_k(1)
         group_k_half(2, 1)
-
-        added = 0
-        for g in range(FG - 1):
-            woven = 1 <= g <= 4
-            wg, wh = divmod(g - 1, 2)
-            if g >= 1:
-                for i in range(RING):
-                    rectify(g, i)
-                square(g - 1)
-            if woven:
-                weave_v(ring_bank(g, 0), wh, wg, 0)
-                weave_v(ring_bank(g, 1), wh, wg, 1)
-            if g <= 4:
-                keys(g + 1, 0)
-                keys(g + 1, 1)
-            else:
-                for i in (2, 3, 0, 1):
-                    keys(g + 1, i)
-            s = g + 3
-            if g == 3:
-                quant_v(0, sgrp)
-            if s < FG:
-                group_k_slab(s)
-            else:
-                group_v(0, 2 * (s - FG) + 2, grp[s % 2])
-            if g == 0:
-                quant_k(2)
-                load_k(6)
-                load_k(7)
-            if g == 2:
-                load_v(2)
-                load_v(3)
-                load_r(3)
-            if g == 4:
-                load_v(4)
-                load_v(5)
-                load_v(6)
-                load_v(7)
-            if g == 1:
-                quant_h(0)
-            if g >= 3:
-                quant_h(g - 2)
-            if g == 5:
-                quant_v(1, sgrp)
-            if s < FG:
-                quant_k(s)
-            else:
-                quant_v(s - FG + 2, grp[s % 2])
-            if woven:
-                unload_v(ring_bank(g, 0), wh, 0)
-                unload_v(ring_bank(g, 1), wh, 1)
-            if g == 3:
-                values(0, added)
-                added = added + 1
-            if g <= 4:
-                keys(g + 1, 2)
-                keys(g + 1, 3)
-            else:
-                values(0, added)
-                values(0, added + 1)
-                added = added + 2
-
+        weave_k(banks[1], 2, 0)
+        weave_k(banks[2], 2, 1)
         for i in range(RING):
-            rectify(FG - 1, i)
-        square(FG - 2)
-        square(FG - 1)
-        for n in range(TT, 2 * TT - 1):
-            load_r(n)
-        group_v(0, 6, grp[0])
+            rectify(0, i)
+        square(0)
+        unload_k(banks[1], 2, 0)
+        unload_k(banks[2], 2, 1)
+        keys(1, 0)
+        keys(1, 1)
+        keys(1, 2)
+        keys(1, 3)
+        group_k_slab(3)
+        quant_k(2)
+        quant_k(3)
+        load_k(6)
+        load_k(7)
+        load_v(1)
+        for i in range(RING):
+            rectify(1, i)
+        sigmoid(0, PRE, D)
+        sigmoid(1)
+        weave_k(ring_bank(1, 0), 4, 0)
+        weave_k(ring_bank(1, 1), 4, 1)
+        keys(2, 0)
+        keys(2, 1)
+        group_k_half(4, 1)
+        quant_h(0)
+        group_k_slab(5)
+        unload_k(ring_bank(1, 0), 4, 0)
+        unload_k(ring_bank(1, 1), 4, 1)
+        keys(2, 2)
+        keys(2, 3)
+        quant_k(4)
+        quant_k(5)
+        load_v(2)
+        load_v(3)
+        for i in range(RING):
+            rectify(2, i)
+        square(1)
+        weave_v(ring_bank(2, 0), 0, 0, 0)
+        weave_v(ring_bank(2, 1), 0, 0, 1)
+        keys(3, 0)
+        keys(3, 1)
+        group_k_slab(6)
+        quant_h(1)
+        unload_v(ring_bank(2, 0), 0, 0)
+        unload_v(ring_bank(2, 1), 0, 1)
+        keys(3, 2)
+        keys(3, 3)
+        quant_k(6)
+        for i in range(RING):
+            rectify(3, i)
+        square(2)
+        weave_v(ring_bank(3, 0), 1, 0, 0)
+        weave_v(ring_bank(3, 1), 1, 0, 1)
+        keys(4, 0)
+        keys(4, 1)
+        group_k_slab(7)
+        load_v(4)
+        load_v(5)
+        load_v(6)
+        quant_h(2)
+        quant_k(7)
+        unload_v(ring_bank(3, 0), 1, 0)
+        unload_v(ring_bank(3, 1), 1, 1)
+        keys(4, 2)
+        keys(4, 3)
+        quant_v(0, sgrp)
+        for i in range(RING):
+            rectify(4, i)
+        square(3)
+        weave_v(ring_bank(4, 0), 0, 1, 0)
+        weave_v(ring_bank(4, 1), 0, 1, 1)
+        keys(5, 0)
+        keys(5, 1)
+        group_v_one(1, 1)
+        load_v(7)
+        load_r(2)
+        load_r(3)
+        group_v(0, 2, grp[0])
+        quant_h(3)
+        unload_v(ring_bank(4, 0), 0, 0)
+        unload_v(ring_bank(4, 1), 0, 1)
+        values(0, 0)
+        keys(5, 2)
+        keys(5, 3)
+        quant_v(1, sgrp)
+        quant_v(2, grp[0])
+        for i in range(RING):
+            rectify(5, i)
+        square(4)
+        keys(6, 2)
+        keys(6, 3)
+        keys(6, 0)
+        keys(6, 1)
+        values(0, 1)
+        values(0, 2)
+        group_v(0, 4, grp[1])
+        quant_h(4)
+        quant_v(3, grp[1])
+        for i in range(RING):
+            rectify(6, i)
+        square(5)
+        keys(7, 2)
+        keys(7, 3)
+        keys(7, 0)
+        keys(7, 1)
+        values(0, 3)
+        values(0, 4)
+        group_v(1, 2, grp[0])
+        quant_h(5)
+        quant_v(5, grp[0])
+        for i in range(RING):
+            rectify(7, i)
+        square(6)
+        square(7)
+        values(0, 5)
         values(1, 0)
         values(1, 1)
-        quant_h(5)
-        values(0, 5)
-        quant_v(4, grp[0])
-        group_v(1, 2, grp[1])
+        group_v(0, 6, grp[1])
         quant_h(6)
-        values(0, 6)
-        quant_v(5, grp[1])
+        quant_v(4, grp[1])
         values(1, 2)
+        values(0, 6)
         values(1, 3)
         group_v(1, 4, grp[0])
         quant_h(7)
         values(0, 7)
-        sigmoid(TT - 1)
-        load_r(2 * TT - 1)
-        group_v_scalar(6)
-        group_v_scalar(7)
         quant_v(6, grp[0])
         values(1, 4)
         values(1, 5)
-        for n in range(TT):
-            gate_y(n)
-            if n < 2:
-                quant_v(7, sgrp, n * KP, (n + 1) * KP)
-            if n == 1:
-                for tt in range(2):
-                    values(1, 6, [tt])
-                    values(1, 7, [tt])
-            sigmoid(TT + n)
-            if n + 1 < TT:
-                round_y(nc.scalar.copy, n)
-
+        sigmoid(2, 0, KP)
+        group_v_scalar(6)
+        group_v_scalar(7)
+        sigmoid(3, 0, KP)
+        gate_y(0)
+        quant_v(7, sgrp, 0, KP)
+        gate_y(1)
+        quant_v(7, sgrp, KP, SLAB)
+        for tt in range(2):
+            values(1, 6, [tt])
+            values(1, 7, [tt])
+        round_y(nc.scalar.copy, 0)
+        round_y(nc.scalar.copy, 1)
+        gate_y(2)
+        gate_y(3)
+        sigmoid(2, KP, D)
+        round_y(nc.scalar.copy, 2)
+        sigmoid(3, KP, D)
         turn_y(0)
         for tt in range(2, TT):
             values(1, 6, [tt])

@@ -63,12 +63,12 @@ def tile_rwkv_channel_mix_gated_b14_kernel(
         bscale = sbuf.tile([P, TT * D // BLOCK], F32, name="bscale")
         rscale = sbuf.tile([P, TT], F32, name="rscale")
         xbytes = tiles("xbytes", 2, [P, 2, D], U8)
-        xwide = tiles("xwide", TT, [P, D], BF16)
-        xfull = tiles("xfull", TT, [P, D], BF16)
+        xwide = [t[:] for t in tiles("xwide", 2, [P, D], BF16)]
+        xfull = [t[:] for t in tiles("xfull", 2, [P, D], BF16)]
         xgrp = tiles("xgrp", 2, [P, 2 * D], BF16)
         xcode = tiles("xcode", 2, [P, XP * HALF], U32)
         xscal = tiles("xscal", 2, [P, XP * HALF], U8)
-        rraw = tiles("rraw", 2, [P, D], BF16) + xfull[:2]
+        rraw = [t[:] for t in tiles("rraw", 2, [P, D], BF16)] + xfull
         raw = tiles("raw", 3, [P, 2 * PACK * SLAB], BF16)
         grp = tiles("grp", N_GRP, [P, SLAB * PACK], BF16)
         sgrp = sbuf.tile([P, SLAB * PACK], BF16, name="sgrp", align_bytes=64)
@@ -77,6 +77,8 @@ def tile_rwkv_channel_mix_gated_b14_kernel(
         vcode = tiles("vcode", FG, [P, SLAB], U32)
         vscal = tiles("vscal", FG, [P, SLAB], U8)
         hgrp = tiles("hgrp", N_HGRP, [P, T * PACK], BF16)
+        xwide = xwide + [hgrp[1][:, cut(i, D)] for i in range(2)]
+        xfull = xfull + [hgrp[2][:, cut(i, D)] for i in range(2)]
         hcode = tiles("hcode", FG, [P, T], U32)
         hscal = tiles("hscal", FG, [P, T], U8)
         relu = tiles("relu", 2, [P, T * PACK], F32)
@@ -153,13 +155,13 @@ def tile_rwkv_channel_mix_gated_b14_kernel(
 
         def scale_x(a):
             nc.vector.tensor_scalar(
-                out=xfull[a][:].rearrange("p (u w e) -> p u w e", u=2, e=2),
-                in0=xwide[a][:].rearrange("p (w u e) -> p u w e", u=2, e=2),
+                out=xfull[a].rearrange("p (u w e) -> p u w e", u=2, e=2),
+                in0=xwide[a].rearrange("p (w u e) -> p u w e", u=2, e=2),
                 scalar1=rscale[:, a : a + 1], scalar2=None, op0=ALU.mult,
             )
 
         def turn_x(a):
-            words = xfull[a][:].bitcast(F32)
+            words = xfull[a].bitcast(F32)
             for i in range(2 * XP):
                 nc.tensor.transpose(banks[TT + a][:, cut(i, P)], words[:, cut(i, P)], ident[:])
 
@@ -362,9 +364,9 @@ def tile_rwkv_channel_mix_gated_b14_kernel(
         load_x(1)
         load_k_group(0)
         load_k_group(1)
+        load_r(0, PRE, D)
         load_k(2)
         load_k(3)
-        load_r(0, PRE, D)
         sigmoid(0, 0, PRE)
         nc.vector.tensor_copy(out=ident16[:], in_=ident[:])
         nc.vector.tensor_copy(out=bscale[:], in_=sbytes[:].bitcast(FP8))
@@ -385,9 +387,9 @@ def tile_rwkv_channel_mix_gated_b14_kernel(
         unload_x(0)
         unload_x(2)
         unload_x(3)
+        sigmoid(0, PRE, D)
         group_k_half(0, 1)
         weave_k(banks[0], 1, 0)
-        group_k_half(1, 0, HALF, nc.scalar.copy)
         quant_x(0)
         quant_k(0)
         unload_k(banks[0], 1, 0)
@@ -395,14 +397,15 @@ def tile_rwkv_channel_mix_gated_b14_kernel(
         keys(0, 1)
         quant_x(1)
         group_k_half(1, 1)
+        group_k_half(1, 0, HALF)
         load_k(4)
         load_r(1)
         load_k(5)
         load_v(0)
         keys(0, 2)
         keys(0, 3)
-        quant_k(1)
         group_k_half(2, 1)
+        quant_k(1)
         weave_k(banks[1], 2, 0)
         weave_k(banks[2], 2, 1)
         for i in range(RING):
@@ -422,7 +425,6 @@ def tile_rwkv_channel_mix_gated_b14_kernel(
         load_v(1)
         for i in range(RING):
             rectify(1, i)
-        sigmoid(0, PRE, D)
         sigmoid(1)
         weave_k(ring_bank(1, 0), 4, 0)
         weave_k(ring_bank(1, 1), 4, 1)

@@ -34,8 +34,12 @@ WOVEN = 2
 N_GRP = 2
 N_KCODE = 4
 N_HGRP = 3
-HALVED = (0, 1, 2, 4)
+KEY_SLOT = (0, 1, 2, 3, 4, 5, 0, 3)
+VALUE_SLOT = (1, 2, 4, 5, 2, 3, 0, 1)
+KEY_STAGE = (0, 1, 0, 0, 0, 1, 0, 1)
+HALVED = (0, 1, 2, 4, 6, 7)
 PRE = 16
+FIRST = (1, 0)
 SLAB = 2 * KP
 
 
@@ -106,14 +110,19 @@ def tile_rwkv_channel_mix_gated_b14_kernel(
         def load_r(tt, lo=0, hi=D):
             nc.sync.dma_start(out=rraw[tt][:, lo:hi], in_=R[cut(tt, P), lo:hi])
 
+        def slot(i):
+            return raw[i // 2][:, cut(i % 2, PACK * SLAB)]
+
         def kraw(s):
-            rows = raw[s // 2 % 2][:]
-            if s < 2:
-                return rows.rearrange("p (g c j f) -> p g j c f", g=2, c=XP, j=PACK)[:, s]
-            return rows.rearrange("p (c j x f) -> p c j x f", c=XP, j=PACK, x=2)[:, s % 2]
+            if s in (0, 1, FG - 1):
+                return slot(KEY_SLOT[s]).rearrange("p (c j f) -> p j c f", c=XP, j=PACK)
+            return slot(KEY_SLOT[s]).rearrange("p (j x f) -> p j x f", j=PACK, x=2)
 
         def vraw(g):
-            return raw[(g // 2 + 2) % 3][:].rearrange("p (x j h d) -> p x j h d", x=2, j=PACK, h=HALVES)
+            return slot(VALUE_SLOT[g]).rearrange("p (j h d) -> p j h d", j=PACK, h=HALVES)
+
+        def vraw_pair(g):
+            return raw[VALUE_SLOT[g] // 2][:].rearrange("p (x j h d) -> p x j h d", x=2, j=PACK, h=HALVES)
 
         def load_k_group(g):
             for c in range(XP):
@@ -122,15 +131,22 @@ def tile_rwkv_channel_mix_gated_b14_kernel(
                     in_=Wk[cut(c, KP), cut(g, KP)].rearrange("(p j) f -> p j f", j=PACK),
                 )
 
+        def load_k_part(s, x, c, g):
+            nc.sync.dma_start(
+                out=kraw(s)[:, :, x],
+                in_=Wk[cut(c, KP), cut(g, KP)].rearrange("(p j) f -> p j f", j=PACK),
+            )
+
         def load_k(s):
+            first = KP + (s - 1) // 2 * SLAB
             nc.sync.dma_start(
                 out=kraw(s).rearrange("p j x f -> p j (x f)"),
-                in_=Wk[cut(s % 2, KP), cut(s // 2, SLAB)].rearrange("(p j) f -> p j f", j=PACK),
+                in_=Wk[cut((s - 1) % 2, KP), first : first + SLAB].rearrange("(p j) f -> p j f", j=PACK),
             )
 
         def load_v(g):
             nc.sync.dma_start(
-                out=vraw(g)[:, g % 2].rearrange("p j h d -> p (j h d)"),
+                out=vraw(g).rearrange("p j h d -> p (j h d)"),
                 in_=Wv[cut(g, KP), :].rearrange("(p j) d -> p (j d)", j=PACK),
             )
 
@@ -182,54 +198,58 @@ def tile_rwkv_channel_mix_gated_b14_kernel(
                 in_=rows.rearrange("p j (w e t) -> p w j t e", e=2, t=PACK),
             )
 
+        def kstage(s):
+            return sgrp if s in (2, 4, 6) else grp[KEY_STAGE[s]]
+
         def group_k_slab(s):
-            group_k(nc.vector.tensor_copy, grp[s % N_GRP][:], kraw(s).rearrange("p j x f -> p j (x f)"))
+            group_k(nc.vector.tensor_copy, kstage(s)[:], kraw(s).rearrange("p j x f -> p j (x f)"))
 
-        def group_k_half(s, x, lo=0, copy=nc.vector.tensor_copy):
-            group_k(copy, grp[s % N_GRP][:, cut(x, KP * PACK)], kraw(s)[:, :, x, lo:], lo)
+        def group_k_half(s, x, lo=0):
+            group_k(nc.vector.tensor_copy, kstage(s)[:, cut(x, KP * PACK)], kraw(s)[:, :, x, lo:], lo)
 
-        def weave_k(bank, g, part):
+        def weave_k(bank, s, x, part):
             woven = bank[:].bitcast(BF16).rearrange("p (t i m j) -> p i j m t", t=PACK, i=2, j=PACK)
             for i in range(2):
                 nc.tensor.matmul(
                     out=woven[:, i],
                     lhsT=ident16[:],
-                    rhs=kraw(g)[:, :, 0, cut(2 * part + i, P)].rearrange("p j (m t) -> p j m t", t=PACK),
+                    rhs=kraw(s)[:, :, x, cut(2 * part + i, P)].rearrange("p j (m t) -> p j m t", t=PACK),
                     start=True,
                     stop=True,
                 )
 
-        def unload_k(bank, g, part):
-            words = grp[g % N_GRP][:].bitcast(F32).rearrange("p (x t r w) -> p x r t w", t=PACK, x=2, r=2)
-            nc.scalar.copy(out=words[:, 0, part], in_=bank[:].rearrange("p (t w) -> p t w", t=PACK))
+        def unload_k(bank, s, x, part):
+            words = kstage(s)[:].bitcast(F32).rearrange("p (x t r w) -> p x r t w", t=PACK, x=2, r=2)
+            nc.scalar.copy(out=words[:, x, part], in_=bank[:].rearrange("p (t w) -> p t w", t=PACK))
 
-        def quant_k(s):
-            quant(kcode[s % N_KCODE][:], kscal[s % N_KCODE][:], grp[s % N_GRP][:])
+        def quant_k(s, lo=0, hi=SLAB):
+            quant(kcode[s % N_KCODE][:, lo:hi], kscal[s % N_KCODE][:, lo:hi], kstage(s)[:, lo * PACK : hi * PACK])
+
+        def quant_k_half(s, x):
+            quant_k(s, x * KP, (x + 1) * KP)
 
         def key_place(g, c):
-            return (g, c) if g < 2 else (g - g % 2 + c, g % 2)
+            return (g, c) if g in (0, FG - 1) else (1 + (g - 1) // 2 * 2 + c, (g - 1) % 2)
 
         def value_place(h, g):
             return (g, h) if g < WOVEN else (WOVEN + (FG - WOVEN) // 2 * h + (g - WOVEN) // 2, g % 2)
 
         def group_v(h, g, staged):
             nc.vector.tensor_copy(
-                out=staged[:].rearrange(
-                    "p (x c i j) -> p x c j i", x=2, i=LINE, j=PACK
-                ),
-                in_=vraw(g)[:, :, :, h].rearrange("p x j (c i) -> p x c j i", i=LINE),
+                out=staged[:].rearrange("p (x c i j) -> p x c j i", x=2, i=LINE, j=PACK),
+                in_=vraw_pair(g)[:, :, :, h].rearrange("p x j (c i) -> p x c j i", i=LINE),
             )
 
-        def group_v_one(h, g):
+        def group_v_both(g, staged):
             nc.vector.tensor_copy(
-                out=sgrp[:, cut(h, KP * PACK)].rearrange("p (c i j) -> p c j i", i=LINE, j=PACK),
-                in_=vraw(g)[:, g % 2, :, h].rearrange("p j (c i) -> p c j i", i=LINE),
+                out=staged[:].rearrange("p (c i j) -> p c j i", i=LINE, j=PACK),
+                in_=vraw(g).rearrange("p j h (c i) -> p (h c) j i", i=LINE),
             )
 
         def group_v_scalar(g):
             nc.scalar.copy(
                 out=sgrp[:, cut(g % 2, KP * PACK)].rearrange("p (c i j) -> p c j i", i=RUN, j=PACK),
-                in_=vraw(g)[:, g % 2, :, 1].rearrange("p j (c i) -> p c j i", i=RUN),
+                in_=vraw(g)[:, :, 1].rearrange("p j (c i) -> p c j i", i=RUN),
             )
 
         def weave_v(bank, h, g, part):
@@ -237,19 +257,19 @@ def tile_rwkv_channel_mix_gated_b14_kernel(
                 nc.tensor.matmul(
                     out=bank[:].bitcast(BF16)[:, cut(i, KP)].rearrange("p (n j) -> p j n", j=PACK),
                     lhsT=ident16[:],
-                    rhs=vraw(g)[:, g % 2, :, h, cut(2 * part + i, P)],
+                    rhs=vraw(g)[:, :, h, cut(2 * part + i, P)],
                     start=True,
                     stop=True,
                 )
 
-        def unload_v(bank, g, part):
-            nc.scalar.copy(out=sgrp[:].bitcast(F32)[:, cut(2 * g + part, KP)], in_=bank[:])
+        def unload_v(bank, h, part):
+            nc.scalar.copy(out=sgrp[:].bitcast(F32)[:, cut(2 * h + part, KP)], in_=bank[:])
 
         def quant_v(s, staged, lo=0, hi=SLAB):
             quant(vcode[s][:, lo:hi], vscal[s][:, lo:hi], staged[:, lo * PACK : hi * PACK])
 
         def ring_bank(g, i):
-            return banks[TT + (2 * g + i) % RING]
+            return banks[TT + i]
 
         def keys(g, i):
             q, u = divmod(i, 2)
@@ -268,19 +288,28 @@ def tile_rwkv_channel_mix_gated_b14_kernel(
                     )
 
         def rectify(g, i):
-            q, u = divmod(i, 2)
             nc.scalar.activation(
-                out=relu[g % 2][:].rearrange("p (u n q a e) -> p u q n a e", u=2, q=2, a=2, e=2)[:, u, q],
+                out=relu[g % 2][:, cut(i, KP)].rearrange("p (n a e) -> p n a e", a=2, e=2),
                 in_=ring_bank(g, i)[:].rearrange("p (e a n) -> p n a e", e=2, a=2),
                 func=ACT.Relu,
             )
 
-        def square(g):
+        def square(g, q):
             nc.scalar.activation(
-                out=hgrp[g % N_HGRP][:].rearrange("p (m u e) -> p m u e", u=2, e=2),
-                in_=relu[g % 2][:].rearrange("p (u m e) -> p m u e", u=2, e=2),
+                out=hgrp[g % N_HGRP][:].rearrange("p (n q a u e) -> p q n a u e", q=2, a=2, u=2, e=2)[:, q],
+                in_=relu[g % 2][:].rearrange("p (q u n a e) -> p q n a u e", q=2, a=2, u=2, e=2)[:, q],
                 func=ACT.Square,
             )
+
+        def rectify_square(g):
+            for i in range(RING):
+                rectify(g, i)
+            for q in range(2):
+                square(g, q)
+
+        def keys_all(g):
+            for i in range(RING):
+                keys(g, i)
 
         def quant_h(g):
             quant(hcode[g][:], hscal[g][:], hgrp[g % N_HGRP][:])
@@ -296,7 +325,7 @@ def tile_rwkv_channel_mix_gated_b14_kernel(
                     lhsT_scale=hscal[g][:, cut(tt, P)],
                     rhs=vcode[s][:, cut(x, KP)].bitcast(FP8X4),
                     rhs_scale=vscal[s][:, cut(x, KP)],
-                    start=(g == 0),
+                    start=(g == FIRST[h]),
                     stop=(g == FG - 1),
                 )
 
@@ -341,6 +370,8 @@ def tile_rwkv_channel_mix_gated_b14_kernel(
 
         def quant_y(h, lo, hi):
             quant(ycode[h][:, lo:hi], yscal[PACK * h :, lo:hi], ygrp[h][:, lo * PACK : hi * PACK])
+
+        def store_y(h, lo, hi):
             nc.sync.dma_start(
                 out=out_1[h].rearrange("p m t -> p (m t)").bitcast(I32)[:, lo:hi],
                 in_=ycode[h][:, lo:hi].bitcast(I32),
@@ -363,10 +394,11 @@ def tile_rwkv_channel_mix_gated_b14_kernel(
         load_rscale()
         load_x(1)
         load_k_group(0)
-        load_k_group(1)
+        load_k_part(1, 0, 0, 1)
         load_r(0, PRE, D)
-        load_k(2)
-        load_k(3)
+        load_k_part(1, 1, 0, 2)
+        for s in range(2, 6):
+            load_k(s)
         sigmoid(0, 0, PRE)
         nc.vector.tensor_copy(out=ident16[:], in_=ident[:])
         nc.vector.tensor_copy(out=bscale[:], in_=sbytes[:].bitcast(FP8))
@@ -383,186 +415,178 @@ def tile_rwkv_channel_mix_gated_b14_kernel(
         group_k_half(0, 0)
         scale_x(3)
         turn_x(3)
+        weave_k(banks[0], 1, 0, 0)
         unload_x(1)
         unload_x(0)
         unload_x(2)
         unload_x(3)
         sigmoid(0, PRE, D)
+        unload_k(banks[0], 1, 0, 0)
         group_k_half(0, 1)
-        weave_k(banks[0], 1, 0)
+        load_k(6)
         quant_x(0)
         quant_k(0)
-        unload_k(banks[0], 1, 0)
         keys(0, 0)
         keys(0, 1)
         quant_x(1)
-        group_k_half(1, 1)
-        group_k_half(1, 0, HALF)
-        load_k(4)
-        load_r(1)
-        load_k(5)
-        load_v(0)
         keys(0, 2)
         keys(0, 3)
-        group_k_half(2, 1)
-        quant_k(1)
-        weave_k(banks[1], 2, 0)
-        weave_k(banks[2], 2, 1)
+        group_k_half(1, 1)
+        group_k_half(1, 0, HALF)
+        load_v(0)
+        weave_k(banks[1], 2, 1, 0)
+        weave_k(banks[2], 2, 1, 1)
+        quant_k_half(1, 1)
+        group_k_half(2, 0)
+        load_v(1)
+        quant_k_half(1, 0)
+        quant_k_half(2, 0)
         for i in range(RING):
             rectify(0, i)
-        square(0)
-        unload_k(banks[1], 2, 0)
-        unload_k(banks[2], 2, 1)
-        keys(1, 0)
-        keys(1, 1)
-        keys(1, 2)
-        keys(1, 3)
+        square(0, 0)
+        unload_k(banks[1], 2, 1, 0)
+        square(0, 1)
+        unload_k(banks[2], 2, 1, 1)
+        keys_all(1)
+        weave_k(banks[3], 4, 1, 0)
+        weave_k(banks[0], 4, 1, 1)
         group_k_slab(3)
-        quant_k(2)
+        group_k_half(4, 0)
+        load_k_group(7)
+        load_v(2)
+        quant_k_half(2, 1)
         quant_k(3)
-        load_k(6)
-        load_k(7)
-        load_v(1)
+        quant_h(0)
+        quant_k_half(4, 0)
+        group_k_slab(5)
+        load_v(3)
+        group_k_half(6, 0)
         for i in range(RING):
             rectify(1, i)
-        sigmoid(1)
-        weave_k(ring_bank(1, 0), 4, 0)
-        weave_k(ring_bank(1, 1), 4, 1)
-        keys(2, 0)
-        keys(2, 1)
-        group_k_half(4, 1)
-        quant_h(0)
-        group_k_slab(5)
-        unload_k(ring_bank(1, 0), 4, 0)
-        unload_k(ring_bank(1, 1), 4, 1)
-        keys(2, 2)
-        keys(2, 3)
-        quant_k(4)
+        square(1, 0)
+        unload_k(banks[3], 4, 1, 0)
+        square(1, 1)
+        unload_k(banks[0], 4, 1, 1)
+        keys_all(2)
+        weave_k(banks[1], 6, 1, 0)
+        weave_k(banks[2], 6, 1, 1)
+        quant_k_half(4, 1)
         quant_k(5)
-        load_v(2)
-        load_v(3)
+        quant_h(1)
+        quant_k_half(6, 0)
+        group_v_both(1, grp[0])
+        load_v(4)
         for i in range(RING):
             rectify(2, i)
-        square(1)
-        weave_v(ring_bank(2, 0), 0, 0, 0)
-        weave_v(ring_bank(2, 1), 0, 0, 1)
-        keys(3, 0)
-        keys(3, 1)
-        group_k_slab(6)
-        quant_h(1)
-        unload_v(ring_bank(2, 0), 0, 0)
-        unload_v(ring_bank(2, 1), 0, 1)
-        keys(3, 2)
-        keys(3, 3)
-        quant_k(6)
-        for i in range(RING):
-            rectify(3, i)
-        square(2)
-        weave_v(ring_bank(3, 0), 1, 0, 0)
-        weave_v(ring_bank(3, 1), 1, 0, 1)
-        keys(4, 0)
-        keys(4, 1)
-        group_k_slab(7)
-        load_v(4)
+        square(2, 0)
+        unload_k(banks[1], 6, 1, 0)
+        square(2, 1)
+        unload_k(banks[2], 6, 1, 1)
+        keys_all(3)
+        weave_v(banks[3], 0, 0, 0)
+        weave_v(banks[0], 0, 0, 1)
+        quant_k_half(6, 1)
+        group_k_half(7, 0)
+        group_k_half(7, 1)
         load_v(5)
         load_v(6)
+        load_r(1)
+        quant_v(1, grp[0])
         quant_h(2)
-        quant_k(7)
-        unload_v(ring_bank(3, 0), 1, 0)
-        unload_v(ring_bank(3, 1), 1, 1)
-        keys(4, 2)
-        keys(4, 3)
-        quant_v(0, sgrp)
+        group_v(0, 2, grp[0])
         for i in range(RING):
-            rectify(4, i)
-        square(3)
-        weave_v(ring_bank(4, 0), 0, 1, 0)
-        weave_v(ring_bank(4, 1), 0, 1, 1)
-        keys(5, 0)
-        keys(5, 1)
-        group_v_one(1, 1)
+            rectify(3, i)
+        square(3, 0)
+        unload_v(banks[3], 0, 0)
+        square(3, 1)
+        unload_v(banks[0], 0, 1)
+        keys_all(4)
+        weave_v(banks[1], 1, 0, 0)
+        weave_v(banks[2], 1, 0, 1)
         load_v(7)
         load_r(2)
         load_r(3)
-        group_v(0, 2, grp[0])
-        quant_h(3)
-        unload_v(ring_bank(4, 0), 0, 0)
-        unload_v(ring_bank(4, 1), 0, 1)
-        values(0, 0)
-        keys(5, 2)
-        keys(5, 3)
-        quant_v(1, sgrp)
+        quant_k(7)
+        quant_v(0, sgrp, 0, KP)
         quant_v(2, grp[0])
-        for i in range(RING):
-            rectify(5, i)
-        square(4)
-        keys(6, 2)
-        keys(6, 3)
-        keys(6, 0)
-        keys(6, 1)
-        values(0, 1)
-        values(0, 2)
+        quant_h(3)
         group_v(0, 4, grp[1])
+        for i in range(RING):
+            rectify(4, i)
+        unload_v(banks[1], 1, 0)
+        square(4, 0)
+        unload_v(banks[2], 1, 1)
+        square(4, 1)
+        keys_all(5)
         quant_h(4)
         quant_v(3, grp[1])
-        for i in range(RING):
-            rectify(6, i)
-        square(5)
-        keys(7, 2)
-        keys(7, 3)
-        keys(7, 0)
-        keys(7, 1)
-        values(0, 3)
-        values(0, 4)
+        quant_v(0, sgrp, KP, SLAB)
+        values(0, 1)
+        values(0, 0)
         group_v(1, 2, grp[0])
+        for i in range(RING):
+            rectify(5, i)
+        keys_all(6)
+        square(5, 0)
+        rectify(6, 0)
+        square(5, 1)
+        values(0, 2)
+        values(0, 3)
         quant_h(5)
         quant_v(5, grp[0])
-        for i in range(RING):
-            rectify(7, i)
-        square(6)
-        square(7)
-        values(0, 5)
-        values(1, 0)
-        values(1, 1)
         group_v(0, 6, grp[1])
+        for i in range(1, RING):
+            rectify(6, i)
+        keys_all(7)
+        square(6, 0)
+        rectify(7, 0)
+        square(6, 1)
+        values(0, 4)
+        values(0, 5)
         quant_h(6)
         quant_v(4, grp[1])
+        for i in range(1, RING):
+            rectify(7, i)
+        square(7, 0)
+        sigmoid(1, 0, KP)
+        square(7, 1)
+        values(1, 0)
+        values(1, 1)
         values(1, 2)
-        values(0, 6)
         values(1, 3)
+        values(0, 6)
         group_v(1, 4, grp[0])
         quant_h(7)
         values(0, 7)
-        quant_v(6, grp[0])
-        values(1, 4)
-        values(1, 5)
-        sigmoid(2, 0, KP)
         group_v_scalar(6)
         group_v_scalar(7)
-        sigmoid(3, 0, KP)
-        gate_y(0)
         quant_v(7, sgrp, 0, KP)
-        gate_y(1)
+        quant_v(6, grp[0])
         quant_v(7, sgrp, KP, SLAB)
-        for tt in range(2):
-            values(1, 6, [tt])
-            values(1, 7, [tt])
+        values(1, 6)
+        sigmoid(2, 0, KP)
+        sigmoid(3, 0, KP)
+        sigmoid(1, KP, D)
+        sigmoid(2, KP, D)
+        gate_y(0)
+        gate_y(1)
         round_y(nc.scalar.copy, 0)
         round_y(nc.scalar.copy, 1)
+        for tt in range(3):
+            for g in (4, 5, 7):
+                values(1, g, [tt])
         gate_y(2)
         gate_y(3)
-        sigmoid(2, KP, D)
         round_y(nc.scalar.copy, 2)
         sigmoid(3, KP, D)
         turn_y(0)
-        for tt in range(2, TT):
-            values(1, 6, [tt])
-            values(1, 7, [tt])
+        for g in (4, 5, 7):
+            values(1, g, [3])
         gate_y(TT)
         round_y(nc.vector.tensor_copy, TT - 1)
         turn_y(1)
-        unload_y(0)
         round_y(nc.scalar.copy, TT)
+        unload_y(0)
         gate_y(TT + 1)
         gate_y(TT + 2)
         round_y(nc.vector.tensor_copy, TT + 1)
@@ -572,9 +596,13 @@ def tile_rwkv_channel_mix_gated_b14_kernel(
         round_y(nc.vector.tensor_copy, TT + 2)
         turn_y(3)
         unload_y(2)
+        quant_y(0, 0, T // 2)
         gate_y(TT + 3)
-        quant_y(0, 0, T)
         unload_y(3)
+        quant_y(0, T // 2, T)
+        store_y(0, 0, T)
         quant_y(1, 0, T // 2)
+        store_y(1, 0, T // 2)
         quant_y(1, T // 2, T)
+        store_y(1, T // 2, T)
         store_scales()

@@ -107,8 +107,8 @@ def tile_rwkv_channel_mix_gated_b14_kernel(
                 out=xbytes[q][:], in_=X_bytes.rearrange("(p q a) d -> q p a d", q=2, a=2)[q]
             )
 
-        def load_r(tt, lo=0, hi=D):
-            nc.sync.dma_start(out=rraw[tt][:, lo:hi], in_=R[cut(tt, P), lo:hi])
+        def load_r(tt, lo=0, hi=D, queue=nc.sync):
+            queue.dma_start(out=rraw[tt][:, lo:hi], in_=R[cut(tt, P), lo:hi])
 
         def slot(i):
             return raw[i // 2][:, cut(i % 2, PACK * SLAB)]
@@ -181,6 +181,11 @@ def tile_rwkv_channel_mix_gated_b14_kernel(
             for i in range(2 * XP):
                 nc.tensor.transpose(banks[TT + a][:, cut(i, P)], words[:, cut(i, P)], ident[:])
 
+        def warm_up(width):
+            nc.tensor.matmul(
+                out=banks[3][:, :width], lhsT=ident[:], rhs=ident[:, :1].to_broadcast([P, width]), start=True, stop=True
+            )
+
         def unload_x(a):
             words = xgrp[a // 2][:].bitcast(F32).rearrange("p (c a n u) -> p a c n u", c=XP, a=2, u=2)
             nc.scalar.copy(
@@ -238,6 +243,12 @@ def tile_rwkv_channel_mix_gated_b14_kernel(
             nc.vector.tensor_copy(
                 out=staged[:].rearrange("p (x c i j) -> p x c j i", x=2, i=LINE, j=PACK),
                 in_=vraw_pair(g)[:, :, :, h].rearrange("p x j (c i) -> p x c j i", i=LINE),
+            )
+
+        def group_v_one(h, g, staged):
+            nc.vector.tensor_copy(
+                out=staged[:, cut(g % 2, KP * PACK)].rearrange("p (c i j) -> p c j i", i=LINE, j=PACK),
+                in_=vraw(g)[:, :, h].rearrange("p j (c i) -> p c j i", i=LINE),
             )
 
         def group_v_both(g, staged):
@@ -350,6 +361,13 @@ def tile_rwkv_channel_mix_gated_b14_kernel(
         def round_y(copy, n):
             copy(out=as_sorted(ybf[n]), in_=as_stored(yout[n]))
 
+        def round_y_gpsimd(n):
+            nc.gpsimd.tensor_scalar(
+                out=ybf[n].rearrange("p (u w e) -> p u w e", u=2, e=2),
+                in0=yout[n].rearrange("p (w u e) -> p u w e", u=2, e=2),
+                scalar1=1.0, scalar2=0.0, op0=ALU.mult, op1=ALU.add,
+            )
+
         def gate_y_rounded(n):
             nc.vector.tensor_tensor(
                 out=as_sorted(ybf[n]), in0=as_stored(acc[n][:]), in1=as_stored(gate_of(n)), op=ALU.mult
@@ -389,8 +407,8 @@ def tile_rwkv_channel_mix_gated_b14_kernel(
 
         make_identity(nc, ident[:])
         load_scales()
-        load_r(0, 0, PRE)
         load_x(0)
+        load_r(0, 0, PRE, nc.scalar)
         load_rscale()
         load_x(1)
         load_k_group(0)
@@ -409,12 +427,16 @@ def tile_rwkv_channel_mix_gated_b14_kernel(
         scale_x(1)
         scale_x(0)
         scale_x(2)
+        warm_up(KP)
+        warm_up(KP)
         turn_x(1)
         turn_x(0)
+        warm_up(HALF)
         turn_x(2)
         group_k_half(0, 0)
         scale_x(3)
         turn_x(3)
+        warm_up(HALF)
         weave_k(banks[0], 1, 0, 0)
         unload_x(1)
         unload_x(0)
@@ -460,7 +482,6 @@ def tile_rwkv_channel_mix_gated_b14_kernel(
         quant_k_half(4, 0)
         group_k_slab(5)
         load_v(3)
-        group_k_half(6, 0)
         for i in range(RING):
             rectify(1, i)
         square(1, 0)
@@ -471,6 +492,7 @@ def tile_rwkv_channel_mix_gated_b14_kernel(
         weave_k(banks[1], 6, 1, 0)
         weave_k(banks[2], 6, 1, 1)
         quant_k_half(4, 1)
+        group_k_half(6, 0)
         quant_k(5)
         quant_h(1)
         quant_k_half(6, 0)
@@ -555,8 +577,9 @@ def tile_rwkv_channel_mix_gated_b14_kernel(
         values(1, 2)
         values(1, 3)
         values(0, 6)
-        group_v(1, 4, grp[0])
+        group_v_one(1, 4, grp[0])
         quant_h(7)
+        group_v_one(1, 5, grp[0])
         values(0, 7)
         group_v_scalar(6)
         group_v_scalar(7)
@@ -568,36 +591,36 @@ def tile_rwkv_channel_mix_gated_b14_kernel(
         sigmoid(3, 0, KP)
         sigmoid(1, KP, D)
         sigmoid(2, KP, D)
+        sigmoid(3, KP, D)
         gate_y(0)
+        round_y_gpsimd(0)
         gate_y(1)
-        round_y(nc.scalar.copy, 0)
         round_y(nc.scalar.copy, 1)
         for tt in range(3):
             for g in (4, 5, 7):
                 values(1, g, [tt])
         gate_y(2)
+        round_y_gpsimd(2)
         gate_y(3)
-        round_y(nc.scalar.copy, 2)
-        sigmoid(3, KP, D)
+        round_y(nc.scalar.copy, 3)
         turn_y(0)
         for g in (4, 5, 7):
             values(1, g, [3])
-        gate_y(TT)
-        round_y(nc.vector.tensor_copy, TT - 1)
         turn_y(1)
-        round_y(nc.scalar.copy, TT)
+        gate_y(TT)
+        round_y_gpsimd(TT)
         unload_y(0)
         gate_y(TT + 1)
+        round_y(nc.scalar.copy, TT + 1)
         gate_y(TT + 2)
-        round_y(nc.vector.tensor_copy, TT + 1)
         turn_y(2)
         unload_y(1)
         gate_y_rounded(TT + 3)
         round_y(nc.vector.tensor_copy, TT + 2)
         turn_y(3)
         unload_y(2)
-        quant_y(0, 0, T // 2)
         gate_y(TT + 3)
+        quant_y(0, 0, T // 2)
         unload_y(3)
         quant_y(0, T // 2, T)
         store_y(0, 0, T)

@@ -181,11 +181,6 @@ def tile_rwkv_channel_mix_gated_b14_kernel(
             for i in range(2 * XP):
                 nc.tensor.transpose(banks[TT + a][:, cut(i, P)], words[:, cut(i, P)], ident[:])
 
-        def warm_up(width):
-            nc.tensor.matmul(
-                out=banks[3][:, :width], lhsT=ident[:], rhs=ident[:, :1].to_broadcast([P, width]), start=True, stop=True
-            )
-
         def unload_x(a):
             words = xgrp[a // 2][:].bitcast(F32).rearrange("p (c a n u) -> p a c n u", c=XP, a=2, u=2)
             nc.scalar.copy(
@@ -427,16 +422,12 @@ def tile_rwkv_channel_mix_gated_b14_kernel(
         scale_x(1)
         scale_x(0)
         scale_x(2)
-        warm_up(KP)
-        warm_up(KP)
         turn_x(1)
         turn_x(0)
-        warm_up(HALF)
         turn_x(2)
         group_k_half(0, 0)
         scale_x(3)
         turn_x(3)
-        warm_up(HALF)
         weave_k(banks[0], 1, 0, 0)
         unload_x(1)
         unload_x(0)

@@ -192,11 +192,12 @@ def tile_rwkv_channel_mix_gated_b14_kernel(
             quant(xcode[q][:], xscal[q][:], xgrp[q][:])
 
         def group_k(copy, staged, rows, lo=0):
-            grouped = staged.rearrange("p (t w e j) -> p w j t e", t=PACK, e=2, j=PACK)
-            copy(
-                out=grouped[:, lo // LINE :],
-                in_=rows.rearrange("p j (w e t) -> p w j t e", e=2, t=PACK),
-            )
+            grouped = staged.rearrange("p (s t w e j) -> p s w j t e", s=2, t=2, e=2, j=PACK)
+            for s in range(2):
+                copy(
+                    out=grouped[:, s, lo // LINE :],
+                    in_=rows.rearrange("p j (w e s t) -> p s w j t e", e=2, s=2, t=2)[:, s],
+                )
 
         def kstage(s):
             return sgrp if s in (2, 4, 6) else grp[KEY_STAGE[s]]
@@ -236,26 +237,26 @@ def tile_rwkv_channel_mix_gated_b14_kernel(
 
         def group_v(h, g, staged):
             nc.vector.tensor_copy(
-                out=staged[:].rearrange("p (x c i j) -> p x c j i", x=2, i=LINE, j=PACK),
-                in_=vraw_pair(g)[:, :, :, h].rearrange("p x j (c i) -> p x c j i", i=LINE),
+                out=staged[:].rearrange("p (x c i j) -> p x c j i", x=2, i=RUN, j=PACK),
+                in_=vraw_pair(g)[:, :, :, h].rearrange("p x j (c i) -> p x c j i", i=RUN),
             )
 
         def group_v_one(h, g, staged):
             nc.vector.tensor_copy(
-                out=staged[:, cut(g % 2, KP * PACK)].rearrange("p (c i j) -> p c j i", i=LINE, j=PACK),
-                in_=vraw(g)[:, :, h].rearrange("p j (c i) -> p c j i", i=LINE),
+                out=staged[:, cut(g % 2, KP * PACK)].rearrange("p (c i j) -> p c j i", i=RUN, j=PACK),
+                in_=vraw(g)[:, :, h].rearrange("p j (c i) -> p c j i", i=RUN),
             )
 
         def group_v_both(g, staged):
             nc.vector.tensor_copy(
-                out=staged[:].rearrange("p (c i j) -> p c j i", i=LINE, j=PACK),
-                in_=vraw(g).rearrange("p j h (c i) -> p (h c) j i", i=LINE),
+                out=staged[:].rearrange("p (c i j) -> p c j i", i=RUN, j=PACK),
+                in_=vraw(g).rearrange("p j h (c i) -> p (h c) j i", i=RUN),
             )
 
-        def group_v_scalar(g):
+        def group_v_scalar(g, staged, lo=0, hi=KP):
             nc.scalar.copy(
-                out=sgrp[:, cut(g % 2, KP * PACK)].rearrange("p (c i j) -> p c j i", i=RUN, j=PACK),
-                in_=vraw(g)[:, :, 1].rearrange("p j (c i) -> p c j i", i=RUN),
+                out=staged[:, cut(g % 2, KP * PACK)][:, lo * PACK : hi * PACK].rearrange("p (c i j) -> p c j i", i=RUN, j=PACK),
+                in_=vraw(g)[:, :, 1, lo:hi].rearrange("p j (c i) -> p c j i", i=RUN),
             )
 
         def weave_v(bank, h, g, part):
@@ -343,9 +344,14 @@ def tile_rwkv_channel_mix_gated_b14_kernel(
             return gate[tt][:, cut(h, KP)]
 
         def gate_y(n):
-            h, tt = divmod(n, TT)
             nc.vector.tensor_tensor(out=yout[n], in0=acc[n][:], in1=gate_of(n), op=ALU.mult)
-            nc.sync.dma_start(out=out_0[cut(tt, P), cut(h, KP)], in_=yout[n])
+
+        def store_out(n, count=1):
+            h, tt = divmod(n, TT)
+            nc.sync.dma_start(
+                out=out_0[tt * P : (tt + count) * P, cut(h, KP)].rearrange("(i p) d -> p i d", p=P),
+                in_=relu[h][:, tt * KP : (tt + count) * KP].rearrange("p (i d) -> p i d", d=KP),
+            )
 
         def as_stored(ap):
             return ap.rearrange("p (w u e) -> p w u e", u=2, e=2)
@@ -373,6 +379,18 @@ def tile_rwkv_channel_mix_gated_b14_kernel(
                 words = ybf[2 * pair + i].bitcast(F32)
                 for u in range(2):
                     nc.tensor.transpose(banks[pair][:, cut(2 * i + u, P)], words[:, cut(u, P)], ident[:])
+
+        def turn_y_tile(bank, n):
+            words = ybf[n].bitcast(F32)
+            for u in range(2):
+                nc.tensor.transpose(bank[:, cut(u, P)], words[:, cut(u, P)], ident[:])
+
+        def unload_y_tile(bank, n):
+            h, tt = divmod(n, TT)
+            nc.scalar.copy(
+                out=ygrp[h][:, cut(tt, KP)].bitcast(F32).rearrange("p (n u) -> p n u", u=2),
+                in_=bank[:, :HALF].rearrange("p (u n) -> p n u", u=2),
+            )
 
         def unload_y(pair):
             h, r = divmod(pair, 2)
@@ -572,10 +590,12 @@ def tile_rwkv_channel_mix_gated_b14_kernel(
         quant_h(7)
         group_v_one(1, 5, grp[0])
         values(0, 7)
-        group_v_scalar(6)
-        group_v_scalar(7)
+        group_v_scalar(6, sgrp)
+        group_v_scalar(7, sgrp)
         quant_v(7, sgrp, 0, KP)
         quant_v(6, grp[0])
+        gate_y(0)
+        store_out(0)
         quant_v(7, sgrp, KP, SLAB)
         values(1, 6)
         sigmoid(2, 0, KP)
@@ -583,40 +603,52 @@ def tile_rwkv_channel_mix_gated_b14_kernel(
         sigmoid(1, KP, D)
         sigmoid(2, KP, D)
         sigmoid(3, KP, D)
-        gate_y(0)
         round_y_gpsimd(0)
         gate_y(1)
+        store_out(1)
         round_y(nc.scalar.copy, 1)
-        for tt in range(3):
-            for g in (4, 5, 7):
+        for tt in range(2):
+            for g in (4, 5):
                 values(1, g, [tt])
+        values(1, 7, range(2))
+        for g in (4, 5, 7):
+            values(1, g, [2])
         gate_y(2)
+        store_out(2)
         round_y_gpsimd(2)
         gate_y(3)
+        store_out(3)
         round_y(nc.scalar.copy, 3)
         turn_y(0)
         for g in (4, 5, 7):
             values(1, g, [3])
         turn_y(1)
         gate_y(TT)
+        store_out(TT)
         round_y_gpsimd(TT)
         unload_y(0)
         gate_y(TT + 1)
+        store_out(TT + 1)
         round_y(nc.scalar.copy, TT + 1)
         gate_y(TT + 2)
+        store_out(TT + 2)
         turn_y(2)
         unload_y(1)
-        gate_y_rounded(TT + 3)
-        round_y(nc.vector.tensor_copy, TT + 2)
-        turn_y(3)
-        unload_y(2)
         gate_y(TT + 3)
+        store_out(TT + 3)
+        round_y(nc.vector.tensor_copy, TT + 2)
+        turn_y_tile(banks[3], TT + 2)
+        round_y(nc.vector.tensor_copy, TT + 3)
+        turn_y_tile(banks[0], TT + 3)
+        unload_y(2)
         quant_y(0, 0, T // 2)
-        unload_y(3)
+        unload_y_tile(banks[3], TT + 2)
+        unload_y_tile(banks[0], TT + 3)
         quant_y(0, T // 2, T)
         store_y(0, 0, T)
         quant_y(1, 0, T // 2)
         store_y(1, 0, T // 2)
-        quant_y(1, T // 2, T)
+        quant_y(1, T // 2, T - P)
+        quant_y(1, T - P, T)
         store_y(1, T // 2, T)
         store_scales()

@@ -34,10 +34,10 @@ WOVEN = 2
 N_GRP = 2
 N_KCODE = 4
 N_HGRP = 3
-KEY_SLOT = (0, 1, 2, 3, 4, 5, 0, 3)
-VALUE_SLOT = (1, 2, 4, 5, 2, 3, 0, 1)
-KEY_STAGE = (0, 1, 0, 0, 0, 1, 0, 1)
-HALVED = (0, 1, 2, 4, 6, 7)
+KEY_SLOT = (0, 1, 2, 3, 4, 5, 0, 1)
+VALUE_SLOT = (2, 3, 4, 5, 0, 1, 2, 3)
+KEY_STAGE = (0, 1, 0, 0, 0, 1, 0, 0)
+HALVED = (0, 1, 2, 4, 6)
 PRE = 16
 FIRST = (1, 0)
 SLAB = 2 * KP
@@ -114,8 +114,6 @@ def tile_rwkv_channel_mix_gated_b14_kernel(
             return raw[i // 2][:, cut(i % 2, PACK * SLAB)]
 
         def kraw(s):
-            if s in (0, 1, FG - 1):
-                return slot(KEY_SLOT[s]).rearrange("p (c j f) -> p j c f", c=XP, j=PACK)
             return slot(KEY_SLOT[s]).rearrange("p (j x f) -> p j x f", j=PACK, x=2)
 
         def vraw(g):
@@ -124,24 +122,10 @@ def tile_rwkv_channel_mix_gated_b14_kernel(
         def vraw_pair(g):
             return raw[VALUE_SLOT[g] // 2][:].rearrange("p (x j h d) -> p x j h d", x=2, j=PACK, h=HALVES)
 
-        def load_k_group(g):
-            for c in range(XP):
-                nc.sync.dma_start(
-                    out=kraw(g)[:, :, c],
-                    in_=Wk[cut(c, KP), cut(g, KP)].rearrange("(p j) f -> p j f", j=PACK),
-                )
-
-        def load_k_part(s, x, c, g):
-            nc.sync.dma_start(
-                out=kraw(s)[:, :, x],
-                in_=Wk[cut(c, KP), cut(g, KP)].rearrange("(p j) f -> p j f", j=PACK),
-            )
-
         def load_k(s):
-            first = KP + (s - 1) // 2 * SLAB
             nc.sync.dma_start(
                 out=kraw(s).rearrange("p j x f -> p j (x f)"),
-                in_=Wk[cut((s - 1) % 2, KP), first : first + SLAB].rearrange("(p j) f -> p j f", j=PACK),
+                in_=Wk[cut(s % 2, KP), cut(s // 2, SLAB)].rearrange("(p j) f -> p j f", j=PACK),
             )
 
         def load_v(g):
@@ -230,7 +214,7 @@ def tile_rwkv_channel_mix_gated_b14_kernel(
             quant_k(s, x * KP, (x + 1) * KP)
 
         def key_place(g, c):
-            return (g, c) if g in (0, FG - 1) else (1 + (g - 1) // 2 * 2 + c, (g - 1) % 2)
+            return g - g % 2 + c, g % 2
 
         def value_place(h, g):
             return (g, h) if g < WOVEN else (WOVEN + (FG - WOVEN) // 2 * h + (g - WOVEN) // 2, g % 2)
@@ -241,10 +225,10 @@ def tile_rwkv_channel_mix_gated_b14_kernel(
                 in_=vraw_pair(g)[:, :, :, h].rearrange("p x j (c i) -> p x c j i", i=RUN),
             )
 
-        def group_v_one(h, g, staged):
+        def group_v_one(h, g, staged, hi=KP):
             nc.vector.tensor_copy(
-                out=staged[:, cut(g % 2, KP * PACK)].rearrange("p (c i j) -> p c j i", i=RUN, j=PACK),
-                in_=vraw(g)[:, :, h].rearrange("p j (c i) -> p c j i", i=RUN),
+                out=staged[:, cut(g % 2, KP * PACK)][:, : hi * PACK].rearrange("p (c i j) -> p c j i", i=RUN, j=PACK),
+                in_=vraw(g)[:, :, h, :hi].rearrange("p j (c i) -> p c j i", i=RUN),
             )
 
         def group_v_both(g, staged):
@@ -424,10 +408,10 @@ def tile_rwkv_channel_mix_gated_b14_kernel(
         load_r(0, 0, PRE, nc.scalar)
         load_rscale()
         load_x(1)
-        load_k_group(0)
-        load_k_part(1, 0, 0, 1)
+        load_k(0)
+        load_k(1)
         load_r(0, PRE, D)
-        load_k_part(1, 1, 0, 2)
+        load_r(1)
         for s in range(2, 6):
             load_k(s)
         sigmoid(0, 0, PRE)
@@ -440,38 +424,40 @@ def tile_rwkv_channel_mix_gated_b14_kernel(
         scale_x(1)
         scale_x(0)
         scale_x(2)
+        scale_x(3)
         turn_x(1)
         turn_x(0)
         turn_x(2)
         group_k_half(0, 0)
-        scale_x(3)
         turn_x(3)
-        weave_k(banks[0], 1, 0, 0)
+        weave_k(banks[0], 0, 1, 0)
+        weave_k(banks[3], 0, 1, 1)
+        load_k(6)
         unload_x(1)
         unload_x(0)
         unload_x(2)
         unload_x(3)
+        unload_k(banks[0], 0, 1, 0)
         sigmoid(0, PRE, D)
-        unload_k(banks[0], 1, 0, 0)
-        group_k_half(0, 1)
-        load_k(6)
+        unload_k(banks[3], 0, 1, 1)
+        sigmoid(1)
         quant_x(0)
-        quant_k(0)
-        keys(0, 0)
-        keys(0, 1)
+        quant_k_half(0, 0)
+        group_k_half(1, 0)
         quant_x(1)
-        keys(0, 2)
-        keys(0, 3)
+        quant_k_half(1, 0)
+        keys_all(0)
         group_k_half(1, 1)
-        group_k_half(1, 0, HALF)
-        load_v(0)
+        load_k(7)
         weave_k(banks[1], 2, 1, 0)
         weave_k(banks[2], 2, 1, 1)
-        quant_k_half(1, 1)
         group_k_half(2, 0)
-        load_v(1)
-        quant_k_half(1, 0)
+        load_v(0)
+        quant_k_half(1, 1)
+        quant_k_half(0, 1)
         quant_k_half(2, 0)
+        group_k_slab(3)
+        load_v(1)
         for i in range(RING):
             rectify(0, i)
         square(0, 0)
@@ -481,16 +467,14 @@ def tile_rwkv_channel_mix_gated_b14_kernel(
         keys_all(1)
         weave_k(banks[3], 4, 1, 0)
         weave_k(banks[0], 4, 1, 1)
-        group_k_slab(3)
         group_k_half(4, 0)
-        load_k_group(7)
         load_v(2)
-        quant_k_half(2, 1)
         quant_k(3)
-        quant_h(0)
-        quant_k_half(4, 0)
+        quant_k_half(2, 1)
         group_k_slab(5)
         load_v(3)
+        quant_h(0)
+        quant_k_half(4, 0)
         for i in range(RING):
             rectify(1, i)
         square(1, 0)
@@ -501,12 +485,11 @@ def tile_rwkv_channel_mix_gated_b14_kernel(
         weave_k(banks[1], 6, 1, 0)
         weave_k(banks[2], 6, 1, 1)
         quant_k_half(4, 1)
-        group_k_half(6, 0)
         quant_k(5)
-        quant_h(1)
-        quant_k_half(6, 0)
-        group_v_both(1, grp[0])
+        group_k_half(6, 0)
         load_v(4)
+        group_k_slab(7)
+        load_v(5)
         for i in range(RING):
             rectify(2, i)
         square(2, 0)
@@ -516,13 +499,12 @@ def tile_rwkv_channel_mix_gated_b14_kernel(
         keys_all(3)
         weave_v(banks[3], 0, 0, 0)
         weave_v(banks[0], 0, 0, 1)
+        quant_h(1)
+        quant_k_half(6, 0)
+        quant_k(7)
+        group_v_both(1, grp[1])
         quant_k_half(6, 1)
-        group_k_half(7, 0)
-        group_k_half(7, 1)
-        load_v(5)
-        load_v(6)
-        load_r(1)
-        quant_v(1, grp[0])
+        quant_v(1, grp[1])
         quant_h(2)
         group_v(0, 2, grp[0])
         for i in range(RING):
@@ -534,10 +516,10 @@ def tile_rwkv_channel_mix_gated_b14_kernel(
         keys_all(4)
         weave_v(banks[1], 1, 0, 0)
         weave_v(banks[2], 1, 0, 1)
+        load_v(6)
         load_v(7)
         load_r(2)
         load_r(3)
-        quant_k(7)
         quant_v(0, sgrp, 0, KP)
         quant_v(2, grp[0])
         quant_h(3)
@@ -579,7 +561,7 @@ def tile_rwkv_channel_mix_gated_b14_kernel(
         for i in range(1, RING):
             rectify(7, i)
         square(7, 0)
-        sigmoid(1, 0, KP)
+        group_v_scalar(5, grp[0], KP - P, KP)
         square(7, 1)
         values(1, 0)
         values(1, 1)
@@ -588,7 +570,7 @@ def tile_rwkv_channel_mix_gated_b14_kernel(
         values(0, 6)
         group_v_one(1, 4, grp[0])
         quant_h(7)
-        group_v_one(1, 5, grp[0])
+        group_v_one(1, 5, grp[0], KP - P)
         values(0, 7)
         group_v_scalar(6, sgrp)
         group_v_scalar(7, sgrp)
@@ -600,13 +582,12 @@ def tile_rwkv_channel_mix_gated_b14_kernel(
         values(1, 6)
         sigmoid(2, 0, KP)
         sigmoid(3, 0, KP)
-        sigmoid(1, KP, D)
-        sigmoid(2, KP, D)
-        sigmoid(3, KP, D)
         round_y_gpsimd(0)
         gate_y(1)
         store_out(1)
+        sigmoid(2, KP, D)
         round_y(nc.scalar.copy, 1)
+        sigmoid(3, KP, D)
         for tt in range(2):
             for g in (4, 5):
                 values(1, g, [tt])

@@ -149,8 +149,8 @@ def tile_rwkv_channel_mix_gated_b14_kernel(
             for wide, codes, scale in x_blocks(a):
                 nc.scalar.activation(out=wide, in_=codes, func=ACT.Copy, scale=scale)
 
-        def widen_x_vector(a):
-            for wide, codes, scale in x_blocks(a):
+        def widen_x_vector(a, lo=0, hi=D // BLOCK):
+            for wide, codes, scale in x_blocks(a)[lo:hi]:
                 nc.vector.tensor_scalar(out=wide, in0=codes, scalar1=scale, scalar2=None, op0=ALU.mult)
 
         def scale_x(a):
@@ -162,14 +162,16 @@ def tile_rwkv_channel_mix_gated_b14_kernel(
 
         def turn_x(a):
             words = xfull[a].bitcast(F32)
-            for i in range(2 * XP):
-                nc.tensor.transpose(banks[TT + a][:, cut(i, P)], words[:, cut(i, P)], ident[:])
+            for c in range(XP):
+                for u in range(2):
+                    nc.tensor.transpose(
+                        banks[TT + a // 2 * XP + c][:, cut(a % 2 * 2 + u, P)], words[:, cut(u * XP + c, P)], ident[:]
+                    )
 
-        def unload_x(a):
-            words = xgrp[a // 2][:].bitcast(F32).rearrange("p (c a n u) -> p a c n u", c=XP, a=2, u=2)
+        def unload_x(q, c):
             nc.scalar.copy(
-                out=words[:, a % 2],
-                in_=banks[TT + a][:].rearrange("p (u c n) -> p c n u", c=XP, u=2),
+                out=xgrp[q][:].bitcast(F32)[:, cut(c, KP)].rearrange("p (a n u) -> p a n u", a=2, u=2),
+                in_=banks[TT + q * XP + c][:].rearrange("p (a u n) -> p a n u", a=2, u=2),
             )
 
         def quant_x(q):
@@ -419,9 +421,10 @@ def tile_rwkv_channel_mix_gated_b14_kernel(
         nc.vector.tensor_copy(out=bscale[:], in_=sbytes[:].bitcast(FP8))
         widen_x_vector(1)
         widen_x_scalar(0)
-        widen_x_vector(2)
-        widen_x_scalar(3)
+        widen_x_vector(2, 0, 4)
         scale_x(1)
+        widen_x_vector(2, 4)
+        widen_x_scalar(3)
         scale_x(0)
         scale_x(2)
         scale_x(3)
@@ -433,14 +436,14 @@ def tile_rwkv_channel_mix_gated_b14_kernel(
         weave_k(banks[0], 0, 1, 0)
         weave_k(banks[3], 0, 1, 1)
         load_k(6)
-        unload_x(1)
-        unload_x(0)
-        unload_x(2)
-        unload_x(3)
-        unload_k(banks[0], 0, 1, 0)
+        unload_x(0, 0)
+        unload_x(0, 1)
+        unload_x(1, 0)
+        unload_x(1, 1)
         sigmoid(0, PRE, D)
-        unload_k(banks[3], 0, 1, 1)
+        unload_k(banks[0], 0, 1, 0)
         sigmoid(1)
+        unload_k(banks[3], 0, 1, 1)
         quant_x(0)
         quant_k_half(0, 0)
         group_k_half(1, 0)

@@ -233,6 +233,12 @@ def tile_rwkv_channel_mix_gated_b14_kernel(
                 in_=vraw(g)[:, :, h, :hi].rearrange("p j (c i) -> p c j i", i=RUN),
             )
 
+        def group_v_half(h, g, staged):
+            nc.vector.tensor_copy(
+                out=staged[:, cut(h, KP * PACK)].rearrange("p (c i j) -> p c j i", i=RUN, j=PACK),
+                in_=vraw(g)[:, :, h].rearrange("p j (c i) -> p c j i", i=RUN),
+            )
+
         def group_v_both(g, staged):
             nc.vector.tensor_copy(
                 out=staged[:].rearrange("p (c i j) -> p c j i", i=RUN, j=PACK),
@@ -262,7 +268,7 @@ def tile_rwkv_channel_mix_gated_b14_kernel(
             quant(vcode[s][:, lo:hi], vscal[s][:, lo:hi], staged[:, lo * PACK : hi * PACK])
 
         def ring_bank(g, i):
-            return banks[TT + i]
+            return banks[TT + (2 + i % 2 if g == FG - 1 else i)]
 
         def keys(g, i):
             q, u = divmod(i, 2)
@@ -307,7 +313,7 @@ def tile_rwkv_channel_mix_gated_b14_kernel(
         def quant_h(g):
             quant(hcode[g][:], hscal[g][:], hgrp[g % N_HGRP][:])
 
-        acc = banks[:TT] + [ring_bank(FG - 1, tt) for tt in range(TT)]
+        acc = banks
 
         def values(h, g, tts=range(TT)):
             s, x = value_place(h, g)
@@ -487,12 +493,10 @@ def tile_rwkv_channel_mix_gated_b14_kernel(
         keys_all(2)
         weave_k(banks[1], 6, 1, 0)
         weave_k(banks[2], 6, 1, 1)
-        quant_k_half(4, 1)
         quant_k(5)
+        quant_k_half(4, 1)
         group_k_half(6, 0)
         load_v(4)
-        group_k_slab(7)
-        load_v(5)
         for i in range(RING):
             rectify(2, i)
         square(2, 0)
@@ -502,101 +506,115 @@ def tile_rwkv_channel_mix_gated_b14_kernel(
         keys_all(3)
         weave_v(banks[3], 0, 0, 0)
         weave_v(banks[0], 0, 0, 1)
-        quant_h(1)
-        quant_k_half(6, 0)
-        quant_k(7)
-        group_v_both(1, grp[1])
-        quant_k_half(6, 1)
-        quant_v(1, grp[1])
-        quant_h(2)
-        group_v(0, 2, grp[0])
-        for i in range(RING):
-            rectify(3, i)
-        square(3, 0)
-        unload_v(banks[3], 0, 0)
-        square(3, 1)
-        unload_v(banks[0], 0, 1)
-        keys_all(4)
         weave_v(banks[1], 1, 0, 0)
         weave_v(banks[2], 1, 0, 1)
+        quant_h(1)
+        quant_k_half(6, 0)
+        group_k_slab(7)
+        load_v(5)
         load_v(6)
+        quant_k_half(6, 1)
+        group_v_half(0, 1, grp[1])
+        quant_k(7)
+        quant_v(1, grp[1], 0, KP)
+        for i in range(RING):
+            rectify(3, i)
+        unload_v(banks[3], 0, 0)
+        unload_v(banks[0], 0, 1)
+        unload_v(banks[1], 1, 0)
+        unload_v(banks[2], 1, 1)
+        keys_all(4)
+        square(3, 0)
+        rectify(4, 0)
+        square(3, 1)
+        quant_v(0, sgrp, 0, KP)
+        quant_h(2)
+        values(0, 1)
+        values(0, 0)
+        group_v(0, 2, grp[0])
+        quant_v(0, sgrp, KP, SLAB)
+        quant_v(2, grp[0])
+        quant_h(3)
+        for i in range(1, RING):
+            rectify(4, i)
+        keys_all(5)
+        square(4, 0)
+        rectify(5, 0)
+        square(4, 1)
+        values(0, 2)
+        group_v(0, 4, grp[0])
+        quant_h(4)
+        quant_v(3, grp[0])
+        group_v_half(1, 1, grp[1])
         load_v(7)
         load_r(2)
         load_r(3)
-        quant_v(0, sgrp, 0, KP)
-        quant_v(2, grp[0])
-        quant_h(3)
-        group_v(0, 4, grp[1])
-        for i in range(RING):
-            rectify(4, i)
-        unload_v(banks[1], 1, 0)
-        square(4, 0)
-        unload_v(banks[2], 1, 1)
-        square(4, 1)
-        keys_all(5)
-        quant_h(4)
-        quant_v(3, grp[1])
-        quant_v(0, sgrp, KP, SLAB)
-        values(0, 1)
-        values(0, 0)
-        group_v(1, 2, grp[0])
-        for i in range(RING):
+        for i in range(1, RING):
             rectify(5, i)
         keys_all(6)
         square(5, 0)
         rectify(6, 0)
         square(5, 1)
-        values(0, 2)
         values(0, 3)
         quant_h(5)
-        quant_v(5, grp[0])
-        group_v(0, 6, grp[1])
-        for i in range(1, RING):
-            rectify(6, i)
-        keys_all(7)
-        square(6, 0)
-        rectify(7, 0)
-        square(6, 1)
+        group_v(1, 2, grp[0])
+        quant_v(1, grp[1], KP, SLAB)
+        quant_v(5, grp[0], 0, KP)
         values(0, 4)
+        rectify(6, 1)
+        values(1, 0, range(2))
+        rectify(6, 2)
+        keys(7, 0)
+        rectify(6, 3)
+        keys(7, 1)
+        square(6, 0)
         values(0, 5)
+        rectify(7, 0)
+        keys(7, 2)
+        rectify(7, 1)
+        keys(7, 3)
+        square(6, 1)
+        for g in range(1, 3):
+            values(1, g, range(2))
+        group_v_one(1, 4, sgrp)
+        quant_v(5, grp[0], KP, SLAB)
+        quant_v(6, sgrp, 0, KP)
+        group_v(0, 6, grp[1])
         quant_h(6)
         quant_v(4, grp[1])
-        for i in range(1, RING):
-            rectify(7, i)
+        values(1, 3, range(2))
+        rectify(7, 2)
+        rectify(7, 3)
         square(7, 0)
         group_v_scalar(5, grp[0], KP - P, KP)
         square(7, 1)
-        values(1, 0)
-        values(1, 1)
-        values(1, 2)
-        values(1, 3)
+        for g in range(4):
+            values(1, g, range(2, TT))
+        values(1, 4)
         values(0, 6)
-        group_v_one(1, 4, grp[0])
         quant_h(7)
         group_v_one(1, 5, grp[0], KP - P)
         values(0, 7)
         group_v_scalar(6, sgrp)
         group_v_scalar(7, sgrp)
         quant_v(7, sgrp, 0, KP)
-        quant_v(6, grp[0])
+        quant_v(6, grp[0], KP, SLAB)
         gate_y(0)
         store_out(0)
         quant_v(7, sgrp, KP, SLAB)
         values(1, 6)
+        values(1, 5, range(2))
+        values(1, 7, range(2))
         sigmoid(2, 0, KP)
         sigmoid(3, 0, KP)
-        round_y_gpsimd(0)
+        round_y(nc.scalar.copy, 0)
         gate_y(1)
         store_out(1)
+        round_y_gpsimd(1)
         sigmoid(2, KP, D)
-        round_y(nc.scalar.copy, 1)
         sigmoid(3, KP, D)
-        for tt in range(2):
-            for g in (4, 5):
-                values(1, g, [tt])
-        values(1, 7, range(2))
-        for g in (4, 5, 7):
-            values(1, g, [2])
+        values(1, 5, [2])
+        values(1, 7, [2])
         gate_y(2)
         store_out(2)
         round_y_gpsimd(2)
@@ -604,8 +622,8 @@ def tile_rwkv_channel_mix_gated_b14_kernel(
         store_out(3)
         round_y(nc.scalar.copy, 3)
         turn_y(0)
-        for g in (4, 5, 7):
-            values(1, g, [3])
+        values(1, 5, [3])
+        values(1, 7, [3])
         turn_y(1)
         gate_y(TT)
         store_out(TT)

from contextlib import ExitStack

import concourse.mybir as mybir
from concourse.masks import make_identity

T, D, F = 512, 1024, 4096
FLOPS = 2 * 2 * T * D * F

F32 = mybir.dt.float32
BF16 = mybir.dt.bfloat16
U32 = mybir.dt.uint32
I32 = mybir.dt.int32
U8 = mybir.dt.uint8
FP8 = mybir.dt.float8_e4m3fn
FP8X4 = mybir.dt.float8_e4m3fn_x4
ACT = mybir.ActivationFunctionType
ALU = mybir.AluOpType

P = 128
PACK = 4
KP = P * PACK
HALF = KP // 2
TT = T // P
XP = D // KP
FG = F // KP
HALVES = D // KP
BLOCK = 128
LINE = 8
RUN = 4
RING = 4

WOVEN = 2

N_GRP = 2
N_KCODE = 4
N_HGRP = 3
KEY_SLOT = (0, 1, 2, 3, 4, 5, 0, 1)
VALUE_SLOT = (2, 3, 4, 5, 0, 1, 2, 3)
KEY_STAGE = (0, 1, 0, 0, 0, 1, 0, 0)
HALVED = (0, 1, 2, 4, 6)
PRE = 16
FIRST = (1, 0)
SLAB = 2 * KP


def tile_rwkv_channel_mix_gated_b14_kernel(
    tc, X_bytes, X_sbytes, X_rscale, Wk, Wv, R, out_0, out_1, out_2
):
    nc = tc.nc
    with ExitStack() as ctx:
        sbuf = ctx.enter_context(tc.tile_pool(name="sbuf", bufs=1))
        psum = ctx.enter_context(tc.psum_pool(name="psum", bufs=1))

        def tiles(name, count, shape, dtype):
            return [
                sbuf.tile(shape, dtype, name="%s%d" % (name, i), align_bytes=64)
                for i in range(count)
            ]

        def cut(i, width):
            return slice(i * width, (i + 1) * width)

        banks = [psum.tile([P, KP], F32, name="bank%d" % i) for i in range(TT + RING)]
        ident = sbuf.tile([P, P], F32, name="ident")
        ident16 = sbuf.tile([P, P], BF16, name="ident16")
        sbytes = sbuf.tile([P, TT * D // BLOCK], U8, name="sbytes")
        bscale = sbuf.tile([P, TT * D // BLOCK], F32, name="bscale")
        rscale = sbuf.tile([P, TT], F32, name="rscale")
        xbytes = tiles("xbytes", 2, [P, 2, D], U8)
        xwide = [t[:] for t in tiles("xwide", 2, [P, D], BF16)]
        xfull = [t[:] for t in tiles("xfull", 2, [P, D], BF16)]
        xgrp = tiles("xgrp", 2, [P, 2 * D], BF16)
        xcode = tiles("xcode", 2, [P, XP * HALF], U32)
        xscal = tiles("xscal", 2, [P, XP * HALF], U8)
        rraw = [t[:] for t in tiles("rraw", 2, [P, D], BF16)] + xfull
        raw = tiles("raw", 3, [P, 2 * PACK * SLAB], BF16)
        grp = tiles("grp", N_GRP, [P, SLAB * PACK], BF16)
        sgrp = sbuf.tile([P, SLAB * PACK], BF16, name="sgrp", align_bytes=64)
        kcode = tiles("kcode", N_KCODE, [P, SLAB], U32)
        kscal = tiles("kscal", N_KCODE, [P, SLAB], U8)
        vcode = tiles("vcode", FG, [P, SLAB], U32)
        vscal = tiles("vscal", FG, [P, SLAB], U8)
        hgrp = tiles("hgrp", N_HGRP, [P, T * PACK], BF16)
        xwide = xwide + [hgrp[1][:, cut(i, D)] for i in range(2)]
        xfull = xfull + [hgrp[2][:, cut(i, D)] for i in range(2)]
        hcode = tiles("hcode", FG, [P, T], U32)
        hscal = tiles("hscal", FG, [P, T], U8)
        relu = tiles("relu", 2, [P, T * PACK], F32)
        ycode = tiles("ycode", HALVES, [P, T], U32)
        yscal = sbuf.tile([P, T], U8, name="yscal", align_bytes=64)
        gate = [t[:] for t in tiles("gate", 2, [P, D], F32)] + [t[:].bitcast(F32) for t in xgrp]
        yout = [t[:, cut(i, KP)] for t in relu for i in range(TT)]
        ybf = [t[:, cut(i, KP)] for t in xwide for i in range(2)]
        ygrp = [grp[0][:, cut(h, T * PACK)] for h in range(HALVES)]

        def quant(code, scal, src):
            nc.vector.quantize_mx(out=code.bitcast(FP8X4), scales=scal, in_=src)

        def load_scales():
            nc.sync.dma_start(out=sbytes[:], in_=X_sbytes.rearrange("(p a) j -> p (a j)", a=TT))

        def load_rscale():
            nc.scalar.dma_start(out=rscale[:], in_=X_rscale.rearrange("(p a) o -> p (a o)", a=TT))

        def load_x(q):
            nc.sync.dma_start(
                out=xbytes[q][:], in_=X_bytes.rearrange("(p q a) d -> q p a d", q=2, a=2)[q]
            )

        def load_r(tt, lo=0, hi=D, queue=nc.sync):
            queue.dma_start(out=rraw[tt][:, lo:hi], in_=R[cut(tt, P), lo:hi])

        def slot(i):
            return raw[i // 2][:, cut(i % 2, PACK * SLAB)]

        def kraw(s):
            return slot(KEY_SLOT[s]).rearrange("p (j x f) -> p j x f", j=PACK, x=2)

        def vraw(g):
            return slot(VALUE_SLOT[g]).rearrange("p (j h d) -> p j h d", j=PACK, h=HALVES)

        def vraw_pair(g):
            return raw[VALUE_SLOT[g] // 2][:].rearrange("p (x j h d) -> p x j h d", x=2, j=PACK, h=HALVES)

        def load_k(s):
            nc.sync.dma_start(
                out=kraw(s).rearrange("p j x f -> p j (x f)"),
                in_=Wk[cut(s % 2, KP), cut(s // 2, SLAB)].rearrange("(p j) f -> p j f", j=PACK),
            )

        def load_v(g):
            nc.sync.dma_start(
                out=vraw(g).rearrange("p j h d -> p (j h d)"),
                in_=Wv[cut(g, KP), :].rearrange("(p j) d -> p (j d)", j=PACK),
            )

        def x_blocks(a):
            per_row = D // BLOCK
            return [
                (
                    xwide[a][:, cut(b, BLOCK)],
                    xbytes[a // 2][:, a % 2, cut(b, BLOCK)].bitcast(FP8),
                    bscale[:, a * per_row + b : a * per_row + b + 1],
                )
                for b in range(per_row)
            ]

        def widen_x_scalar(a):
            for wide, codes, scale in x_blocks(a):
                nc.scalar.activation(out=wide, in_=codes, func=ACT.Copy, scale=scale)

        def widen_x_vector(a, lo=0, hi=D // BLOCK):
            for wide, codes, scale in x_blocks(a)[lo:hi]:
                nc.vector.tensor_scalar(out=wide, in0=codes, scalar1=scale, scalar2=None, op0=ALU.mult)

        def scale_x(a):
            nc.vector.tensor_scalar(
                out=xfull[a].rearrange("p (u w e) -> p u w e", u=2, e=2),
                in0=xwide[a].rearrange("p (w u e) -> p u w e", u=2, e=2),
                scalar1=rscale[:, a : a + 1], scalar2=None, op0=ALU.mult,
            )

        def turn_x(a):
            words = xfull[a].bitcast(F32)
            for c in range(XP):
                for u in range(2):
                    nc.tensor.transpose(
                        banks[TT + a // 2 * XP + c][:, cut(a % 2 * 2 + u, P)], words[:, cut(u * XP + c, P)], ident[:]
                    )

        def unload_x(q, c):
            nc.scalar.copy(
                out=xgrp[q][:].bitcast(F32)[:, cut(c, KP)].rearrange("p (a n u) -> p a n u", a=2, u=2),
                in_=banks[TT + q * XP + c][:].rearrange("p (a u n) -> p a n u", a=2, u=2),
            )

        def quant_x(q):
            quant(xcode[q][:], xscal[q][:], xgrp[q][:])

        def group_k(copy, staged, rows, lo=0):
            grouped = staged.rearrange("p (s t w e j) -> p s w j t e", s=2, t=2, e=2, j=PACK)
            for s in range(2):
                copy(
                    out=grouped[:, s, lo // LINE :],
                    in_=rows.rearrange("p j (w e s t) -> p s w j t e", e=2, s=2, t=2)[:, s],
                )

        def kstage(s):
            return sgrp if s in (2, 4, 6) else grp[KEY_STAGE[s]]

        def group_k_slab(s):
            group_k(nc.vector.tensor_copy, kstage(s)[:], kraw(s).rearrange("p j x f -> p j (x f)"))

        def group_k_half(s, x, lo=0):
            group_k(nc.vector.tensor_copy, kstage(s)[:, cut(x, KP * PACK)], kraw(s)[:, :, x, lo:], lo)

        def weave_k(bank, s, x, part):
            woven = bank[:].bitcast(BF16).rearrange("p (t i m j) -> p i j m t", t=PACK, i=2, j=PACK)
            for i in range(2):
                nc.tensor.matmul(
                    out=woven[:, i],
                    lhsT=ident16[:],
                    rhs=kraw(s)[:, :, x, cut(2 * part + i, P)].rearrange("p j (m t) -> p j m t", t=PACK),
                    start=True,
                    stop=True,
                )

        def unload_k(bank, s, x, part):
            words = kstage(s)[:].bitcast(F32).rearrange("p (x t r w) -> p x r t w", t=PACK, x=2, r=2)
            nc.scalar.copy(out=words[:, x, part], in_=bank[:].rearrange("p (t w) -> p t w", t=PACK))

        def quant_k(s, lo=0, hi=SLAB):
            quant(kcode[s % N_KCODE][:, lo:hi], kscal[s % N_KCODE][:, lo:hi], kstage(s)[:, lo * PACK : hi * PACK])

        def quant_k_half(s, x):
            quant_k(s, x * KP, (x + 1) * KP)

        def key_place(g, c):
            return g - g % 2 + c, g % 2

        def value_place(h, g):
            return (g, h) if g < WOVEN else (WOVEN + (FG - WOVEN) // 2 * h + (g - WOVEN) // 2, g % 2)

        def group_v(h, g, staged):
            nc.vector.tensor_copy(
                out=staged[:].rearrange("p (x c i j) -> p x c j i", x=2, i=RUN, j=PACK),
                in_=vraw_pair(g)[:, :, :, h].rearrange("p x j (c i) -> p x c j i", i=RUN),
            )

        def group_v_one(h, g, staged, hi=KP):
            nc.vector.tensor_copy(
                out=staged[:, cut(g % 2, KP * PACK)][:, : hi * PACK].rearrange("p (c i j) -> p c j i", i=RUN, j=PACK),
                in_=vraw(g)[:, :, h, :hi].rearrange("p j (c i) -> p c j i", i=RUN),
            )

        def group_v_half(h, g, staged):
            nc.vector.tensor_copy(
                out=staged[:, cut(h, KP * PACK)].rearrange("p (c i j) -> p c j i", i=RUN, j=PACK),
                in_=vraw(g)[:, :, h].rearrange("p j (c i) -> p c j i", i=RUN),
            )

        def group_v_both(g, staged):
            nc.vector.tensor_copy(
                out=staged[:].rearrange("p (c i j) -> p c j i", i=RUN, j=PACK),
                in_=vraw(g).rearrange("p j h (c i) -> p (h c) j i", i=RUN),
            )

        def group_v_scalar(g, staged, lo=0, hi=KP):
            nc.scalar.copy(
                out=staged[:, cut(g % 2, KP * PACK)][:, lo * PACK : hi * PACK].rearrange("p (c i j) -> p c j i", i=RUN, j=PACK),
                in_=vraw(g)[:, :, 1, lo:hi].rearrange("p j (c i) -> p c j i", i=RUN),
            )

        def weave_v(bank, h, g, part):
            for i in range(2):
                nc.tensor.matmul(
                    out=bank[:].bitcast(BF16)[:, cut(i, KP)].rearrange("p (n j) -> p j n", j=PACK),
                    lhsT=ident16[:],
                    rhs=vraw(g)[:, :, h, cut(2 * part + i, P)],
                    start=True,
                    stop=True,
                )

        def unload_v(bank, h, part):
            nc.scalar.copy(out=sgrp[:].bitcast(F32)[:, cut(2 * h + part, KP)], in_=bank[:])

        def quant_v(s, staged, lo=0, hi=SLAB):
            quant(vcode[s][:, lo:hi], vscal[s][:, lo:hi], staged[:, lo * PACK : hi * PACK])

        def ring_bank(g, i):
            return banks[TT + (2 + i % 2 if g == FG - 1 else i)]

        def keys(g, i):
            q, u = divmod(i, 2)
            for e in range(2):
                for c in range(XP):
                    s, x = key_place(g, c)
                    cols = cut(PACK * x + 2 * u + e if s in HALVED else (2 * u + e) * 2 + x, P)
                    nc.tensor.matmul_mx(
                        out=ring_bank(g, i)[:, cut(e, HALF)],
                        lhsT=kcode[s % N_KCODE][:, cols].bitcast(FP8X4),
                        lhsT_scale=kscal[s % N_KCODE][:, cols],
                        rhs=xcode[q][:, cut(c, HALF)].bitcast(FP8X4),
                        rhs_scale=xscal[q][:, cut(c, HALF)],
                        start=(c == 0),
                        stop=(c == XP - 1),
                    )

        def rectify(g, i):
            nc.scalar.activation(
                out=relu[g % 2][:, cut(i, KP)].rearrange("p (n a e) -> p n a e", a=2, e=2),
                in_=ring_bank(g, i)[:].rearrange("p (e a n) -> p n a e", e=2, a=2),
                func=ACT.Relu,
            )

        def square(g, q):
            nc.scalar.activation(
                out=hgrp[g % N_HGRP][:].rearrange("p (n q a u e) -> p q n a u e", q=2, a=2, u=2, e=2)[:, q],
                in_=relu[g % 2][:].rearrange("p (q u n a e) -> p q n a u e", q=2, a=2, u=2, e=2)[:, q],
                func=ACT.Square,
            )

        def rectify_square(g):
            for i in range(RING):
                rectify(g, i)
            for q in range(2):
                square(g, q)

        def keys_all(g):
            for i in range(RING):
                keys(g, i)

        def quant_h(g):
            quant(hcode[g][:], hscal[g][:], hgrp[g % N_HGRP][:])

        acc = banks

        def values(h, g, tts=range(TT)):
            s, x = value_place(h, g)
            for tt in tts:
                nc.tensor.matmul_mx(
                    out=acc[h * TT + tt][:],
                    lhsT=hcode[g][:, cut(tt, P)].bitcast(FP8X4),
                    lhsT_scale=hscal[g][:, cut(tt, P)],
                    rhs=vcode[s][:, cut(x, KP)].bitcast(FP8X4),
                    rhs_scale=vscal[s][:, cut(x, KP)],
                    start=(g == FIRST[h]),
                    stop=(g == FG - 1),
                )

        def sigmoid(tt, lo=0, hi=D):
            nc.scalar.activation(out=gate[tt][:, lo:hi], in_=rraw[tt][:, lo:hi], func=ACT.Sigmoid)

        def gate_of(n):
            h, tt = divmod(n, TT)
            return gate[tt][:, cut(h, KP)]

        def gate_y(n):
            nc.vector.tensor_tensor(out=yout[n], in0=acc[n][:], in1=gate_of(n), op=ALU.mult)

        def store_out(n, count=1):
            h, tt = divmod(n, TT)
            nc.sync.dma_start(
                out=out_0[tt * P : (tt + count) * P, cut(h, KP)].rearrange("(i p) d -> p i d", p=P),
                in_=relu[h][:, tt * KP : (tt + count) * KP].rearrange("p (i d) -> p i d", d=KP),
            )

        def as_stored(ap):
            return ap.rearrange("p (w u e) -> p w u e", u=2, e=2)

        def as_sorted(ap):
            return ap.rearrange("p (u w e) -> p w u e", u=2, e=2)

        def round_y(copy, n):
            copy(out=as_sorted(ybf[n]), in_=as_stored(yout[n]))

        def round_y_gpsimd(n):
            nc.gpsimd.tensor_scalar(
                out=ybf[n].rearrange("p (u w e) -> p u w e", u=2, e=2),
                in0=yout[n].rearrange("p (w u e) -> p u w e", u=2, e=2),
                scalar1=1.0, scalar2=0.0, op0=ALU.mult, op1=ALU.add,
            )

        def gate_y_rounded(n):
            nc.vector.tensor_tensor(
                out=as_sorted(ybf[n]), in0=as_stored(acc[n][:]), in1=as_stored(gate_of(n)), op=ALU.mult
            )

        def turn_y(pair):
            for i in range(2):
                words = ybf[2 * pair + i].bitcast(F32)
                for u in range(2):
                    nc.tensor.transpose(banks[pair][:, cut(2 * i + u, P)], words[:, cut(u, P)], ident[:])

        def turn_y_tile(bank, n):
            words = ybf[n].bitcast(F32)
            for u in range(2):
                nc.tensor.transpose(bank[:, cut(u, P)], words[:, cut(u, P)], ident[:])

        def unload_y_tile(bank, n):
            h, tt = divmod(n, TT)
            nc.scalar.copy(
                out=ygrp[h][:, cut(tt, KP)].bitcast(F32).rearrange("p (n u) -> p n u", u=2),
                in_=bank[:, :HALF].rearrange("p (u n) -> p n u", u=2),
            )

        def unload_y(pair):
            h, r = divmod(pair, 2)
            nc.scalar.copy(
                out=ygrp[h][:, cut(r, 2 * KP)].bitcast(F32).rearrange("p (i n u) -> p i n u", i=2, u=2),
                in_=banks[pair][:].rearrange("p (i u n) -> p i n u", i=2, u=2),
            )

        def quant_y(h, lo, hi):
            quant(ycode[h][:, lo:hi], yscal[PACK * h :, lo:hi], ygrp[h][:, lo * PACK : hi * PACK])

        def store_y(h, lo, hi):
            nc.sync.dma_start(
                out=out_1[h].rearrange("p m t -> p (m t)").bitcast(I32)[:, lo:hi],
                in_=ycode[h][:, lo:hi].bitcast(I32),
            )

        def store_scales():
            for q in range(4):
                queue = nc.scalar if q % 2 == 0 else nc.sync
                queue.dma_start(
                    out=out_2[:, cut(q, 4), :].bitcast(I32),
                    in_=yscal[32 * q : 32 * q + 8].bitcast(I32),
                )

        ctx.enter_context(tc.manual_schedule())

        make_identity(nc, ident[:])
        load_scales()
        load_x(0)
        load_r(0, 0, PRE, nc.scalar)
        load_rscale()
        load_x(1)
        load_k(0)
        load_k(1)
        load_r(0, PRE, D)
        load_r(1)
        for s in range(2, 6):
            load_k(s)
        sigmoid(0, 0, PRE)
        nc.vector.tensor_copy(out=ident16[:], in_=ident[:])
        nc.vector.tensor_copy(out=bscale[:], in_=sbytes[:].bitcast(FP8))
        widen_x_vector(1)
        widen_x_scalar(0)
        widen_x_vector(2, 0, 4)
        scale_x(1)
        widen_x_vector(2, 4)
        widen_x_scalar(3)
        scale_x(0)
        scale_x(2)
        scale_x(3)
        turn_x(1)
        turn_x(0)
        turn_x(2)
        group_k_half(0, 0)
        turn_x(3)
        weave_k(banks[0], 0, 1, 0)
        weave_k(banks[3], 0, 1, 1)
        load_k(6)
        unload_x(0, 0)
        unload_x(0, 1)
        unload_x(1, 0)
        unload_x(1, 1)
        sigmoid(0, PRE, D)
        unload_k(banks[0], 0, 1, 0)
        sigmoid(1)
        unload_k(banks[3], 0, 1, 1)
        quant_x(0)
        quant_k_half(0, 0)
        group_k_half(1, 0)
        quant_x(1)
        quant_k_half(1, 0)
        keys_all(0)
        group_k_half(1, 1)
        load_k(7)
        weave_k(banks[1], 2, 1, 0)
        weave_k(banks[2], 2, 1, 1)
        group_k_half(2, 0)
        load_v(0)
        quant_k_half(1, 1)
        quant_k_half(0, 1)
        quant_k_half(2, 0)
        group_k_slab(3)
        load_v(1)
        for i in range(RING):
            rectify(0, i)
        square(0, 0)
        unload_k(banks[1], 2, 1, 0)
        square(0, 1)
        unload_k(banks[2], 2, 1, 1)
        keys_all(1)
        weave_k(banks[3], 4, 1, 0)
        weave_k(banks[0], 4, 1, 1)
        group_k_half(4, 0)
        load_v(2)
        quant_k(3)
        quant_k_half(2, 1)
        group_k_slab(5)
        load_v(3)
        quant_h(0)
        quant_k_half(4, 0)
        for i in range(RING):
            rectify(1, i)
        square(1, 0)
        unload_k(banks[3], 4, 1, 0)
        square(1, 1)
        unload_k(banks[0], 4, 1, 1)
        keys_all(2)
        weave_k(banks[1], 6, 1, 0)
        weave_k(banks[2], 6, 1, 1)
        quant_k(5)
        quant_k_half(4, 1)
        group_k_half(6, 0)
        load_v(4)
        for i in range(RING):
            rectify(2, i)
        square(2, 0)
        unload_k(banks[1], 6, 1, 0)
        square(2, 1)
        unload_k(banks[2], 6, 1, 1)
        keys_all(3)
        weave_v(banks[3], 0, 0, 0)
        weave_v(banks[0], 0, 0, 1)
        weave_v(banks[1], 1, 0, 0)
        weave_v(banks[2], 1, 0, 1)
        quant_h(1)
        quant_k_half(6, 0)
        group_k_slab(7)
        load_v(5)
        load_v(6)
        quant_k_half(6, 1)
        group_v_half(0, 1, grp[1])
        quant_k(7)
        quant_v(1, grp[1], 0, KP)
        for i in range(RING):
            rectify(3, i)
        unload_v(banks[3], 0, 0)
        unload_v(banks[0], 0, 1)
        unload_v(banks[1], 1, 0)
        unload_v(banks[2], 1, 1)
        keys_all(4)
        square(3, 0)
        rectify(4, 0)
        square(3, 1)
        quant_v(0, sgrp, 0, KP)
        quant_h(2)
        values(0, 1)
        values(0, 0)
        group_v(0, 2, grp[0])
        quant_v(0, sgrp, KP, SLAB)
        quant_v(2, grp[0])
        quant_h(3)
        for i in range(1, RING):
            rectify(4, i)
        keys_all(5)
        square(4, 0)
        rectify(5, 0)
        square(4, 1)
        values(0, 2)
        group_v(0, 4, grp[0])
        quant_h(4)
        quant_v(3, grp[0])
        group_v_half(1, 1, grp[1])
        load_v(7)
        load_r(2)
        load_r(3)
        for i in range(1, RING):
            rectify(5, i)
        keys_all(6)
        square(5, 0)
        rectify(6, 0)
        square(5, 1)
        values(0, 3)
        quant_h(5)
        group_v(1, 2, grp[0])
        quant_v(1, grp[1], KP, SLAB)
        quant_v(5, grp[0], 0, KP)
        values(0, 4)
        rectify(6, 1)
        values(1, 0, range(2))
        rectify(6, 2)
        keys(7, 0)
        rectify(6, 3)
        keys(7, 1)
        square(6, 0)
        values(0, 5)
        rectify(7, 0)
        keys(7, 2)
        rectify(7, 1)
        keys(7, 3)
        square(6, 1)
        for g in range(1, 3):
            values(1, g, range(2))
        group_v_one(1, 4, sgrp)
        quant_v(5, grp[0], KP, SLAB)
        quant_v(6, sgrp, 0, KP)
        group_v(0, 6, grp[1])
        quant_h(6)
        quant_v(4, grp[1])
        values(1, 3, range(2))
        rectify(7, 2)
        rectify(7, 3)
        square(7, 0)
        group_v_scalar(5, grp[0], KP - P, KP)
        square(7, 1)
        for g in range(4):
            values(1, g, range(2, TT))
        values(1, 4)
        values(0, 6)
        quant_h(7)
        group_v_one(1, 5, grp[0], KP - P)
        values(0, 7)
        group_v_scalar(6, sgrp)
        group_v_scalar(7, sgrp)
        quant_v(7, sgrp, 0, KP)
        quant_v(6, grp[0], KP, SLAB)
        gate_y(0)
        store_out(0)
        quant_v(7, sgrp, KP, SLAB)
        values(1, 6)
        values(1, 5, range(2))
        values(1, 7, range(2))
        sigmoid(2, 0, KP)
        sigmoid(3, 0, KP)
        round_y(nc.scalar.copy, 0)
        gate_y(1)
        store_out(1)
        round_y_gpsimd(1)
        sigmoid(2, KP, D)
        sigmoid(3, KP, D)
        values(1, 5, [2])
        values(1, 7, [2])
        gate_y(2)
        store_out(2)
        round_y_gpsimd(2)
        gate_y(3)
        store_out(3)
        round_y(nc.scalar.copy, 3)
        turn_y(0)
        values(1, 5, [3])
        values(1, 7, [3])
        turn_y(1)
        gate_y(TT)
        store_out(TT)
        round_y_gpsimd(TT)
        unload_y(0)
        gate_y(TT + 1)
        store_out(TT + 1)
        round_y(nc.scalar.copy, TT + 1)
        gate_y(TT + 2)
        store_out(TT + 2)
        turn_y(2)
        unload_y(1)
        gate_y(TT + 3)
        store_out(TT + 3)
        round_y(nc.vector.tensor_copy, TT + 2)
        turn_y_tile(banks[3], TT + 2)
        round_y(nc.vector.tensor_copy, TT + 3)
        turn_y_tile(banks[0], TT + 3)
        unload_y(2)
        quant_y(0, 0, T // 2)
        unload_y_tile(banks[3], TT + 2)
        unload_y_tile(banks[0], TT + 3)
        quant_y(0, T // 2, T)
        store_y(0, 0, T)
        quant_y(1, 0, T // 2)
        store_y(1, 0, T // 2)
        quant_y(1, T // 2, T - P)
        quant_y(1, T - P, T)
        store_y(1, T // 2, T)
        store_scales()
